import numpy as np, ml_dtypes
CORES = [48,51,52,55]
N = 4
BF = ml_dtypes.bfloat16
W, M, B, T = 4096, 256, 1024, 4
S = (1, 2, 4)
WQ = (2 * np.arange(16) + 1).reshape(1, 1, 16, 1)
def place(l, a):
    return ((l * a >> 5) + l + 37 * a) & (W - 1)
def spot(u):
    return ((u * u >> 5) + 37 * u) & (B - 1)
def fetch(x, l, a):
    return np.take_along_axis(x, place(l, a).reshape(l.shape[:2] + (1, 16 * M)), 3).reshape(l.shape[:2] + (16, 16, M))
def gaps(rec, s):
    return np.add.reduce(np.abs(rec - np.roll(rec, -s, axis=3)), axis=2, dtype=np.int32)
def parts(rng):
    x = rng.integers(0, 256, (N, 8, 16, W)).astype(np.int16); body = rng.integers(0, 4096, (N, 8, 16, B)); l = rng.integers(0, 4096, (N, 8, 16, M))
    many = rng.choice(np.array([1, 2, 2, 3, 4, 6, 8, 8, 12, 16, 16, 16]), (N, 8, 1, M))
    a = np.take_along_axis(rng.integers(0, 4096, (N, 8, 16, M)), (rng.random((N, 8, 16, M)) * many).astype(np.int64), 2)
    c = rng.integers(0, 256, (N, 8, 16, M)); c = np.where(rng.random((N, 8, 1, M)) < 0.3, c & 7, c)
    return x, body, l, a, c, rng.integers(700, 1300, (N, 8, M))
def apart(rng):
    return rng.integers(0, 256, (16, M)) * 16 + np.argsort(rng.random((16, M)), axis=0)
def named(rng, cols):
    l = np.concatenate([np.array(cols), rng.integers(0, 4096, 2 ** 18)]); a = np.concatenate([np.zeros(len(cols), np.int64), rng.integers(0, 4096, 2 ** 18)])
    ix = np.nonzero(np.isin(place(l, a), np.array(cols)))[0]; l, a = l[ix], a[ix]
    ix = np.unique(a, return_index=True)[1]; ix = rng.permutation(ix)
    return l[ix], a[ix]
def uneven(rng, bits, shape):
    return np.minimum(np.exp2(bits * rng.random(shape)).astype(np.int64), 2 ** bits - 1) * (rng.random(shape) > 0.03)
def always(x, body, l, a, c):
    x = x.copy(); row = np.arange(16).reshape(1, 1, 16, 1); first = 16 * np.arange(M).reshape(1, 1, 1, M); d = []
    for t in range(T):
        full = np.ones(l.shape, bool); rec = fetch(x, l, a)
        for s in S:
            ok = full & np.roll(full, -s, axis=2) & (a != np.roll(a, -s, axis=2))
            key = np.where(ok, gaps(rec, s), 2 ** 20)
            k = np.argmin(key, axis=2)[:, :, None, :]; j = (k + s) & 15
            least = np.take_along_axis(key, k, 2); go = least < 2 ** 20; d.append(least[:, :, 0])
            ak, aj = np.take_along_axis(a, k, 2), np.take_along_axis(a, j, 2)
            low = np.minimum(np.take_along_axis(c, k, 2), np.take_along_axis(c, j, 2))
            c = np.where(go & (row == k), low, c); full = full & ~(go & (row == j))
            a = np.where(go & (a == np.maximum(ak, aj)), np.minimum(ak, aj), a)
            rec = fetch(x, l, a)
        k = np.argmax(np.where(full, c, -1), axis=2)[:, :, None, :]
        z = np.take_along_axis(rec, k[:, :, None], 3)[:, :, :, 0]
        top = np.max(np.where(full[:, :, None], rec, np.int16(0)), axis=3)
        u = np.add.reduce(z.astype(np.int64) * WQ, axis=2, keepdims=True) & 4095
        b = np.take_along_axis(body, spot(u), 3); new = ~full | (row == k)
        ak, ck = np.take_along_axis(a, k, 2), np.take_along_axis(c, k, 2) >> 1
        a = np.where(new, np.where((row & 1) == 1, ak, ((b * u >> 5) + t) & 4095), a)
        l = np.where(new, b, l); c = np.where(new, ck, c)
        np.put_along_axis(x, np.broadcast_to(first + (u & 15), l.shape), (z + top) >> 1, 3)
        l, a, c = np.roll(l, 1, axis=0), np.roll(a, 1, axis=0), np.roll(c, 1, axis=0)
    return np.stack(d)
def pack(x, body, l, a, c, t):
    return {"xs": np.ascontiguousarray(x.reshape(N, 128, W)).astype(np.float32).astype(BF), "rb": np.ascontiguousarray(body.reshape(N, 128, B)).astype(np.int32),
            "lt": np.ascontiguousarray(l.reshape(N, 128, M)).astype(np.int32), "ag": np.ascontiguousarray(a.reshape(N, 128, M)).astype(np.int32),
            "cs": np.ascontiguousarray(c.reshape(N, 128, M)).astype(np.int32), "th": np.ascontiguousarray(t).astype(np.int32)}
def setup_inputs(rng):
    return pack(*parts(rng))
def setup_inputs_spread(rng):
    x = np.minimum(np.exp2(8 * rng.random((N, 8, 1, W))) * rng.random((N, 8, 16, W)), 255).astype(np.int16)
    sh = (N, 8, 16, M)
    return pack(x, uneven(rng, 12, (N, 8, 16, B)), uneven(rng, 12, sh), uneven(rng, 12, sh), uneven(rng, 8, sh), uneven(rng, 12, (N, 8, M)))
def setup_inputs_ends(rng):
    sh = (N, 8, 16, M); half = lambda s: (rng.random(s) < 0.5).astype(np.int64)
    x = (255 * (rng.random((N, 8, 16, W)) < rng.choice(np.array([0.0, 0.5, 1.0]), (N, 8, 1, W)))).astype(np.int16)
    body = 4095 * half((N, 8, 16, B)); c = 255 * half(sh); t = 4095 * half((N, 8, M))
    c = np.where(rng.random((N, 8, 1, M)) < 0.1, 255, c)
    alt = rng.random((N, 8, 1, M)) < 0.3; alt[..., 0] = True; alt[..., M - 1] = True; t[..., 0] = 4095; t[..., M - 1] = 4095
    way = ((np.arange(16) // S[0]) & 1).reshape(1, 1, 16, 1)
    l = 4095 * np.where(alt, way, half(sh)); a = 4095 * np.where(alt, way, half(sh))
    top = np.full(16, 255); top[7] = 0; top[0] = 239
    ub = int(np.argmax(spot(np.arange(4096)))); far = np.zeros(16, np.int64); far[15] = ub // 31; far[0] = ub - 31 * (ub // 31)
    put = rng.random((N, 8)) < 0.6; put[:, 7] = True; put[N - 1] = True
    for q in range(N):
        for g in range(8):
            if put[q, g]:
                x[q, g, :, place(0, 0)] = 0; x[q, g, :, place(4095, 4095)] = 255; x[q, g, :, place(4095, 0)] = top; x[q, g, :, place(0, 4095)] = far
                body[q, g, :, spot(4095)] = 4095; body[q, g, :, spot(ub)] = 4095 * (np.arange(16) & 1)
    return pack(x, body, l, a, c, t)
def setup_inputs_corners(rng):
    x, body, l, a, c, t = parts(rng); k = np.arange(16).reshape(16, 1); i = np.arange(M)
    for q in range(N):
        fl, fa = named(rng, [0, W - 1])
        for g in range(8):
            kind = (g + q) & 7
            if kind == 0: t[q, g] = 0
            if kind == 1: a[q, g] = apart(rng); t[q, g] = 4095
            if kind == 2: a[q, g] = rng.choice(np.array([0, 4095, 77, 2048]), (1, M)); t[q, g] = 4095
            if kind == 3:
                if (q & 1) == 0:
                    m = rng.integers(S[0], 16, M); m[M - 1] = 8; t[q, g] = 4095
                    l[q, g, 15, M - 1] = 4095; c[q, g, :, M - 1] = rng.integers(0, 255, 16); c[q, g, 15, M - 1] = 255
                    l[q, g, m, i] = place(l[q, g, (m - S[0]) & 15, i], 4095)
                else:
                    m = rng.integers(0, 16, M); t[q, g] = np.where(rng.random(M) < 0.8, 4095, t[q, g])
                a[q, g] = np.where(k == m.reshape(1, M), 0, 4095)
            if kind == 4: c[q, g] = rng.choice(np.array([0, 1, 254, 255]), (1, M))
            if kind == 5:
                c[q, g] = np.where(k == rng.choice(np.array([0, 7, 8, 15]), (1, M)), 255, rng.choice(np.array([0, 254, 255]), (1, M))); t[q, g] = rng.choice(np.array([0, 4095]), M)
            if kind == 6:
                x[q, g] = 255 * (rng.random((1, W)) < 0.5); t[q, g] = rng.choice(np.array([0, 1, 4080, 4081]), M)
                x[q, g, :, place(0, 4095)] = 0; x[q, g, :, W - 1] = 255
                lone = rng.random(M) < 0.25; lone[0] = True; lone[M - 1] = True; one = k == rng.integers(0, 16, (1, M))
                l[q, g] = np.where(lone, np.where(one, 0, 4095), l[q, g]); a[q, g] = np.where(lone, np.where(one, 4095, 0), a[q, g])
                t[q, g] = np.where(lone, 4080 + (rng.random(M) < 0.3), t[q, g]); t[q, g, 0] = 4081; t[q, g, M - 1] = 4080
            if kind == 7:
                ix = rng.integers(0, len(fl), (16, M)); l[q, g] = fl[ix]; a[q, g] = fa[ix]
    return pack(x, body, l, a, c, t)
def setup_inputs_crowd(rng):
    x, body, l, a, c, t = parts(rng)
    for q in range(N):
        fl, fa = named(rng, [int(rng.integers(0, W))]); one = (int(rng.integers(0, M)), M - 1)
        for g in range(8):
            kind = (g + q) & 7; i = one[int(rng.integers(0, 2))]
            if g in (3, 4): kind = 8
            if kind in (0, 1, 4):
                ix = (rng.integers(0, len(fl), (1, M)) + np.arange(16).reshape(16, 1)) % len(fl); l[q, g] = fl[ix]; a[q, g] = fa[ix]
            if kind == 1: t[q, g] = 1; t[q, g, i] = 0
            if kind in (2, 3, 8): a[q, g] = apart(rng); t[q, g] = 4095
            if kind == 3: a[q, g, :, i] = a[q, g, 0, i]
            if kind == 4: t[q, g] = rng.integers(0, 3, M); c[q, g] = 200
            if kind == 5: a[q, g] = apart(rng); l[q, g] = l[q, g, 0, 0]; c[q, g] = 255
    d = always(x[:, 3:5], body[:, 3:5], l[:, 3:5], a[:, 3:5], c[:, 3:5])
    edge = d[-1] - ((M * (len(S) * T - 1)) & 31)
    t[:, 3:5] = np.where((d[-1] <= 4080) & (np.max(d[:-1], axis=0) < edge), edge, 4095)
    return pack(x, body, l, a, c, t)
def setup_inputs_ties(rng):
    x, body, l, a, c, t = parts(rng); few = rng.integers(0, 256, (N, 4, 16, 4)).astype(np.int16)
    x[:, ::2] = np.take_along_axis(few, rng.integers(0, 4, (N, 4, 1, W)), 3)
    c[:, 1::2] = rng.integers(5, 7, (N, 4, 16, M))
    key = np.where(a != np.roll(a, -S[0], axis=2), gaps(fetch(x, l, a), S[0]), 5000)
    t = np.where(rng.random((N, 8, M)) < 0.6, np.minimum(np.min(key, axis=2) + rng.integers(0, 2, (N, 8, M)), 4095), t)
    return pack(x, body, l, a, c, t)
def check_inputs(d):
    bad = []
    for k, lo, hi in (("xs", 0, 255), ("rb", 0, 4095), ("lt", 0, 4095), ("ag", 0, 4095), ("cs", 0, 255), ("th", 0, 4095)):
        v = np.asarray(d[k]).astype(np.float64)
        if not (np.min(v) >= lo and np.max(v) <= hi): bad.append("range of " + k)
        elif k == "xs" and np.any(v != np.floor(v)): bad.append("whole numbers of xs")
    return bad
def reference(xs, rb, lt, ag, cs, th):
    x = xs.astype(np.float32).astype(np.int16).reshape(N, 8, 16, W); body = rb.astype(np.int32).reshape(N, 8, 16, B)
    l = lt.astype(np.int32).reshape(N, 8, 16, M); a = ag.astype(np.int32).reshape(N, 8, 16, M); c = cs.astype(np.int32).reshape(N, 8, 16, M)
    limit = th.astype(np.int64); made = np.zeros((N, 8), np.int64)
    row = np.arange(16).reshape(1, 1, 16, 1); first = 16 * np.arange(M).reshape(1, 1, 1, M)
    for t in range(T):
        full = np.ones((N, 8, 16, M), bool); rec = fetch(x, l, a)
        for s in S:
            ok = full & np.roll(full, -s, axis=2) & (a != np.roll(a, -s, axis=2))
            key = np.where(ok, gaps(rec, s), 2 ** 20)
            k = np.argmin(key, axis=2)[:, :, None, :]; j = (k + s) & 15
            go = np.take_along_axis(key, k, 2) < (limit + (made & 31)[:, :, None])[:, :, None, :]
            ak, aj = np.take_along_axis(a, k, 2), np.take_along_axis(a, j, 2)
            low = np.minimum(np.take_along_axis(c, k, 2), np.take_along_axis(c, j, 2))
            c = np.where(go & (row == k), low, c); full = full & ~(go & (row == j))
            a = np.where(go & (a == np.maximum(ak, aj)), np.minimum(ak, aj), a)
            made = made + np.add.reduce(go[:, :, 0].astype(np.int64), axis=2)
            rec = fetch(x, l, a)
        k = np.argmax(np.where(full, c, -1), axis=2)[:, :, None, :]
        z = np.take_along_axis(rec, k[:, :, None], 3)[:, :, :, 0]
        top = np.max(np.where(full[:, :, None], rec, np.int16(0)), axis=3)
        u = (np.add.reduce(z.astype(np.int32) * WQ, axis=2, keepdims=True) & 4095).astype(np.int32)
        b = np.take_along_axis(body, spot(u), 3); new = ~full | (row == k)
        ak, ck = np.take_along_axis(a, k, 2), np.take_along_axis(c, k, 2) >> 1
        a = np.where(new, np.where((row & 1) == 1, ak, ((b * u >> 5) + t) & 4095), a)
        l = np.where(new, b, l); c = np.where(new, ck, c)
        np.put_along_axis(x, np.broadcast_to(first + (u & 15), (N, 8, 16, M)), (z + top) >> 1, 3)
        if t < T - 1: l, a, c = np.roll(l, 1, axis=0), np.roll(a, 1, axis=0), np.roll(c, 1, axis=0)
    return {"yl": l.reshape(N, 128, M).astype(np.float32), "ya": a.reshape(N, 128, M).astype(np.float32), "yc": c.reshape(N, 128, M).astype(np.float32), "yx": x.reshape(N, 128, W).astype(np.float32).astype(BF)}

@@ -1,0 +1,626 @@
+from concourse.mybir import AluOpType as A, ActivationFunctionType as F
+
+NV, SH = 4, (1, 2, 4)
+NP = 2
+W = 256 // NP
+NL = W // 16
+NU = 4
+BIG = 131072.0
+FAR = 16777216.0
+f32, b16, h16, i32, u16 = "float32", "bfloat16", "float16", "int32", "uint16"
+
+SCRATCH = {"X0": ("sbuf", [128, 4112], b16), "X1": ("sbuf", [128, 4112], b16), "rbs": ("sbuf", [128, 1024], i32),
+           "inp": ("sbuf", [128, 768], i32), "thi": ("sbuf", [128, 256], i32), "thf": ("sbuf", [128, 256], f32),
+           "th16": ("sbuf", [128, 8 * NP], f32), "rs": ("sbuf", [128, 128 * NP], f32), "cnt": ("sbuf", [128, 8 * NP], i32),
+           "go": ("sbuf", [128, 8 * NP], b16),
+           "ri": ("sbuf", [128, 8], i32), "col": ("sbuf", [128, 16], f32), "im": ("sbuf", [128, 128], f32),
+           "ix": ("sbuf", [128, 144], f32), "mg": ("sbuf", [128, 128], f32), "mgE": ("sbuf", [128, 128], f32),
+           "mgO": ("sbuf", [128, 128], f32), "tx": ("sbuf", [128, 8, 32], f32), "mk": ("sbuf", [128, 128], b16),
+           "cz": ("sbuf", [128, 8], b16), "csl": ("sbuf", [128, 8], i32),
+           "l16i": ("sbuf", [128, 8], i32), "l16": ("sbuf", [128, 8], u16),
+           "rstm": ("sbuf", [128, 128], f32), "rst1": ("sbuf", [128, 1024], b16), "rows": ("sbuf", [128, 1024], b16),
+           "one16": ("sbuf", [128, 128], b16), "I32": ("sbuf", [128, 8], f32), "blkD": ("sbuf", [128, 8], b16),
+           "Wb": ("sbuf", [128, 144], b16), "mb": ("sbuf", [128, 16, 128], b16), "mh": ("sbuf", [128, 19, 128], h16),
+           "pm": ("psum", [128, 512], f32), "pq": ("psum", [128, 512], f32)}
+for _h in range(NP):
+    for _n, _sh, _d in (("tl", [128, NV, 3 * W], h16), ("to", [128, 3 * W], h16), ("tf", [128, 3 * W], f32),
+                        ("rec", [128, 16 * W], b16), ("abd", [128, 16 * W], b16), ("top", [128, 16 * W], b16), ("ex", [128, 3, W], b16),
+                        ("pn", [128, 128], f32), ("bm", [128, 128], f32), ("ou", [128, 2, 128], b16),
+                        ("off", [128, W], u16), ("wf", [128, 4, W], f32), ("wi", [128, 5, W], i32), ("wh", [128, 3, W], h16),
+                        ("wb", [128, 4, W], b16), ("sk", [128, 8], i32),
+                        ("si", [128, 5, 8], i32), ("sf", [128, 2, 8], f32), ("su", [128, 24], u16)):
+        SCRATCH[_n + str(_h)] = ("sbuf", _sh, _d)
+    SCRATCH["ph%d" % _h] = ("psum", [128, 512], f32)
+for _b in range(6 - NP):
+    SCRATCH["pd%d" % _b] = ("psum", [128, 512], f32)
+
+SEMAPHORES = ["pe", "dve", "act", "pool", "lx0", "lx1", "lx2", "lx3", "ll", "la", "lc", "lth", "lrb"] + \
+    ["cx%d" % _t for _t in range(NV)] + ["sx%d" % _h for _h in range(NP)] + ["sy%d%d" % (_h, _j) for _h in range(NP) for _j in range(3)] + \
+    ["%s%d%d" % (_p, _t, _h) for _p in ("ar", "sn") for _t in range(NV - 1) for _h in range(NP)]
+
+PAR = {"g": 1.56, "cyc": 0.83 * 1.2, "pe": 0.42 * 1.2, "fix": 30.0, "hop": 120.0, "pen": 0.0, "per": 10500.0, "extra": 4000.0,
+       "dm": 0, "relu": 0, "pu": 8, "rounds": 6}
+CACHE = {}
+
+
+def build(g, core, T, topo):
+    ops, stage = [], [0]
+    V, S, P = g.vector, g.scalar, g.tensor
+    rank = T.rank_of(core)
+    nxt = T.cores[(rank + 1) % len(T.cores)]
+    rid, pid = topo.addr(nxt)[:2]
+    eng = topo.engines(core, nxt)[::2]
+    mask = sum(1 << e for e in eng)
+
+    def bank(names):
+        return sorted(set(n.split("_")[0] for n in names if n[0] == "p" and n[1] in "dhmq" and "_" in n))
+
+    def op(q, calls, R, Wr, cyc, sem=None, inc=1, lat=0.0, after=None):
+        ops.append({"q": q, "calls": calls, "R": list(R), "W": list(Wr), "cyc": cyc, "banks": bank(list(R) + list(Wr)), "sem": sem,
+                    "inc": inc, "lat": lat, "after": after, "stage": stage[0]})
+        return len(ops) - 1
+
+    def tt(out, a, b, o, R, Wr, n, gat=False):
+        op("dve", [lambda: V.tensor_tensor(out, a, b, o)], R, Wr, ("g", n) if gat else (n if bank(R) else 2 * n))
+
+    def ts(out, a, s1, s2, o0, o1, R, Wr, n):
+        if o1 is None:
+            op("dve", [lambda: V.tensor_scalar(out, a, s1, None, o0)], R, Wr, n)
+        else:
+            op("dve", [lambda: V.tensor_scalar(out, a, s1, s2, o0, o1)], R, Wr, n)
+
+    def cp(out, a, R, Wr, n):
+        op("dve", [lambda: V.tensor_copy(out, a)], R, Wr, n)
+
+    def scan(out, d0, d1, init, o0, o1, R, Wr, n):
+        op("dve", [lambda: V.tensor_tensor_scan(out, d0, d1, init, o0, o1)], R, Wr, n)
+
+    def either(out, a, R, Wr, n):
+        i = op("any", None, R, Wr, n)
+        ops[i]["alt"] = {"dve": [lambda: V.tensor_copy(out, a)], "act": [lambda: S.activation(out, a, F.Copy)]}
+
+    def affine(out, a, f, scale, bias, R, Wr, n):
+        i = op("any", None, R, Wr, n)
+        if f == "relu":
+            ops[i]["alt"] = {"dve": [lambda: V.tensor_scalar(out, a, 0.0, scale, A.max, A.mult)],
+                             "act": [lambda: S.activation(out, a, F.Relu, bias=0.0, scale=scale)]}
+        else:
+            ops[i]["alt"] = {"dve": [lambda: V.tensor_scalar(out, a, scale, bias, A.mult, A.add)],
+                             "act": [lambda: S.activation(out, a, F.Identity, bias=bias, scale=scale)]}
+
+    def ms(out, c, Wr, n):
+        op("dve", [lambda: V.memset(out, c)], [], Wr, n)
+
+    def mm(terms, R, Wr, first=True, last=True, pairs=False):
+        calls = []
+        for j, (o, l, r, n) in enumerate(terms):
+            st, sp = (j % 2 == 0, j % 2 == 1) if pairs else (first and j == 0, last and j == len(terms) - 1)
+            calls.append(lambda o=o, l=l, r=r, st=st, sp=sp: P.matmul(o, l, r, st, sp))
+        op("pe", calls, R, Wr, sum(max(64, x[3]) for x in terms))
+
+    def iota(out, pat, base, cm, Wr, n, flt=True):
+        if flt:
+            op("pool", [lambda: g.iota(out, pat, base, cm, allow_small_or_imprecise_dtypes=True)], [], Wr, 160 + 2 * n)
+        else:
+            op("pool", [lambda: g.iota(out, pat, base, cm)], [], Wr, 160 + 2 * n)
+
+    def dma(q, out, a, R, Wr, sem, lat):
+        e = {"sp": g.sync, "act": g.scalar}[q]
+        op(q, [lambda: e.dma_start(out, a)], R, Wr, 60, sem=sem, inc=16, lat=lat)
+
+    inp = T["inp"]
+    dma("sp", inp[:, 0:256], T["lt"][:], [], ["inL"], "ll", 2000)
+    dma("act", inp[:, 256:512], T["ag"][:], [], ["inA"], "la", 2000)
+    for j in range(4):
+        dma("sp" if j % 2 == 0 else "act", T["X0"][:, 1024 * j:1024 * j + 1024], T["xs"][:, 1024 * j:1024 * j + 1024], [], ["Xl%d" % j],
+            "lx%d" % j, 3000 + 500 * j)
+    dma("sp", inp[:, 512:768], T["cs"][:], [], ["inC"], "lc", 4500)
+    dma("sp", T["thi"][0:8, :], T["th"][:], [], ["thi"], "lth", 4500)
+    dma("sp", T["rbs"][:], T["rb"][:], [], ["rbs"], "lrb", 6000)
+    for b in range(2):
+        ms(T["X%d" % b][:, 4096:4112], 0.0, ["Xz%d" % b], 16)
+
+    ri, col = T["ri"], T["col"]
+    iota(T["im"][:], [[1, 128]], 0, -1, ["im"], 128)
+    iota(ri[:, 0:1], [[0, 1]], 0, 1, ["ri0"], 1, False)
+    iota(T["mg"][:], [[1, 8], [0, 16]], 0, 0, ["mg"], 128)
+    iota(T["tx"][:], [[16, 8], [0, 2], [1, 16]], 0, -1, ["tx"], 256)
+    iota(T["l16i"][:], [[1, 8]], 0, 0, ["l16i"], 8, False)
+    iota(T["mk"][:], [[0, 8], [1, 16]], 0, 0, ["mk"], 128)
+    iota(T["cz"][:], [[256, 8]], 0, 0, ["cz"], 8)
+    iota(T["mgE"][:], [[1, 8], [0, 8], [100, 2]], 0, 0, ["mgE"], 128)
+    iota(T["mgO"][:], [[1, 8], [0, 8], [-100, 2]], 100, 0, ["mgO"], 128)
+    iota(T["ix"][:], [[1, 144]], -15, 0, ["ix"], 144)
+    ts(ri[:, 1:2], ri[:, 0:1], 15, None, A.bitwise_and, None, ["ri0"], ["ri1"], 1)
+    ts(ri[:, 2:3], ri[:, 0:1], 4, None, A.arith_shift_right, None, ["ri0"], ["ri2"], 1)
+    for e in range(3):
+        ts(ri[:, 3 + e:4 + e], ri[:, 0:1], e, 1, A.arith_shift_right, A.bitwise_and, ["ri0"], ["ri%d" % (3 + e)], 1)
+    C, M, RW = {}, {}, {}
+
+    def column(name, j, src, m, a):
+        C[name] = col[:, j:j + 1]
+        ts(C[name], ri[:, src:src + 1], m, a, A.mult, A.add, ["ri%d" % src], [name], 1)
+    column("rk", 0, 1, 1.0, 0.0)
+    column("rg", 1, 2, 1.0, 0.0)
+    column("rg16", 2, 2, 16.0, 0.0)
+    column("rk16", 3, 1, 16.0, 0.0)
+    column("kB", 4, 1, 1.0 / BIG, 0.0)
+    column("wq", 5, 1, 2.0, 1.0)
+    for e in range(3):
+        column("sg%d" % e, 7 + e, 3 + e, -2.0, 1.0)
+        column("bt%d" % e, 13 + e, 3 + e, -2.0, 0.0)
+    for t in range(1, NV):
+        column("ev%d" % t, 9 + t, 3, -32.0 * t, 32.0 * t)
+
+    def matrix(name, buf, j, src, srcn, s1, s2, extra=()):
+        M[name] = T[buf][:, j, :]
+        ts(M[name], src, s1, s2, A.is_equal, A.mult, [srcn] + list(extra), [name], 128)
+    im, mg, tx = T["im"][:], T["mg"][:], T["tx"]
+    for name, buf, j, c in (("Ih", "mh", 0, 1.0), ("I2080", "mh", 1, 2080.0), ("I", "mb", 0, 1.0), ("nI", "mb", 1, -1.0), ("BI", "mb", 2, BIG),
+                            ("nBI", "mb", 3, -BIG), ("I2", "mb", 4, 2.0), ("I2h", "mh", 2, 2.0), ("n16h", "mh", 3, -16.0)):
+        matrix(name, buf, j, im, "im", 0.0, c)
+    matrix("nblk", "mh", 4, mg, "mg", C["rg"], -1.0, ["rg"])
+    matrix("blk", "mh", 5, mg, "mg", C["rg"], 1.0, ["rg"])
+    matrix("odd", "mh", 6, T["mgO"][:], "mgO", C["rg"], 1.0, ["rg"])
+    matrix("WqO", "mb", 5, T["mgE"][:], "mgE", C["rg"], C["wq"], ["rg", "wq"])
+    matrix("mP", "mb", 6, T["mk"][:], "mk", C["rk"], 1.0 / 16, ["rk"])
+    for si in range(3):
+        s = SH[si]
+        matrix("Sh%d" % si, "mh", 7 + si, tx[:, :, s:s + 16], "tx", 0.0, 1.0)
+        M["SI%d" % si] = T["mh"][:, 10 + si, :]
+        tt(M["SI%d" % si], M["Sh%d" % si], M["Ih"], A.subtract, ["Sh%d" % si, "Ih"], ["SI%d" % si], 128)
+        matrix("sig%d" % si, "mh", 13 + si, mg, "mg", C["rg"], C["sg%d" % si], ["rg", "sg%d" % si])
+        matrix("bit%d" % si, "mh", 16 + si, mg, "mg", C["rg"], C["bt%d" % si], ["rg", "bt%d" % si])
+        matrix("J%d" % si, "mb", 7 + si, tx[:, :, 16 - s:32 - s], "tx", 0.0, BIG)
+        matrix("IJ%d" % si, "mb", 10 + si, tx[:, :, 16 - s:32 - s], "tx", 0.0, 1.0)
+        tt(M["IJ%d" % si], M["IJ%d" % si], M["I"], A.add, ["IJ%d" % si, "I"], ["IJ%d" % si], 128)
+    for j, (e, si) in enumerate(((0, 1), (0, 2), (1, 2))):
+        nm, d = "pen%d%d" % (e, si), SH[si] - SH[e]
+        matrix(nm, "mb", 13 + j, tx[:, :, d:d + 16], "tx", 0.0, BIG)
+        tt(M[nm], M[nm], M["J%d" % e], A.add, [nm, "J%d" % e], [nm], 128)
+    ts(T["blkD"][:], T["mg"][:, ::16], C["rg"], 16.0, A.is_equal, A.mult, ["mg", "rg"], ["blkD"], 8)
+    ts(T["I32"][:], T["im"][:, 0:8], 0.0, 16.0, A.is_equal, A.mult, ["im"], ["I32"], 8)
+    ts(T["Wb"][:], T["ix"][:], C["rg16"], C["wq"], A.is_equal, A.mult, ["ix", "rg16", "wq"], ["Wb"], 144)
+    ts(T["csl"][:], T["cz"][:], C["rk16"], None, A.add, None, ["cz", "rk16"], ["csl"], 8)
+    cp(T["l16"][:], T["l16i"][:], ["l16i"], ["l16"], 8)
+    ms(T["rstm"][:], -FAR, ["rstm"], 128)
+    ms(T["rstm"][:, ::16], FAR, ["rstm"], 8)
+    ms(T["rst1"][:], 1.0, ["rst1"], 512)
+    ms(T["rst1"][:, ::16], 0.0, ["rst1"], 64)
+    ms(T["one16"][:], 16.0, ["one16"], 64)
+    rows = T["rows"]
+    for j, (name, val) in enumerate((("r1", 1.0), ("r3232", 3232.0), ("rBIG", BIG), ("r8192", 8192.0), ("r10240", 10240.0), ("r4096", 4096.0), ("rodd", 0.0))):
+        RW[name] = rows[0:1, 128 * j:128 * j + 128]
+        ms(RW[name], val, [name], 64)
+    ms(rows[0:1, 128 * 6 + 1:128 * 7:2], 2048.0, ["rodd"], 64)
+    RW["rgo"] = rows[0:1, 896:1024]
+    ts(RW["rgo"], T["mg"][0:1, :], -1048576.0, None, A.mult, None, ["mg"], ["rgo"], 128)
+    one = rows[0:1, 0:W]
+
+    def const(out, name):
+        return (out, RW[name], one, W)
+
+    pm, pq, rs = T["pm"], T["pq"], T["rs"]
+    cp(T["thf"][0:8, :], T["thi"][0:8, :], ["thi"], ["thf"], 256)
+    for h in range(NP):
+        o = pm[0:W, 304 + 8 * h:312 + 8 * h]
+        mm([(o, T["thf"][0:8, W * h:W * h + W], T["I32"][0:8, :], 256), (o, one, rows[0:1, 896:1024:16], 8)], ["thf", "I32", "r1", "rgo"], ["pm_t%d" % h])
+        ms(T["sk%d" % h][:], 0, ["sk%d" % h], 8)
+        tl = T["tl%d" % h]
+        ts(tl[:, 0, 0:W], inp[:, W * h:W * h + W], -2048.0, None, A.add, None, ["inL"], ["L0%d" % h], W)
+        ts(tl[:, 0, W:2 * W], inp[:, 256 + W * h:256 + W * h + W], -2048.0, None, A.add, None, ["inA"], ["a0%d" % h], W)
+        cp(tl[:, 0, 2 * W:3 * W], inp[:, 512 + W * h:512 + W * h + W], ["inC"], ["C0%d" % h], W)
+    ts(T["th16"][0:W, :], pm[0:W, 304:304 + 8 * NP], -0.5, None, A.add, None, ["pm_t%d" % h for h in range(NP)], ["th16"], 8 * NP)
+    ms(rs[:], FAR, ["thr"], 128 * NP)
+    cp(rs[0:W, ::16], T["th16"][0:W, :], ["th16"], ["thr"], 8 * NP)
+    ms(T["cnt"][:], 0, ["cnt"], 16)
+
+    def slot(h, name):
+        if NP == 2:
+            b, j = {"key": ("ph%d" % h, 0), "x1": ("ph%d" % h, 1), "x2": ("ph%d" % h, 2), "x3": ("ph%d" % h, 3),
+                    "uo": ("pd%d" % (2 * h), 0), "a2": ("pd%d" % (2 * h), 1), "c2": ("pd%d" % (2 * h), 2), "zt": ("pd%d" % (2 * h), 3),
+                    "l1": ("pd%d" % (2 * h + 1), 0), "a1": ("pd%d" % (2 * h + 1), 1), "c1": ("pd%d" % (2 * h + 1), 2),
+                    "sm": ("pd%d" % (2 * h + 1), 3)}[name]
+        else:
+            b, j = "ph%d" % h, {"key": 0, "x1": 2, "x2": 3, "x3": 4, "uo": 0, "zt": 1, "a2": 2, "c2": 3, "l1": 4, "a1": 5, "c1": 6, "sm": 7}[name]
+            if name == "key":
+                return T[b][0:W, 0:128], [b + "_0", b + "_1"]
+        if name == "sm":
+            return (T[b][:, W * j:W * j + NL], T[b][:, W * j + 8:W * j + 8 + NL]), ["%s_%d" % (b, j)]
+        return T[b][:, W * j:W * j + W], ["%s_%d" % (b, j)]
+
+    def state(t, h):
+        tl = T["tl%d" % h]
+        return tl[:, t, 0:W], tl[:, t, W:2 * W], tl[:, t, 2 * W:3 * W], "L%d%d" % (t, h), "a%d%d" % (t, h), "C%d%d" % (t, h)
+
+    def index(t, h, final):
+        H = str(h)
+        L, a, Cc, ln, an, cn = state(t, h)
+        v1, v = T["wf" + H][:, 0, :], T["wi" + H][:, 0, :]
+        tt(v1, pq[:, 2 * W * h:2 * W * h + W], a, A.mult, ["pq_L" + H, an], ["v1" + H], W)
+        tt(v, pq[:, 2 * W * h + W:2 * W * h + 2 * W], v1, A.add, ["pq_Q" + H, "v1" + H], ["v" + H], W)
+        ts(v, v, 5, 4095, A.arith_shift_right, A.bitwise_and, ["v" + H], ["v" + H], W)
+        if final:
+            x1, k1 = slot(h, "x1")
+            tt(v, x1, v, A.max, k1 + ["v" + H], ["v" + H], W)
+            ts(T["off" + H][:], v, 4096.0, None, A.min, None, ["v" + H], ["off" + H], W)
+        else:
+            cp(T["off" + H][:], v, ["v" + H], ["off" + H], W)
+
+    def xnames(t):
+        return ["Xz%d" % (t % 2)] + (["Xl%d" % j for j in range(4)] if t == 0 else []) + ["X%d%d" % (t % 2, h) for h in range(NP)]
+
+    def gather(t, h):
+        H, n = str(h), W // NU
+        for c in range(NU):
+            src = T["X%d" % (t % 2)][:, 0:4112].indirect(T["off" + H][:, n * c:n * c + n])
+            either(T["rec" + H][:, 16 * n * c:16 * n * (c + 1)], src, xnames(t) + ["off" + H], ["rec%s%d" % (H, c)], ("g", 16 * n))
+
+    def pick(h, rst, rn):
+        H = str(h)
+        (key, k0), pmin, bm = slot(h, "key"), T["pn" + H], T["bm" + H]
+        scan(pmin[0:W, :], rst, key, FAR, A.max if rn == "rstm" else A.min, A.min, [rn] + k0, ["least" + H], 128)
+        scan(bm[0:W, ::-1], T["rstm"][0:W, :], pmin[0:W, ::-1], 0.0, A.max, A.min, ["rstm", "least" + H], ["bm" + H], 128)
+        tt(T["ou" + H][0:W, 0, :], key, bm[0:W, :], A.is_equal, k0 + ["bm" + H], ["ohU" + H], 128)
+
+    def step(t, h, si):
+        H, s = str(h), SH[si]
+        L, a, Cc, ln, an, cn = state(t, h)
+        (key, k0), (x1, k1), (x2, k2), (x3, k3) = [slot(h, x) for x in ("key", "x1", "x2", "x3")]
+        index(t, h, False)
+        eqk, w, m = T["wb" + H][:, 0, :], T["wh" + H][:, 0, :], T["wb" + H][:, 1, :]
+        mm([(x1, M["SI%d" % si], a, W)], ["SI%d" % si, an], k1)
+        ts(eqk, x1, 0.0, C["kB"], A.is_equal, A.add, k1 + ["kB"], ["eqk" + H], W)
+        terms, R = [(key, eqk, M["BI"], 128), (key, one, RW["rgo"], 128)], ["eqk" + H, "BI", "r1", "rgo"]
+        for e in range(si):
+            terms.append((key, T["ex" + H][:, e, :], M["pen%d%d" % (e, si)], 128))
+            R += ["ex%d%d" % (e, h), "pen%d%d" % (e, si)]
+        mm(terms, R, k0, last=False)
+        rec, abd, nq = T["rec" + H], T["abd" + H], W // 64
+        gather(t, h)
+        for q in range(nq):
+            for kh in range(2):
+                b = kh if NP == 4 else 2 * (q ^ h if t == 0 or si or h else h) + kh
+                pd, pn = T["pd%d" % b], ["pd%d_%d" % (b, j) for j in range(4)]
+                terms = []
+                for kk in range(8):
+                    for sign in ("I", "nI"):
+                        k = (8 * kh + kk + (s if sign == "nI" else 0)) & 15
+                        terms.append((pd[:, kk::8], M[sign], rec[:, 1024 * q + k:1024 * q + 1024:16], 64))
+                for x in range(0, 16, PAR["pu"]):
+                    mm(terms[x:x + PAR["pu"]], ["I", "nI"] + ["rec%s%d" % (H, c) for c in range(q * NU // nq, (q + 1) * NU // nq)], pn, pairs=True)
+                o = abd[:, 8 * W * kh + 512 * q:8 * W * kh + 512 * q + 512]
+                op("act", [lambda o=o, pd=pd: S.activation(o, pd[:], F.Abs)], pn, ["abd%s%d%d" % (H, kh, q)], 512)
+        for kh in range(2):
+            mm([(T["ph" + H][0:W, 8 * kh + kk:128:16], abd[:, 8 * W * kh + kk:8 * W * (kh + 1):8], T["blkD"][:], 64) for kk in range(8)],
+               ["blkD"] + ["abd%s%d%d" % (H, kh, q) for q in range(nq)], k0, first=False, last=kh == 1)
+        pick(h, rs[0:W, 128 * h:128 * h + 128], "thr")
+        en, oh = "ex%d%d" % (si, h), T["ex" + H][:, si, :]
+        if (t, si) != (NV - 1, 2):
+            tt(T["go"][0:W, 8 * h:8 * h + 8], T["pn" + H][0:W, 15::16], rs[0:W, 128 * h:128 * h + 128:16], A.is_lt, ["least" + H, "thr"], ["go" + H], 8)
+        mm([(x2, T["ou" + H][0:W, 0, :], T["mb"][0:W, 0, 0:W], W)], ["ohU" + H, "I"], k2)
+        either(oh, x2, k2, [en], W)
+        mm([(x1, M["IJ%d" % si], oh, W)], [en, "IJ%d" % si], k1)
+        tt(w, x1, a, A.mult, k1 + [an], ["w" + H], W)
+        xd, kd = (pm[:, 384:384 + W], ["pm_d"]) if PAR["dm"] else (x2, k2)
+        mm([(xd, M["sig%d" % si], w, W)], ["sig%d" % si, "w" + H], kd)
+        ad = T["wf" + H][:, 1, :]
+        if PAR["relu"]:
+            mm([(x3, M["I2h"], a, W), (x3, M["bit%d" % si], w, W)], ["I2h", "bit%d" % si, an, "w" + H], k3)
+        mm([(x1, M["I2h"], a, W), (x1, M["nblk"], w, W)], ["I2h", "nblk", an, "w" + H], k1)
+        if PAR["relu"]:
+            affine(ad, xd, "relu", 2.0, 0.0, kd, ["ad" + H], W)
+            tt(m, x3, ad, A.is_equal, k3 + ["ad" + H], ["m" + H], W)
+        else:
+            op("act", [lambda: S.activation(ad, xd, F.Abs)], kd, ["ad" + H], W)
+            tt(m, x1, ad, A.is_equal, k1 + ["ad" + H], ["m" + H], W)
+        tt(x1, x1, m, A.mult, k1 + ["m" + H], k1, W)
+        tt(a, a, x1, A.subtract, [an] + k1, [an], W)
+        cc = pm[:, W * h:W * h + W]
+        mm([(cc, M["Sh%d" % si], Cc, W), const(cc, "rBIG"), (cc, M["nBI"], oh, W)], ["Sh%d" % si, cn, "r1", "rBIG", en, "nBI"], ["pm_c" + H])
+        tt(Cc, cc, Cc, A.min, ["pm_c" + H, cn], [cn], W)
+
+    def count():
+        go, o, n = T["go"], T["one16"][0:W, 0:W], 8 * NP
+        terms = [(pm[0:W, 256:256 + n], o, go[0:W, :], n)]
+        for r in range(8, n, 8):
+            terms += [(pm[0:W, 256:256 + n - r], o, go[0:W, r:n], n), (pm[0:W, 256 + n - r:256 + n], o, go[0:W, 0:r], n)]
+        mm(terms, ["one16"] + ["go%d" % h for h in range(NP)], ["pm_n"])
+        cnt = T["cnt"][0:W, :]
+        tt(cnt, pm[0:W, 256:256 + n], cnt, A.add, ["pm_n", "cnt"], ["cnt"], n)
+        ts(cnt, cnt, 511, None, A.bitwise_and, None, ["cnt"], ["cnt"], n)
+        tt(rs[0:W, ::16], T["th16"][0:W, :], cnt, A.add, ["th16", "cnt"], ["thr"], n)
+
+    def refill(t, h):
+        H, last = str(h), t == NV - 1
+        L, a, Cc, ln, an, cn = state(t, h)
+        (key, k0), (x1, k1), (x2, k2), (x3, k3) = [slot(h, x) for x in ("key", "x1", "x2", "x3")]
+        ex, ohU, kexp = T["ex" + H], T["ou" + H][0:W, 0, :], T["ou" + H]
+        J, exn = ["J%d" % e for e in range(3)], ["ex%d%d" % (e, h) for e in range(3)]
+        off = 0.0 if last else 2048.0
+        si_, sf, su, sk = T["si" + H], T["sf" + H], T["su" + H], T["sk" + H]
+        z, nb, wa, wc = T["wb" + H][:, 3, :], T["wb" + H][:, 2, :], T["wh" + H][:, 1, :], T["wh" + H][:, 2, :]
+        (zp, ul), ks = slot(h, "sm")
+        mm([(x1, M[J[e]], ex[:, e, :], W) for e in range(3)], exn + J, k1)
+        index(t, h, True)
+        gather(t, h)
+        mm([(key, Cc, M["n16h"], 128), (key, T["mb"][:, 0, 0:W], T["mk"][:], 128)] + [(key, ex[:, e, :], M[J[e]], 128) for e in range(3)],
+           [cn, "n16h", "I", "mk"] + J + exn, k0)
+        pick(h, T["rstm"][0:W, :], "rstm")
+        cp(si_[0:W, 4, :], T["pn" + H][0:W, 15::16], ["least" + H], ["sx" + H], 8)
+        ts(sk[0:W, :], si_[0:W, 4, :], 15, None, A.bitwise_and, None, ["sx" + H], ["sk" + H], 8)
+        tt(kexp[:, 1, :], sk[:, 0:8].indirect(T["l16"][:, 0:8]), M["mP"], A.mult, ["sk" + H, "l16", "mP"], ["kexp" + H], 128, True)
+        mm([(zp, kexp[0:W, 1, :], T["blkD"][0:W, 0:NL], 8), (zp, M["I"], T["cz"][:, 0:NL], 8)], ["kexp" + H, "blkD", "I", "cz"], ks)
+        ts(su[:, 0:NL], zp, C["rk16"], None, A.add, None, ks + ["rk16"], ["zo" + H], 8)
+        en = "ohU" + H
+        mm([(x2, ohU, T["mb"][0:W, 0, 0:W], W)], [en, "I"], k2)
+        mm([(x3, ohU, T["mb"][0:W, 2, 0:W], W)] + [(x3, M[J[e]], ex[:, e, :], W) for e in range(3)], [en, "BI"] + J + exn, k3)
+        affine(nb, x3, "id", -(8192.0 + off) / BIG, 8192.0, k3, ["nb" + H], W)
+        tt(wa, x2, a, A.mult, k2 + [an], ["wa" + H], W)
+        tt(wc, x2, Cc, A.mult, k2 + [cn], ["wc" + H], W)
+        rf, top, nq = T["rec" + H], T["top" + H], W // 64
+        rfn = ["rec%s%d" % (H, c) for c in range(NU)]
+        for c in range(nq):
+            scan(top[:, 1024 * c:1024 * c + 1024], T["rst1"][:], rf[:, 1024 * c:1024 * c + 1024], 0.0, A.mult, A.max,
+                 ["rst1"] + rfn[c * NU // nq:(c + 1) * NU // nq], ["top%s%d" % (H, c)], 512)
+        either(z, rf[:, 0:16 * W].indirect(su[:, 0:NL]), rfn + ["zo" + H], ["z" + H], ("g", W))
+        mm([(ul, T["Wb"][:, 15 - p:143 - p], T["wb" + H][:, 3, p::16], 8) for p in range(16)], ["Wb", "z" + H], ks)
+        ui, sl, u, n = [si_[:, j, 0:NL] for j in range(4)]
+        cp(ui, ul, ks, ["ui" + H], 8)
+        (uo, ku), (a2, ka2), (c2, kc2), (zt, kz), (l1, kl1), (a1, ka1), (c1, kc1) = [slot(h, x) for x in ("uo", "a2", "c2", "zt", "l1", "a1", "c1")]
+        mm([(zt, M["I"], z, W), (zt, M["I"], top[:, 15::16], W)], ["I", "z" + H] + ["top%s%d" % (H, c) for c in range(nq)], kz)
+        zti, uoi, ae, ck = [T["wi" + H][:, j, :] for j in range(1, 5)]
+        ts(zti, zt, 0.5, -0.25, A.mult, A.add, kz, ["zti" + H], W)
+        ts(sl, ui, 15, None, A.bitwise_and, None, ["ui" + H], ["sl" + H], 8)
+        tt(sl, sl, T["csl"][:, 0:NL], A.add, ["sl" + H, "csl"], ["sl" + H], 8)
+        cp(su[:, 8:8 + NL], sl, ["sl" + H], ["sl16" + H], 8)
+        dst, dn = T["X%d" % ((t + 1) % 2)], "X%d%d" % ((t + 1) % 2, h)
+        win = dst[:, 16 * W * h:16 * W * (h + 1)]
+        op("dve", [lambda: V.tensor_copy(win.indirect(su[:, 8:8 + NL]), zti)], ["zti" + H, "sl16" + H, dn], [dn], ("s", W))
+        if last:
+            dma("sp", T["yx"][:, 16 * W * h:16 * W * (h + 1)], win, [dn], [], "sx" + H, 3500)
+        ts(u, ui, 4095, None, A.bitwise_and, None, ["ui" + H], ["u" + H], 8)
+        ts(sf[:, 0, 0:NL], u, -2048.0, None, A.add, None, ["u" + H], ["t1" + H], 8)
+        ts(sf[:, 1, 0:NL], u, 3232.0, None, A.add, None, ["u" + H], ["t2" + H], 8)
+        tt(n, sf[:, 0, 0:NL], sf[:, 1, 0:NL], A.mult, ["t1" + H, "t2" + H], ["n" + H], 8)
+        ts(n, n, 5, 1023, A.arith_shift_right, A.bitwise_and, ["n" + H], ["n" + H], 8)
+        cp(su[:, 16:16 + NL], n, ["n" + H], ["nl" + H], 8)
+        mm([(uo, M["WqO"], z, W)], ["WqO", "z" + H], ku)
+        cp(uoi, uo, ku, ["uo" + H], W)
+        ts(uoi, uoi, 4095, None, A.bitwise_and, None, ["uo" + H], ["uo" + H], W)
+        keep = "r10240" if last else "r8192"
+        mm([(a2, M["odd"], wa, W), (a2, M["I"], nb, W), const(a2, "rodd")], ["odd", "wa" + H, "I", "nb" + H, "r1", "rodd"], ka2)
+        mm([(c2, M["blk"], wc, W), (c2, M["I2"], nb, W)] + ([] if last else [const(c2, "r4096")]), ["blk", "wc" + H, "I2", "nb" + H, "r1", "r4096"], kc2)
+        mm([(l1, M["Ih"], L, W), (l1, M["nI"], nb, W), const(l1, keep)], ["Ih", ln, "nI", "nb" + H, "r1", keep], kl1)
+        mm([(a1, M["Ih"], a, W), (a1, M["nI"], nb, W), const(a1, keep)], ["Ih", an, "nI", "nb" + H, "r1", keep], ka1)
+        mm([(c1, M["Ih"], Cc, W), (c1, M["nI"], nb, W), const(c1, "r8192")], ["Ih", cn, "nI", "nb" + H, "r1", "r8192"], kc1)
+        body = T["rbs"][:, 0:1024].indirect(su[:, 16:16 + NL])
+        sL, sA = T["wf" + H][:, 2, :], T["wf" + H][:, 3, :]
+        to = T[("tf" if last else "to") + H]
+        o = ["%s%d%d" % ("f" if last else "o", h, j) for j in range(3)]
+        ts(ck, c2, 0.5, -0.25, A.mult, A.add, kc2, ["ck" + H], W)
+        tt(to[:, 2 * W:3 * W], c1, ck, A.min, kc1 + ["ck" + H], [o[2]], W)
+        tt(ae, body, uoi, A.mult, ["rbs", "nl" + H, "uo" + H], ["ae" + H], W, True)
+        if t:
+            ts(ae, ae, C["ev%d" % t], None, A.add, None, ["ae" + H, "ev%d" % t], ["ae" + H], W)
+        ts(ae, ae, 5, 4095, A.arith_shift_right, A.bitwise_and, ["ae" + H], ["ae" + H], W)
+        tt(sA, a2, ae, A.add, ka2 + ["ae" + H], ["sA" + H], W)
+        tt(to[:, W:2 * W], a1, sA, A.min, ka1 + ["sA" + H], [o[1]], W)
+        tt(sL, body, nb, A.add, ["rbs", "nl" + H, "nb" + H], ["sL" + H], W, True)
+        tt(to[:, 0:W], l1, sL, A.min, kl1 + ["sL" + H], [o[0]], W)
+        if last:
+            for j, y in enumerate(("yl", "ya", "yc")):
+                dma("sp", T[y][:, W * h:W * h + W], to[:, W * j:W * j + W], [o[j]], [], "sy%d%d" % (h, j), 2500)
+            return
+        land, ar, sn = T["tl" + H][:, t + 1, :], "ar%d%d" % (t, h), "sn%d%d" % (t, h)
+        snd = op("pool", [lambda: g.remote_dma(land, to[:], T.sem[ar], T.sem[sn], pid, rid, mask)], o, [], 1000, sem=sn, inc=-len(eng), lat=2000)
+        op(None, [], [], ["%s%d%d" % (x, t + 1, h) for x in "LaC"], 0, sem=ar, inc=-len(eng), lat=200, after=snd)
+
+    for t in range(NV):
+        stage[0] = 4 * NP * t
+        dma("sp", T["X%d" % ((t + 1) % 2)][:, 0:4096], T["X%d" % (t % 2)][:, 0:4096], xnames(t)[1:], ["X%d%d" % ((t + 1) % 2, h) for h in range(NP)],
+            "cx%d" % t, 6000)
+        for si in range(4):
+            for h in range(NP):
+                stage[0] = 4 * NP * t + NP * si + h
+                if si == 0:
+                    L, ln = state(t, h)[0], state(t, h)[3]
+                    lp, qp = pq[:, 2 * W * h:2 * W * h + W], pq[:, 2 * W * h + W:2 * W * h + 2 * W]
+                    mm([(lp, M["Ih"], L, W), const(lp, "r3232")], ["Ih", ln, "r1", "r3232"], ["pq_L%d" % h])
+                    mm([(qp, M["I2080"], L, W)], ["I2080", ln], ["pq_Q%d" % h])
+                if si < 3:
+                    step(t, h, si)
+                else:
+                    refill(t, h)
+            if si < 3 and (t, si) != (NV - 1, 2):
+                count()
+    return ops
+
+
+def cost(o, par):
+    c = o["cyc"]
+    if o["q"] is None:
+        return 0.0
+    if o["q"] == "pe":
+        return c * par["pe"] + par["fix"]
+    if isinstance(c, tuple):
+        c = 60 + c[1] * (par["g"] if c[0] == "g" else 2.4 * par["g"])
+    return max(c, 64) * par["cyc"] + par["fix"]
+
+
+def edges(ops):
+    writer, readers, deps = {}, {}, []
+    for i, o in enumerate(ops):
+        d = set()
+        for r in o["R"]:
+            if r in writer:
+                d.add(writer[r])
+        for w in o["W"]:
+            if w in writer:
+                d.add(writer[w])
+            d.update(readers.get(w, ()))
+        if o["after"] is not None:
+            d.add(o["after"])
+        d.discard(i)
+        deps.append(d)
+        for r in o["R"]:
+            readers.setdefault(r, []).append(i)
+        for w in o["W"]:
+            writer[w] = i
+            readers[w] = []
+    return deps
+
+
+def length(ops, par, plan):
+    free, end = {}, [0.0] * len(ops)
+    for i in plan[0]:
+        q = plan[3][i]
+        st = max([free.get(q, 0.0) if q else 0.0] + [end[d] + (0.0 if q == "pe" == ops[d]["q"] else par["hop"]) for d in plan[1][i]])
+        free[q] = st + cost(ops[i], par)
+        end[i] = free[q] + ops[i]["lat"]
+    return max(end)
+
+
+def place(ops, par, dur, pre, delay, rank, qs):
+    n = len(ops)
+    left = [len(p) for p in pre]
+    post = [[] for _ in range(n)]
+    for i in range(n):
+        for d in pre[i]:
+            post[d].append(i)
+    ready = sorted((rank[i], i) for i in range(n) if left[i] == 0)
+    line, used, st, out = {}, {}, [0.0] * n, list(qs)
+    hop = par["hop"]
+    while ready:
+        i = ready.pop(0)[1]
+        o = ops[i]
+        r = max([0.0] + [st[d] + dur[d] + delay(d, i) for d in pre[i]])
+        best = None
+        for me in (("dve", "act") if qs[i] == "any" else (qs[i],)):
+            t = r
+            moved = me is not None
+            while moved:
+                moved = False
+                for a, b in reversed(line.get(me, ())):
+                    if b <= t:
+                        break
+                    if a < t + dur[i]:
+                        t, moved = b, True
+                        break
+                for bk in o["banks"]:
+                    for a, b, q in used.get(bk, ())[-40:]:
+                        if q != me and a - hop < t + dur[i] and b + hop > t:
+                            t, moved = b + hop, True
+            sc = t + (par["pen"] if me == "dve" else 0.0)
+            if best is None or sc < best[0]:
+                best = (sc, t, me)
+        t, me = best[1:]
+        st[i], out[i] = t, me
+        if me:
+            ln = line.setdefault(me, [])
+            k = len(ln)
+            while k and ln[k - 1][0] > t:
+                k -= 1
+            ln.insert(k, (t, t + dur[i]))
+        for bk in o["banks"]:
+            u = used.setdefault(bk, [])
+            u.append((t, t + dur[i], me))
+            u.sort()
+        for j in post[i]:
+            left[j] -= 1
+            if left[j] == 0:
+                ready.append((rank[j], j))
+        ready.sort()
+    return st, out
+
+
+def refine(ops, par):
+    n = len(ops)
+    dur = [cost(o, par) for o in ops]
+    deps = edges(ops)
+    succ = [[] for _ in range(n)]
+    for i in range(n):
+        for d in deps[i]:
+            succ[d].append(i)
+    qs = [o["q"] for o in ops]
+
+    def fwd(d, i):
+        return ops[d]["lat"] + (0.0 if qs[d] == "pe" == qs[i] else par["hop"])
+    per, extra = par["per"], par["extra"]
+    late = [1e12] * n
+    for i in range(n - 1, -1, -1):
+        s = ops[i]["stage"]
+        if ops[i]["W"] and ops[i]["W"][0][:3] == "off":
+            late[i] = min(late[i], s * per / NP + s // (4 * NP) * extra)
+        if late[i] == 1e12:
+            late[i] = NV * (4 * per + extra) + s % NP * per / NP
+        for d in deps[i]:
+            late[d] = min(late[d], late[i] - dur[d] - fwd(d, i))
+    if par.get("bias"):
+        late = [late[i] + par["bias"][i] for i in range(n)]
+    st, out = place(ops, par, dur, deps, fwd, late, qs)
+    best = None
+    for _ in range(par["rounds"]):
+        order = sorted(range(n), key=lambda i: (st[i], i))
+        full, users = [set(d) for d in deps], {}
+        for i in order:
+            for b in ops[i]["banks"]:
+                u = users.setdefault(b, {})
+                full[i].update(j for q, j in u.items() if q != out[i])
+                u[out[i]] = i
+        cand = [order, full, 0.0, out]
+        cand[2] = length(ops, par, cand)
+        if best is None or cand[2] < best[2]:
+            best = cand
+        back = place(ops, par, dur, succ, lambda d, i: fwd(i, d), [-(st[i] + dur[i] + ops[i]["lat"]) for i in range(n)], qs)[0]
+        st, out = place(ops, par, dur, deps, fwd, [-(back[i] + dur[i]) for i in range(n)], qs)
+    return best
+
+
+def rank_program(g, core, T, topo):
+    if T.rank_of(core) is None:
+        return
+    ops = build(g, core, T, topo)
+    if "plan" not in CACHE:
+        CACHE["plan"] = refine(ops, PAR)
+    order, deps = CACHE["plan"][:2]
+    for i, o in enumerate(ops):
+        if o["q"] == "any":
+            o["q"] = CACHE["plan"][3][i]
+            o["calls"] = o["alt"][o["q"]]
+    queue = {"pe": g.tensor, "dve": g.vector, "act": g.scalar, "pool": g, "sp": g.sync}
+    total, known, mark, clock = {}, {q: {} for q in queue}, {}, {}
+    for i in order:
+        o = ops[i]
+        q = o["q"]
+        sem = o["sem"] or q
+        if q is None:
+            mark[i] = (sem, -o["inc"])
+            clock[i] = {sem: -o["inc"]}
+            total[sem] = -o["inc"]
+            continue
+        kn = known[q]
+        need = {}
+        for d in deps[i]:
+            if not (q == "pe" and ops[d]["q"] == "pe"):
+                s, c = mark[d]
+                if kn.get(s, 0) < c:
+                    need.setdefault(s, []).append(d)
+        tops = sorted((max(ds, key=lambda d: mark[d][1]) for ds in need.values()), reverse=True, key=lambda d: len(clock[d]))
+        for d in tops:
+            s, c = mark[d]
+            if kn.get(s, 0) < c:
+                queue[q].wait_ge(T.sem[s], c)
+                for s2, c2 in clock[d].items():
+                    if kn.get(s2, 0) < c2:
+                        kn[s2] = c2
+        for call in o["calls"]:
+            ins = call()
+            if o["inc"] > 0:
+                ins.then_inc(T.sem[sem], o["inc"])
+            total[sem] = total.get(sem, 0) + abs(o["inc"])
+        mark[i] = (sem, total[sem])
+        clock[i] = dict(kn)
+        clock[i][sem] = total[sem]
+    for s in sorted(total):
+        g.wait_ge(T.sem[s], total[s])

@@ -20,13 +20,13 @@ SCRATCH = {"X0": ("sbuf", [128, 4112], b16), "X1": ("sbuf", [128, 4112], b16), "
            "l16i": ("sbuf", [128, 8], i32), "l16": ("sbuf", [128, 8], u16),
            "rstm": ("sbuf", [128, 128], f32), "rst1": ("sbuf", [128, 1024], b16), "rows": ("sbuf", [128, 1024], b16),
            "one16": ("sbuf", [128, 128], b16), "I32": ("sbuf", [128, 8], f32), "blkD": ("sbuf", [128, 8], b16),
-           "Wb": ("sbuf", [128, 144], b16), "mb": ("sbuf", [128, 16, 128], b16), "mh": ("sbuf", [128, 19, 128], h16),
+           "Wb": ("sbuf", [128, 144], b16), "mb": ("sbuf", [128, 17, 128], b16), "mh": ("sbuf", [128, 19, 128], h16),
            "pm": ("psum", [128, 512], f32), "pq": ("psum", [128, 512], f32)}
 for _h in range(NP):
     for _n, _sh, _d in (("tl", [128, NV, 3 * W], h16), ("to", [128, 3 * W], h16), ("tf", [128, 3 * W], f32),
                         ("rec", [128, 16 * W], b16), ("abd", [128, 16 * W], b16), ("top", [128, 16 * W], b16), ("ex", [128, 3, W], b16),
                         ("pn", [128, 128], f32), ("bm", [128, 128], f32), ("ou", [128, 2, 128], b16),
-                        ("off", [128, W], u16), ("wf", [128, 4, W], f32), ("wi", [128, 5, W], i32), ("wh", [128, 3, W], h16),
+                        ("off", [128, W], u16), ("hl", [128, 2 * W], h16), ("w2", [128, 2 * W], h16), ("wf", [128, 4, W], f32), ("wi", [128, 5, W], i32), ("wh", [128, 3, W], h16),
                         ("wb", [128, 4, W], b16), ("sk", [128, 8], i32),
                         ("si", [128, 5, 8], i32), ("sf", [128, 2, 8], f32), ("su", [128, 24], u16)):
         SCRATCH[_n + str(_h)] = ("sbuf", _sh, _d)
@@ -38,8 +38,8 @@ SEMAPHORES = ["pe", "dve", "act", "pool", "lx0", "lx1", "lx2", "lx3", "ll", "la"
     ["cx%d" % _t for _t in range(NV)] + ["sx%d" % _h for _h in range(NP)] + ["sy%d%d" % (_h, _j) for _h in range(NP) for _j in range(3)] + \
     ["%s%d%d" % (_p, _t, _h) for _p in ("ar", "sn") for _t in range(NV - 1) for _h in range(NP)]
 
-PAR = {"g": 1.56, "cyc": 0.83 * 1.2, "pe": 0.42 * 1.2, "fix": 30.0, "hop": 120.0, "pen": 0.0, "per": 10500.0, "extra": 4000.0,
-       "dm": 0, "relu": 0, "pu": 8, "rounds": 6}
+PAR = {"g": 1.56, "cyc": 0.87, "pe": 0.55, "fix": 25.0, "hop": 160.0, "nd": (2, 2, 2), "ul": 0, "hl": 1, "heat": 500.0, "tries": 38000, "bias": {}, "force": {}, "pen": 600.0, "per": 8500.0, "extra": 4000.0,
+       "dm": 0, "relu": 0, "pu": 8, "rounds": 2}
 CACHE = {}
 
 
@@ -163,15 +163,18 @@ def build(g, core, T, topo):
     matrix("blk", "mh", 5, mg, "mg", C["rg"], 1.0, ["rg"])
     matrix("odd", "mh", 6, T["mgO"][:], "mgO", C["rg"], 1.0, ["rg"])
     matrix("WqO", "mb", 5, T["mgE"][:], "mgE", C["rg"], C["wq"], ["rg", "wq"])
+    matrix("Wq", "mb", 16, mg, "mg", C["rg"], C["wq"], ["rg", "wq"])
     matrix("mP", "mb", 6, T["mk"][:], "mk", C["rk"], 1.0 / 16, ["rk"])
     for si in range(3):
         s = SH[si]
         matrix("Sh%d" % si, "mh", 7 + si, tx[:, :, s:s + 16], "tx", 0.0, 1.0)
         M["SI%d" % si] = T["mh"][:, 10 + si, :]
         tt(M["SI%d" % si], M["Sh%d" % si], M["Ih"], A.subtract, ["Sh%d" % si, "Ih"], ["SI%d" % si], 128)
+        matrix("J%d" % si, "mb", 7 + si, tx[:, :, 16 - s:32 - s], "tx", 0.0, BIG)
+        if PAR["hl"]:
+            continue
         matrix("sig%d" % si, "mh", 13 + si, mg, "mg", C["rg"], C["sg%d" % si], ["rg", "sg%d" % si])
         matrix("bit%d" % si, "mh", 16 + si, mg, "mg", C["rg"], C["bt%d" % si], ["rg", "bt%d" % si])
-        matrix("J%d" % si, "mb", 7 + si, tx[:, :, 16 - s:32 - s], "tx", 0.0, BIG)
         matrix("IJ%d" % si, "mb", 10 + si, tx[:, :, 16 - s:32 - s], "tx", 0.0, 1.0)
         tt(M["IJ%d" % si], M["IJ%d" % si], M["I"], A.add, ["IJ%d" % si, "I"], ["IJ%d" % si], 128)
     for j, (e, si) in enumerate(((0, 1), (0, 2), (1, 2))):
@@ -269,7 +272,12 @@ def build(g, core, T, topo):
         (key, k0), (x1, k1), (x2, k2), (x3, k3) = [slot(h, x) for x in ("key", "x1", "x2", "x3")]
         index(t, h, False)
         eqk, w, m = T["wb" + H][:, 0, :], T["wh" + H][:, 0, :], T["wb" + H][:, 1, :]
-        mm([(x1, M["SI%d" % si], a, W)], ["SI%d" % si, an], k1)
+        if PAR["hl"]:
+            hl, w2 = T["hl" + H], T["w2" + H]
+            mm([(x3, M["Sh%d" % si], a, W)], ["Sh%d" % si, an], k3)
+            tt(hl[:, 0:W], x3, a, A.max, k3 + [an], ["hi" + H], W)
+            tt(hl[:, W:2 * W], x3, a, A.min, k3 + [an], ["lo" + H], W)
+        mm([(x1, M["SI%d" % si], a, W)], ["SI%d" % si, an] + k3, k1)
         ts(eqk, x1, 0.0, C["kB"], A.is_equal, A.add, k1 + ["kB"], ["eqk" + H], W)
         terms, R = [(key, eqk, M["BI"], 128), (key, one, RW["rgo"], 128)], ["eqk" + H, "BI", "r1", "rgo"]
         for e in range(si):
@@ -278,27 +286,74 @@ def build(g, core, T, topo):
         mm(terms, R, k0, last=False)
         rec, abd, nq = T["rec" + H], T["abd" + H], W // 64
         gather(t, h)
-        for q in range(nq):
-            for kh in range(2):
-                b = kh if NP == 4 else 2 * (q ^ h if t == 0 or si or h else h) + kh
-                pd, pn = T["pd%d" % b], ["pd%d_%d" % (b, j) for j in range(4)]
-                terms = []
-                for kk in range(8):
-                    for sign in ("I", "nI"):
-                        k = (8 * kh + kk + (s if sign == "nI" else 0)) & 15
-                        terms.append((pd[:, kk::8], M[sign], rec[:, 1024 * q + k:1024 * q + 1024:16], 64))
-                for x in range(0, 16, PAR["pu"]):
-                    mm(terms[x:x + PAR["pu"]], ["I", "nI"] + ["rec%s%d" % (H, c) for c in range(q * NU // nq, (q + 1) * NU // nq)], pn, pairs=True)
-                o = abd[:, 8 * W * kh + 512 * q:8 * W * kh + 512 * q + 512]
-                op("act", [lambda o=o, pd=pd: S.activation(o, pd[:], F.Abs)], pn, ["abd%s%d%d" % (H, kh, q)], 512)
-        for kh in range(2):
-            mm([(T["ph" + H][0:W, 8 * kh + kk:128:16], abd[:, 8 * W * kh + kk:8 * W * (kh + 1):8], T["blkD"][:], 64) for kk in range(8)],
-               ["blkD"] + ["abd%s%d%d" % (H, kh, q) for q in range(nq)], k0, first=False, last=kh == 1)
+        recn = ["rec%s%d" % (H, c) for c in range(NU)]
+        own = not (t == 0 or si or h)
+        for kh in range(2 if NP == 4 else 0):
+            pd, pn = T["pd%d" % kh], ["pd%d_%d" % (kh, j) for j in range(4)]
+            terms = [(pd[:, k::8], M[sign], rec[:, (8 * kh + k + d) & 15::16], 64) for k in range(8) for sign, d in (("I", 0), ("nI", s))]
+            for x in range(0, 16, PAR["pu"]):
+                mm(terms[x:x + PAR["pu"]], ["I", "nI"] + recn, pn, pairs=True)
+            o = abd[:, 512 * kh:512 * kh + 512]
+            op("act", [lambda o=o, pd=pd: S.activation(o, pd[:], F.Abs)], pn, ["abd%s%d" % (H, kh)], 512)
+            mm([(T["ph" + H][0:W, 8 * kh + k:128:16], abd[:, 512 * kh + k:512 * kh + 512:8], T["blkD"][:], 64) for k in range(8)],
+               ["blkD", "abd%s%d" % (H, kh)], k0, first=False, last=kh == 1)
+        for q in range(2 if NP == 2 else 0):
+            b = 2 * h + q
+            pd, pn = T["pd%d" % b], ["pd%d_%d" % (b, j) for j in range(4)]
+            terms = [(pd[:, k::8], M[sign], rec[:, 1024 * q + ((k + d) & 15):1024 * q + 1024:16], 64) for k in range(8) for sign, d in (("I", 0), ("nI", s))]
+            for x in range(0, 16, PAR["pu"]):
+                mm(terms[x:x + PAR["pu"]], ["I", "nI"] + recn[q * NU // 2:(q + 1) * NU // 2], pn, pairs=True)
+            o = abd[:, 512 * q:512 * q + 512]
+            op("act", [lambda o=o, pd=pd: S.activation(o, pd[:], F.Abs)], pn, ["abd%s0%d" % (H, q)], 512)
+        if NP == 2:
+            mm([(T["ph" + H][:, k:128:16], abd[:, k:1024:8], T["blkD"][:], 64) for k in range(8)], ["blkD", "abd%s00" % H, "abd%s01" % H], k0,
+               first=False, last=False)
+        nd = PAR["nd"][si]
+        for q in range(2 if NP == 2 else 0):
+            b = 2 * (h if own else 1 - h) + q
+            pd, pn = T["pd%d" % b], ["pd%d_%d" % (b, j) for j in range(4)]
+            ks = list(range(8 + 4 * q, 12 + 4 * q))
+            pk = [k for k in ks if k < 16 - nd]
+            an_ = []
+            if pk:
+                terms = [(pd[:, 128 * (k % 4):128 * (k % 4) + 128], M[sign], rec[:, (k + d) & 15::16], 128) for k in pk for sign, d in (("I", 0), ("nI", s))]
+                for x in range(0, len(terms), PAR["pu"] // 2):
+                    mm(terms[x:x + PAR["pu"] // 2], ["I", "nI"] + recn, pn, pairs=True)
+                o, i_ = abd[:, 128 * pk[0]:128 * pk[-1] + 128], pd[:, 0:128 * len(pk)]
+                op("act", [lambda o=o, i_=i_: S.activation(o, i_, F.Abs)], pn, ["abd%s1%d" % (H, q)], 128 * len(pk))
+                an_.append("abd%s1%d" % (H, q))
+            dk = [k for k in ks if k not in pk]
+            if dk:
+                for k in dk:
+                    tt(abd[:, 128 * k:128 * k + 128], rec[:, k::16], rec[:, (k + s) & 15::16], A.subtract, recn, ["df%s%d" % (H, k)], 128)
+                o = abd[:, 128 * dk[0]:128 * dk[-1] + 128]
+                dn = ["df%s%d" % (H, k) for k in dk]
+                op("act", [lambda o=o: S.activation(o, o, F.Abs)], dn, dn, 128 * len(dk))
+                an_ += dn
+            mm([(T["ph" + H][:, k:128:16], abd[:, 128 * k:128 * k + 128], T["blkD"][:], 64) for k in ks], ["blkD"] + an_, k0, first=False, last=q == 1)
         pick(h, rs[0:W, 128 * h:128 * h + 128], "thr")
         en, oh = "ex%d%d" % (si, h), T["ex" + H][:, si, :]
         if (t, si) != (NV - 1, 2):
             tt(T["go"][0:W, 8 * h:8 * h + 8], T["pn" + H][0:W, 15::16], rs[0:W, 128 * h:128 * h + 128:16], A.is_lt, ["least" + H, "thr"], ["go" + H], 8)
         mm([(x2, T["ou" + H][0:W, 0, :], T["mb"][0:W, 0, 0:W], W)], ["ohU" + H, "I"], k2)
+        cc = pm[:, W * h:W * h + W]
+        if PAR["hl"]:
+            mm([(x3, T["ou" + H][0:W, 0, :], T["mb"][0:W, 0, 0:W], W)], ["ohU" + H, "I"], k3)
+            tt(w2[:], T["ph" + H][:, 2 * W:4 * W], hl[:], A.mult, k2 + k3 + ["hi" + H, "lo" + H], ["w" + H], 2 * W)
+            mm([(x1, M["Ih"], a, W), (x1, M["nblk"], w2[:, 0:W], W)], ["Ih", "nblk", an, "w" + H], k1)
+            mm([(x3, M["blk"], w2[:, 0:W], W), (x3, M["nblk"], w2[:, W:2 * W], W)], ["blk", "nblk", "w" + H], k3)
+            ts(m, x1, 0.0, None, A.is_equal, None, k1, ["m" + H], W)
+            tt(x3, x3, m, A.mult, k3 + ["m" + H], k3, W)
+            tt(a, a, x3, A.subtract, [an] + k3, [an], W)
+            if PAR["dm"]:
+                mm([(pm[:, 384:384 + W], T["ou" + H][0:W, 0, :], T["mb"][0:W, 0, 0:W], W)], ["ohU" + H, "I"], ["pm_d"])
+                either(oh, pm[:, 384:384 + W], ["pm_d"], [en], W)
+            else:
+                either(oh, x2, k2, [en], W)
+            mm([(cc, M["Sh%d" % si], Cc, W), const(cc, "rBIG"), (cc, T["ou" + H][0:W, 0, :], T["mb"][0:W, 3, 0:W], W)],
+               ["Sh%d" % si, cn, "r1", "rBIG", "ohU" + H, "nBI"], ["pm_c" + H])
+            tt(Cc, cc, Cc, A.min, ["pm_c" + H, cn], [cn], W)
+            return
         either(oh, x2, k2, [en], W)
         mm([(x1, M["IJ%d" % si], oh, W)], [en, "IJ%d" % si], k1)
         tt(w, x1, a, A.mult, k1 + [an], ["w" + H], W)
@@ -364,9 +419,15 @@ def build(g, core, T, topo):
             scan(top[:, 1024 * c:1024 * c + 1024], T["rst1"][:], rf[:, 1024 * c:1024 * c + 1024], 0.0, A.mult, A.max,
                  ["rst1"] + rfn[c * NU // nq:(c + 1) * NU // nq], ["top%s%d" % (H, c)], 512)
         either(z, rf[:, 0:16 * W].indirect(su[:, 0:NL]), rfn + ["zo" + H], ["z" + H], ("g", W))
-        mm([(ul, T["Wb"][:, 15 - p:143 - p], T["wb" + H][:, 3, p::16], 8) for p in range(16)], ["Wb", "z" + H], ks)
         ui, sl, u, n = [si_[:, j, 0:NL] for j in range(4)]
-        cp(ui, ul, ks, ["ui" + H], 8)
+        if PAR["ul"]:
+            mm([(key, M["Wq"], z, W)], ["Wq", "z" + H], k0)
+            tt(T["bm" + H][:], key, M["mP"], A.mult, k0 + ["mP"], ["bm" + H], W)
+            scan(T["pn" + H][:], T["rst1"][:, 0:W], T["bm" + H][:], 0.0, A.mult, A.add, ["rst1", "bm" + H], ["least" + H], W)
+            ts(ui, T["pn" + H][:, 15::16], 16.0, None, A.mult, None, ["least" + H], ["ui" + H], 8)
+        else:
+            mm([(ul, T["Wb"][:, 15 - p:143 - p], T["wb" + H][:, 3, p::16], 8) for p in range(16)], ["Wb", "z" + H], ks)
+            cp(ui, ul, ks, ["ui" + H], 8)
         (uo, ku), (a2, ka2), (c2, kc2), (zt, kz), (l1, kl1), (a1, ka1), (c1, kc1) = [slot(h, x) for x in ("uo", "a2", "c2", "zt", "l1", "a1", "c1")]
         mm([(zt, M["I"], z, W), (zt, M["I"], top[:, 15::16], W)], ["I", "z" + H] + ["top%s%d" % (H, c) for c in range(nq)], kz)
         zti, uoi, ae, ck = [T["wi" + H][:, j, :] for j in range(1, 5)]
@@ -556,8 +617,11 @@ def refine(ops, par):
             late[i] = NV * (4 * per + extra) + s % NP * per / NP
         for d in deps[i]:
             late[d] = min(late[d], late[i] - dur[d] - fwd(d, i))
-    if par.get("bias"):
-        late = [late[i] + par["bias"][i] for i in range(n)]
+    for i in range(n):
+        key = "%d%s" % (ops[i]["stage"] % (4 * NP), (ops[i]["W"] + [""])[0])
+        late[i] += 100.0 * par["bias"].get(key, 0)
+        if qs[i] == "any":
+            qs[i] = {"a": "act", "d": "dve"}.get(par["force"].get(key), "any")
     st, out = place(ops, par, dur, deps, fwd, late, qs)
     best = None
     for _ in range(par["rounds"]):
@@ -577,12 +641,98 @@ def refine(ops, par):
     return best
 
 
+def polish(ops, par, plan, tries, seed=1):
+    n = len(ops)
+    deps = edges(ops)
+    qn = {"dve": 0, "act": 1, "pe": 2, "pool": 3, "sp": 4, None: 5}
+    dur = [cost(o, par) for o in ops]
+    lat = [o["lat"] for o in ops]
+    hop = par["hop"]
+    pre = [[(d, lat[d] + (0.0 if ops[d]["q"] == "pe" == ops[i]["q"] else hop)) for d in deps[i]] for i in range(n)]
+    succ = [[] for _ in range(n)]
+    for i in range(n):
+        for d in deps[i]:
+            succ[d].append(i)
+    names = sorted(set(b for o in ops for b in o["banks"]))
+    bk = [[3 * names.index(b) for b in o["banks"]] for o in ops]
+    order, q = list(plan[0]), [qn[x] for x in plan[3]]
+
+    def run(order, q):
+        end, why, last, use = [0.0] * (n + 1), [n] * n, [n] * 6, [n] * (3 * len(names))
+        for i in order:
+            me = q[i]
+            w = last[me] if me < 5 else n
+            s = end[w]
+            for d, x in pre[i]:
+                if end[d] + x > s:
+                    s, w = end[d] + x, d
+            for b in bk[i]:
+                for e in (0, 1, 2):
+                    if e != me and end[use[b + e]] + hop > s:
+                        w = use[b + e]
+                        s = end[w] + hop
+                use[b + me] = i
+            end[i], why[i], last[me] = s + dur[i], w, i
+        i = max(range(n), key=lambda j: end[j] + lat[j])
+        total, path = end[i] + lat[i], []
+        while why[i] < n:
+            if why[i] not in deps[i] or ops[i]["q"] == "any":
+                path.append((why[i], i))
+            i = why[i]
+        return total, path
+    cur, path = run(order, q)
+    best = (cur, order, q)
+    for it in range(tries):
+        seed = (seed * 1103515245 + 12345) % 2147483648
+        u, v = path[(seed >> 8) % len(path)]
+        o2, q2 = order, q
+        if ops[v]["q"] == "any" and (u in deps[v] or (seed >> 4) % 4 == 0):
+            q2 = list(q)
+            q2[v] = 1 - q2[v]
+        elif ops[u]["q"] == "any" and (seed >> 4) % 4 == 1:
+            q2 = list(q)
+            q2[u] = 1 - q2[u]
+        else:
+            a, b = order.index(u), order.index(v)
+            mid = order[a:b + 1]
+            if (seed >> 6) % 2:
+                move = {v}
+                for x in reversed(mid):
+                    if x in move:
+                        move.update(deps[x])
+                if u in move:
+                    continue
+                o2 = order[:a] + [x for x in mid if x in move] + [x for x in mid if x not in move] + order[b + 1:]
+            else:
+                move = {u}
+                for x in mid:
+                    if x in move:
+                        move.update(succ[x])
+                if v in move:
+                    continue
+                o2 = order[:a] + [x for x in mid if x not in move] + [x for x in mid if x in move] + order[b + 1:]
+        t, p = run(o2, q2)
+        if t <= cur + par["heat"] * (1.0 - it / tries) * ((seed >> 12) % 100) / 100.0:
+            cur, path, order, q = t, p, o2, q2
+            if t < best[0]:
+                best = (t, o2, q2)
+    back = {x: k for k, x in qn.items()}
+    out = [back[x] for x in best[2]]
+    full, users = [set(d) for d in deps], {}
+    for i in best[1]:
+        for b in ops[i]["banks"]:
+            u = users.setdefault(b, {})
+            full[i].update(j for e, j in u.items() if e != out[i])
+            u[out[i]] = i
+    return [best[1], full, best[0], out]
+
+
 def rank_program(g, core, T, topo):
     if T.rank_of(core) is None:
         return
     ops = build(g, core, T, topo)
     if "plan" not in CACHE:
-        CACHE["plan"] = refine(ops, PAR)
+        CACHE["plan"] = polish(ops, PAR, refine(ops, PAR), PAR["tries"])
     order, deps = CACHE["plan"][:2]
     for i, o in enumerate(ops):
         if o["q"] == "any":

@@ -1,55 +1,72 @@
 from concourse.mybir import AluOpType as A, ActivationFunctionType as F
 
 NV, SH = 4, (1, 2, 4)
-NP = 2
-W = 256 // NP
-NL = W // 16
-NU = 4
+WS = (128, 128)
+NP = len(WS)
+WM = max(WS)
+AT = [sum(WS[:_h]) for _h in range(NP)]
+ND = 3
+PLACE = {2: {"sh": ("m", 2), "cc": ("m", 2), "oh0": ("h", 1), "e0": ("h", 2), "oh1": ("m", 0), "e1": ("m", 1), "emp": ("h", 1), "oz": ("h", 2), "new": ("m", 0),
+             "lz": ("m", 1), "U": ("h", 0), "u": ("h", 1), "zt": ("h", 3), "c2": ("m", 1), "c1": ("m", 2), "l1": ("m", 1),
+             "a2": ("m", 0), "a1": ("h", 0)},
+         3: {"sh": ("m", -1), "cc": ("m", -1), "oh0": ("h", 1), "e0": ("h", 3), "emp": ("h", 1), "oz": ("h", 2), "new": ("h", 4),
+             "lz": ("h", 1), "U": ("h", 4), "u": ("h", 2), "zt": ("h", 1), "c2": ("h", 0), "c1": ("m", 3), "l1": ("m", -1),
+             "a2": ("h", 4), "a1": ("m", 4)}}[NP]
+NM = {2: 2, 3: 1}[NP]
 BIG = 131072.0
 FAR = 16777216.0
+CB = 129.0
+EX = (-1.0, -1.0, 1.75)
+ROT = 712
 f32, b16, h16, i32, u16 = "float32", "bfloat16", "float16", "int32", "uint16"
 
 SCRATCH = {"X0": ("sbuf", [128, 4112], b16), "X1": ("sbuf", [128, 4112], b16), "rbs": ("sbuf", [128, 1024], i32),
            "inp": ("sbuf", [128, 768], i32), "thi": ("sbuf", [128, 256], i32), "thf": ("sbuf", [128, 256], f32),
            "th16": ("sbuf", [128, 8 * NP], f32), "rs": ("sbuf", [128, 128 * NP], f32), "cnt": ("sbuf", [128, 8 * NP], i32),
            "go": ("sbuf", [128, 8 * NP], b16),
-           "ri": ("sbuf", [128, 8], i32), "col": ("sbuf", [128, 16], f32), "im": ("sbuf", [128, 128], f32),
-           "ix": ("sbuf", [128, 144], f32), "mg": ("sbuf", [128, 128], f32), "mgE": ("sbuf", [128, 128], f32),
+           "ri": ("sbuf", [128, 8], i32), "col": ("sbuf", [128, 24], f32), "im": ("sbuf", [128, 128], f32),
+           "mg": ("sbuf", [128, 128], f32), "mgE": ("sbuf", [128, 128], f32),
            "mgO": ("sbuf", [128, 128], f32), "tx": ("sbuf", [128, 8, 32], f32), "mk": ("sbuf", [128, 128], b16),
-           "cz": ("sbuf", [128, 8], b16), "csl": ("sbuf", [128, 8], i32),
-           "l16i": ("sbuf", [128, 8], i32), "l16": ("sbuf", [128, 8], u16),
-           "rstm": ("sbuf", [128, 128], f32), "rst1": ("sbuf", [128, 1024], b16), "rows": ("sbuf", [128, 1024], b16),
-           "one16": ("sbuf", [128, 128], b16), "I32": ("sbuf", [128, 8], f32), "blkD": ("sbuf", [128, 8], b16),
-           "Wb": ("sbuf", [128, 144], b16), "mb": ("sbuf", [128, 17, 128], b16), "mh": ("sbuf", [128, 19, 128], h16),
-           "pm": ("psum", [128, 512], f32), "pq": ("psum", [128, 512], f32)}
-for _h in range(NP):
-    for _n, _sh, _d in (("tl", [128, NV, 3 * W], h16), ("to", [128, 3 * W], h16), ("tf", [128, 3 * W], f32),
-                        ("rec", [128, 16 * W], b16), ("abd", [128, 16 * W], b16), ("top", [128, 16 * W], b16), ("ex", [128, 3, W], b16),
-                        ("pn", [128, 128], f32), ("bm", [128, 128], f32), ("ou", [128, 2, 128], b16),
-                        ("off", [128, W], u16), ("hl", [128, 2 * W], h16), ("w2", [128, 2 * W], h16), ("wf", [128, 4, W], f32), ("wi", [128, 5, W], i32), ("wh", [128, 3, W], h16),
-                        ("wb", [128, 4, W], b16), ("sk", [128, 8], i32),
-                        ("si", [128, 5, 8], i32), ("sf", [128, 2, 8], f32), ("su", [128, 24], u16)):
+           "cz": ("sbuf", [128, 8], f32),
+           "rstm": ("sbuf", [128, 128], f32), "rsth": ("sbuf", [128, 128], h16), "rst1": ("sbuf", [128, 1024], b16),
+           "rows": ("sbuf", [128, 19, 128], b16),
+           "one16": ("sbuf", [128, 128], b16), "I32": ("sbuf", [128, 8], f32), "blkD": ("sbuf", [128, 24], b16), "rst2": ("sbuf", [128, 1024], b16),
+           "mb": ("sbuf", [128, 18, 128], b16), "mh": ("sbuf", [128, 9, 128], h16),
+           "pq": ("psum", [128, 512], f32)}
+for _h, _w in enumerate(WS):
+    for _n, _sh, _d in (("tl", [128, NV, 6 * _w], h16), ("to", [128, 4 * _w], h16), ("tf", [128, 3 * _w], f32),
+                        ("rec", [128, 16 * _w], b16), ("abd", [128, _w, 16], b16), ("top", [128, 16 * _w], b16), ("mx", [128, 16 * _w], b16),
+                        ("ex", [128, 3, _w], b16), ("oz", [128, 128], b16),
+                        ("pn", [128, 128], f32), ("bm", [128, 128], f32), ("pnh", [128, 128], h16), ("bmh", [128, 128], h16),
+                        ("off", [128, _w], u16), ("wf", [128, 4, _w], f32), ("wi", [128, 4, _w], i32), ("vi", [128, 2 * _w], i32), ("sz", [128, 2 * _w], f32),
+                        ("wh", [128, 4, _w], h16), ("wb", [128, 6, _w], b16),
+                        ("ll", [128, 40], i32), ("su", [128, 24], u16), ("cst", [128, 16], i32)):
         SCRATCH[_n + str(_h)] = ("sbuf", _sh, _d)
     SCRATCH["ph%d" % _h] = ("psum", [128, 512], f32)
-for _b in range(6 - NP):
+for _b in range(NM):
+    SCRATCH["pm%d" % _b] = ("psum", [128, 512], f32)
+for _b in range(ND):
     SCRATCH["pd%d" % _b] = ("psum", [128, 512], f32)
 
-SEMAPHORES = ["pe", "dve", "act", "pool", "lx0", "lx1", "lx2", "lx3", "ll", "la", "lc", "lth", "lrb"] + \
+SEMAPHORES = ["pe", "dve", "act", "pool", "lx0", "lx1", "ll", "la", "lc", "lth", "lrb0", "lrb1"] + \
     ["cx%d" % _t for _t in range(NV)] + ["sx%d" % _h for _h in range(NP)] + ["sy%d%d" % (_h, _j) for _h in range(NP) for _j in range(3)] + \
-    ["%s%d%d" % (_p, _t, _h) for _p in ("ar", "sn") for _t in range(NV - 1) for _h in range(NP)]
+    ["%s%d%d%d" % (_p, _t, _h, _j) for _p in ("ar", "sn") for _t in range(NV - 1) for _h in range(NP) for _j in range(2)]
 
-PAR = {"g": 1.56, "cyc": 0.87, "pe": 0.55, "fix": 25.0, "hop": 160.0, "nd": (2, 2, 2), "ul": 0, "hl": 1, "heat": 500.0, "tries": 38000, "bias": {}, "force": {}, "pen": 600.0, "per": 8500.0, "extra": 4000.0,
-       "dm": 0, "relu": 0, "pu": 8, "rounds": 2}
+PAR = {"g": 1.5, "cyc": 0.87, "pe": 0.52, "fix": 25.0, "hop": 220.0, "heat": 100.0, "tries": 0, "pen": 600.0, "per": 7500.0, "extra": 3000.0,
+       "rounds": 2, "gc": (0, 32, 64, 96, 128), "sp": 1, "pu": 8, "period": 42000.0, "beat": 9500.0, "amp": 300.0, "search": ((6000, 1200.0), (3000, 300.0)),
+       "dma": 1.0, "cases": ({"g": 1.3, "cyc": 0.84, "pe": 0.45, "hop": 200.0, "weight": 0.35}, {"g": 1.4, "pe": 0.7, "hop": 200.0, "weight": 0.3},
+                             {"g": 1.9, "cyc": 1.05, "pe": 0.55, "hop": 280.0, "dma": 1.2, "weight": 0.22}),
+       "force": {}, "two": 1, "mx": 0, "mc": 64, "kn": {128: ((64, 8), (64, 8)), 96: ((96, 4),), 64: ((64, 8),)}}
 CACHE = {}
 
 
 def build(g, core, T, topo):
-    ops, stage = [], [0]
+    ops, stage = [], [-1]
     V, S, P = g.vector, g.scalar, g.tensor
     rank = T.rank_of(core)
     nxt = T.cores[(rank + 1) % len(T.cores)]
     rid, pid = topo.addr(nxt)[:2]
-    eng = topo.engines(core, nxt)[::2]
+    eng = topo.engines(core, nxt)
     mask = sum(1 << e for e in eng)
 
     def bank(names):
@@ -75,28 +92,24 @@ def build(g, core, T, topo):
     def scan(out, d0, d1, init, o0, o1, R, Wr, n):
         op("dve", [lambda: V.tensor_tensor_scan(out, d0, d1, init, o0, o1)], R, Wr, n)
 
-    def either(out, a, R, Wr, n):
-        i = op("any", None, R, Wr, n)
-        ops[i]["alt"] = {"dve": [lambda: V.tensor_copy(out, a)], "act": [lambda: S.activation(out, a, F.Copy)]}
+    def either(dve, act, R, Wr, n):
+        ops[op("any", None, R, Wr, n)]["alt"] = {"dve": [dve], "act": [act]}
 
-    def affine(out, a, f, scale, bias, R, Wr, n):
-        i = op("any", None, R, Wr, n)
-        if f == "relu":
-            ops[i]["alt"] = {"dve": [lambda: V.tensor_scalar(out, a, 0.0, scale, A.max, A.mult)],
-                             "act": [lambda: S.activation(out, a, F.Relu, bias=0.0, scale=scale)]}
-        else:
-            ops[i]["alt"] = {"dve": [lambda: V.tensor_scalar(out, a, scale, bias, A.mult, A.add)],
-                             "act": [lambda: S.activation(out, a, F.Identity, bias=bias, scale=scale)]}
+    def pickup(out, a, R, Wr, n):
+        either(lambda: V.tensor_copy(out, a), lambda: S.activation(out, a, F.Copy), R, Wr, ("g", n))
+
+    def affine(out, a, scale, bias, R, Wr, n):
+        either(lambda: V.tensor_scalar(out, a, scale, bias, A.mult, A.add), lambda: S.activation(out, a, F.Identity, bias=bias, scale=scale), R, Wr, n)
 
     def ms(out, c, Wr, n):
         op("dve", [lambda: V.memset(out, c)], [], Wr, n)
 
-    def mm(terms, R, Wr, first=True, last=True, pairs=False):
+    def mm(terms, R, Wr, first=True, last=True, each=False):
         calls = []
         for j, (o, l, r, n) in enumerate(terms):
-            st, sp = (j % 2 == 0, j % 2 == 1) if pairs else (first and j == 0, last and j == len(terms) - 1)
+            st, sp = (j % each == 0, j % each == each - 1) if each else (first and j == 0, last and j == len(terms) - 1)
             calls.append(lambda o=o, l=l, r=r, st=st, sp=sp: P.matmul(o, l, r, st, sp))
-        op("pe", calls, R, Wr, sum(max(64, x[3]) for x in terms))
+        op("pe", calls, R, Wr, sum(x[3] for x in terms))
 
     def iota(out, pat, base, cm, Wr, n, flt=True):
         if flt:
@@ -111,12 +124,12 @@ def build(g, core, T, topo):
     inp = T["inp"]
     dma("sp", inp[:, 0:256], T["lt"][:], [], ["inL"], "ll", 2000)
     dma("act", inp[:, 256:512], T["ag"][:], [], ["inA"], "la", 2000)
-    for j in range(4):
-        dma("sp" if j % 2 == 0 else "act", T["X0"][:, 1024 * j:1024 * j + 1024], T["xs"][:, 1024 * j:1024 * j + 1024], [], ["Xl%d" % j],
-            "lx%d" % j, 3000 + 500 * j)
-    dma("sp", inp[:, 512:768], T["cs"][:], [], ["inC"], "lc", 4500)
-    dma("sp", T["thi"][0:8, :], T["th"][:], [], ["thi"], "lth", 4500)
-    dma("sp", T["rbs"][:], T["rb"][:], [], ["rbs"], "lrb", 6000)
+    for j in range(2):
+        dma(("sp", "act")[j], T["X0"][:, 2048 * j:2048 * j + 2048], T["xs"][:, 2048 * j:2048 * j + 2048], [], ["Xl%d" % j], "lx%d" % j, 5000)
+    dma("sp", inp[:, 512:768], T["cs"][:], [], ["inC"], "lc", 5500)
+    dma("sp", T["thi"][0:8, :], T["th"][:], [], ["thi"], "lth", 5500)
+    dma("sp", T["rbs"][:, ROT:1024], T["rb"][:, 0:1024 - ROT], [], ["rbs0"], "lrb0", 7000)
+    dma("sp", T["rbs"][:, 0:ROT], T["rb"][:, 1024 - ROT:1024], [], ["rbs1"], "lrb1", 7000)
     for b in range(2):
         ms(T["X%d" % b][:, 4096:4112], 0.0, ["Xz%d" % b], 16)
 
@@ -125,370 +138,379 @@ def build(g, core, T, topo):
     iota(ri[:, 0:1], [[0, 1]], 0, 1, ["ri0"], 1, False)
     iota(T["mg"][:], [[1, 8], [0, 16]], 0, 0, ["mg"], 128)
     iota(T["tx"][:], [[16, 8], [0, 2], [1, 16]], 0, -1, ["tx"], 256)
-    iota(T["l16i"][:], [[1, 8]], 0, 0, ["l16i"], 8, False)
-    iota(T["mk"][:], [[0, 8], [1, 16]], 0, 0, ["mk"], 128)
+    iota(T["mk"][:], [[0, 8], [1, 16]], 1, 0, ["mk"], 128)
     iota(T["cz"][:], [[256, 8]], 0, 0, ["cz"], 8)
     iota(T["mgE"][:], [[1, 8], [0, 8], [100, 2]], 0, 0, ["mgE"], 128)
     iota(T["mgO"][:], [[1, 8], [0, 8], [-100, 2]], 100, 0, ["mgO"], 128)
-    iota(T["ix"][:], [[1, 144]], -15, 0, ["ix"], 144)
     ts(ri[:, 1:2], ri[:, 0:1], 15, None, A.bitwise_and, None, ["ri0"], ["ri1"], 1)
     ts(ri[:, 2:3], ri[:, 0:1], 4, None, A.arith_shift_right, None, ["ri0"], ["ri2"], 1)
-    for e in range(3):
-        ts(ri[:, 3 + e:4 + e], ri[:, 0:1], e, 1, A.arith_shift_right, A.bitwise_and, ["ri0"], ["ri%d" % (3 + e)], 1)
+    ts(ri[:, 3:4], ri[:, 0:1], 1, None, A.bitwise_and, None, ["ri0"], ["ri3"], 1)
     C, M, RW = {}, {}, {}
 
-    def column(name, j, src, m, a):
-        C[name] = col[:, j:j + 1]
+    def column(name, src, m, a):
+        C[name] = col[:, len(C):len(C) + 1]
         ts(C[name], ri[:, src:src + 1], m, a, A.mult, A.add, ["ri%d" % src], [name], 1)
-    column("rk", 0, 1, 1.0, 0.0)
-    column("rg", 1, 2, 1.0, 0.0)
-    column("rg16", 2, 2, 16.0, 0.0)
-    column("rk16", 3, 1, 16.0, 0.0)
-    column("kB", 4, 1, 1.0 / BIG, 0.0)
-    column("wq", 5, 1, 2.0, 1.0)
-    for e in range(3):
-        column("sg%d" % e, 7 + e, 3 + e, -2.0, 1.0)
-        column("bt%d" % e, 13 + e, 3 + e, -2.0, 0.0)
-    for t in range(1, NV):
-        column("ev%d" % t, 9 + t, 3, -32.0 * t, 32.0 * t)
+    column("rg", 2, 1.0, 0.0)
+    column("rk16", 1, 16.0, 0.0)
+    column("rk1", 1, 1.0, 1.0)
+    column("wq", 1, 2.0, 1.0)
+    column("wq2", 1, 4096.0, 2048.0)
+    column("gp", 0, 1048576.0, -1048576.0)
+    column("cp", 0, 1.0, 0.0)
+    column("np", 0, -6144.0, 6144.0)
+    for si in range(3):
+        column("up%d" % si, 0, -2 * BIG * si, 2 * BIG * si)
+    column("ev", 3, -1.0, 1.0)
+    used = {"mb": 0, "mh": 0}
 
-    def matrix(name, buf, j, src, srcn, s1, s2, extra=()):
-        M[name] = T[buf][:, j, :]
+    def matrix(name, buf, src, srcn, s1, s2, extra=()):
+        M[name] = T[buf][:, used[buf], :]
+        used[buf] += 1
         ts(M[name], src, s1, s2, A.is_equal, A.mult, [srcn] + list(extra), [name], 128)
     im, mg, tx = T["im"][:], T["mg"][:], T["tx"]
-    for name, buf, j, c in (("Ih", "mh", 0, 1.0), ("I2080", "mh", 1, 2080.0), ("I", "mb", 0, 1.0), ("nI", "mb", 1, -1.0), ("BI", "mb", 2, BIG),
-                            ("nBI", "mb", 3, -BIG), ("I2", "mb", 4, 2.0), ("I2h", "mh", 2, 2.0), ("n16h", "mh", 3, -16.0)):
-        matrix(name, buf, j, im, "im", 0.0, c)
-    matrix("nblk", "mh", 4, mg, "mg", C["rg"], -1.0, ["rg"])
-    matrix("blk", "mh", 5, mg, "mg", C["rg"], 1.0, ["rg"])
-    matrix("odd", "mh", 6, T["mgO"][:], "mgO", C["rg"], 1.0, ["rg"])
-    matrix("WqO", "mb", 5, T["mgE"][:], "mgE", C["rg"], C["wq"], ["rg", "wq"])
-    matrix("Wq", "mb", 16, mg, "mg", C["rg"], C["wq"], ["rg", "wq"])
-    matrix("mP", "mb", 6, T["mk"][:], "mk", C["rk"], 1.0 / 16, ["rk"])
+    for name, buf, c in (("Ih", "mh", 1.0), ("I2080", "mh", 2080.0), ("I", "mb", 1.0), ("n16h", "mh", -16.0)):
+        matrix(name, buf, im, "im", 0.0, c)
+    for name, c in (("nI", -1.0), ("BI", BIG), ("nBI", -BIG), ("I8k", 8192.0), ("nI2", -2.0)):
+        M[name] = T["mb"][:, used["mb"], :]
+        used["mb"] += 1
+        affine(M[name], M["I"], c, 0.0, ["I"], [name], 128)
+    matrix("nI12", "mb", im, "im", -1.0, 4096.0)
+    matrix("nI23", "mb", im, "im", 0.0, 4096.0)
+    tt(M["nI12"], M["nI12"], M["nI23"], A.subtract, ["nI12", "nI23"], ["nI12"], 128)
+    ms(T["mb"][:, used["mb"] - 2, 1::2], 0.0, ["nI12"], 64)
+    affine(M["nI23"], M["nI12"], 2048.0, 0.0, ["nI12"], ["nI23"], 128)
     for si in range(3):
         s = SH[si]
-        matrix("Sh%d" % si, "mh", 7 + si, tx[:, :, s:s + 16], "tx", 0.0, 1.0)
-        M["SI%d" % si] = T["mh"][:, 10 + si, :]
-        tt(M["SI%d" % si], M["Sh%d" % si], M["Ih"], A.subtract, ["Sh%d" % si, "Ih"], ["SI%d" % si], 128)
-        matrix("J%d" % si, "mb", 7 + si, tx[:, :, 16 - s:32 - s], "tx", 0.0, BIG)
-        if PAR["hl"]:
-            continue
-        matrix("sig%d" % si, "mh", 13 + si, mg, "mg", C["rg"], C["sg%d" % si], ["rg", "sg%d" % si])
-        matrix("bit%d" % si, "mh", 16 + si, mg, "mg", C["rg"], C["bt%d" % si], ["rg", "bt%d" % si])
-        matrix("IJ%d" % si, "mb", 10 + si, tx[:, :, 16 - s:32 - s], "tx", 0.0, 1.0)
-        tt(M["IJ%d" % si], M["IJ%d" % si], M["I"], A.add, ["IJ%d" % si, "I"], ["IJ%d" % si], 128)
-    for j, (e, si) in enumerate(((0, 1), (0, 2), (1, 2))):
+        matrix("Sh%d" % si, "mh", tx[:, :, s:s + 16], "tx", 0.0, 1.0)
+        matrix("J%d" % si, "mb", tx[:, :, 16 - s:32 - s], "tx", 0.0, 8192.0)
+    for e, si in ((0, 1), (0, 2), (1, 2)):
         nm, d = "pen%d%d" % (e, si), SH[si] - SH[e]
-        matrix(nm, "mb", 13 + j, tx[:, :, d:d + 16], "tx", 0.0, BIG)
+        matrix(nm, "mb", tx[:, :, d:d + 16], "tx", 0.0, 8192.0)
         tt(M[nm], M[nm], M["J%d" % e], A.add, [nm, "J%d" % e], [nm], 128)
-    ts(T["blkD"][:], T["mg"][:, ::16], C["rg"], 16.0, A.is_equal, A.mult, ["mg", "rg"], ["blkD"], 8)
+        ts(M[nm], M[nm], BIG / 8192, None, A.mult, None, [nm], [nm], 64)
+    matrix("blk", "mh", mg, "mg", C["rg"], 1.0, ["rg"])
+    matrix("odd", "mh", T["mgO"][:], "mgO", C["rg"], 1.0, ["rg"])
+    matrix("WqE", "mb", T["mgE"][:], "mgE", C["rg"], C["wq"], ["rg", "wq"])
+    matrix("WqE2", "mb", T["mgE"][:], "mgE", C["rg"], C["wq2"], ["rg", "wq2"])
+    for j, c in enumerate((16.0, -16.0, 32.0)):
+        ts(T["blkD"][:, 8 * j:8 * j + 8], T["mg"][:, ::16], C["rg"], c, A.is_equal, A.mult, ["mg", "rg"], ["blkD"], 8)
+    ms(T["rst2"][:], 1.0, ["rst2"], 512)
+    ms(T["rst2"][:, ::2], 0.0, ["rst2"], 256)
     ts(T["I32"][:], T["im"][:, 0:8], 0.0, 16.0, A.is_equal, A.mult, ["im"], ["I32"], 8)
-    ts(T["Wb"][:], T["ix"][:], C["rg16"], C["wq"], A.is_equal, A.mult, ["ix", "rg16", "wq"], ["Wb"], 144)
-    ts(T["csl"][:], T["cz"][:], C["rk16"], None, A.add, None, ["cz", "rk16"], ["csl"], 8)
-    cp(T["l16"][:], T["l16i"][:], ["l16i"], ["l16"], 8)
+    matrix("Wq", "mb", mg, "mg", C["rg"], C["wq"], ["rg", "wq"])
+    M["else"] = T["mb"][:, used["mb"], :]
+    ts(M["else"], T["mk"][:], C["rk1"], BIG, A.not_equal, A.mult, ["mk", "rk1"], ["else"], 64)
     ms(T["rstm"][:], -FAR, ["rstm"], 128)
     ms(T["rstm"][:, ::16], FAR, ["rstm"], 8)
+    ms(T["rsth"][:], -30000.0, ["rsth"], 64)
+    ms(T["rsth"][:, ::16], 30000.0, ["rsth"], 8)
     ms(T["rst1"][:], 1.0, ["rst1"], 512)
     ms(T["rst1"][:, ::16], 0.0, ["rst1"], 64)
     ms(T["one16"][:], 16.0, ["one16"], 64)
     rows = T["rows"]
-    for j, (name, val) in enumerate((("r1", 1.0), ("r3232", 3232.0), ("rBIG", BIG), ("r8192", 8192.0), ("r10240", 10240.0), ("r4096", 4096.0), ("rodd", 0.0))):
-        RW[name] = rows[0:1, 128 * j:128 * j + 128]
-        ms(RW[name], val, [name], 64)
-    ms(rows[0:1, 128 * 6 + 1:128 * 7:2], 2048.0, ["rodd"], 64)
-    RW["rgo"] = rows[0:1, 896:1024]
-    ts(RW["rgo"], T["mg"][0:1, :], -1048576.0, None, A.mult, None, ["mg"], ["rgo"], 128)
-    one = rows[0:1, 0:W]
+    ms(rows[0:2, 0, :], 1.0, ["r1"], 64)
+    for name, val in (("r3232", 3232.0), ("rBIG", BIG), ("r8192", 8192.0), ("r10240", 10240.0), ("rnCB", -CB),
+                      ("rodd", 0.0)) + tuple(("rev%d" % t, 0.0) for t in range(1, NV)):
+        j = len(RW) + 1
+        RW[name] = rows[0:1, j, :]
+        affine(RW[name], rows[0:1, 0, :], val, 0.0, ["r1"], [name], 128)
+        if name == "rodd":
+            ms(rows[0:1, j, 1::2], 2048.0, [name], 64)
+        if name[:3] == "rev":
+            ms(rows[0:1, j, 0::2], 32.0 * int(name[3]), [name], 64)
+    RW["rgo"] = rows[0:2, 14, :]
+    ts(RW["rgo"], T["mg"][0:2, :], col[0:2, 5:6], None, A.mult, None, ["mg", "gp"], ["rgo"], 128)
+    ts(rows[0:2, 13, :], T["mk"][0:2, :], -1.0, col[0:2, 6:7], A.add, A.mult, ["mk", "cp"], ["rtmp"], 128)
+    tt(RW["rgo"], RW["rgo"], rows[0:2, 13, :], A.add, ["rgo", "rtmp"], ["rgo"], 128)
+    for si in range(3):
+        RW["rgo%d" % si] = rows[0:2, 16 + si, :]
+        ts(RW["rgo%d" % si], RW["rgo"], col[0:2, 8 + si:9 + si], None, A.add, None, ["rgo", "up%d" % si], ["rgo%d" % si], 64)
+    RW["rk"] = rows[0:2, 15, :]
+    ts(RW["rk"], T["mk"][0:2, :], col[0:2, 6:7], col[0:2, 7:8], A.mult, A.add, ["mk", "cp", "np"], ["rk"], 128)
 
-    def const(out, name):
-        return (out, RW[name], one, W)
+    def place_(h, name, n=1, lo=0, hi=None):
+        W = WS[h]
+        b, j = PLACE[name]
+        j = h if j < 0 else j
+        bn, c = ("ph%d" % h, 128 + W * (j - 1) if j else 0) if b == "h" else ("pm%d" % (h % NM), WM * j)
+        lo, hi = c + lo, c + (n * W if hi is None else hi)
+        return T[bn][:, lo:hi], ["%s_%d" % (bn, x) for x in range(lo // 64, (hi + 63) // 64)]
 
-    pm, pq, rs = T["pm"], T["pq"], T["rs"]
+    def halves(W):
+        return ((0, W // 2), (W // 2, W)) if PAR["sp"] else ((0, W),)
+
+    def both(name):
+        return [name + str(j) for j in range(2 if PAR["sp"] else 1)]
+
+    def const(out, name, W):
+        return (out, RW[name], rows[0:1, 0, 0:W], max(W, 64))
+
+    pq, rs = T["pq"], T["rs"]
     cp(T["thf"][0:8, :], T["thi"][0:8, :], ["thi"], ["thf"], 256)
+    ms(T["th16"][:], 0.0, ["th16"], 8 * NP)
+    ms(T["go"][:], 0.0, ["go%d" % h for h in range(NP)], 8 * NP)
     for h in range(NP):
-        o = pm[0:W, 304 + 8 * h:312 + 8 * h]
-        mm([(o, T["thf"][0:8, W * h:W * h + W], T["I32"][0:8, :], 256), (o, one, rows[0:1, 896:1024:16], 8)], ["thf", "I32", "r1", "rgo"], ["pm_t%d" % h])
-        ms(T["sk%d" % h][:], 0, ["sk%d" % h], 8)
-        tl = T["tl%d" % h]
-        ts(tl[:, 0, 0:W], inp[:, W * h:W * h + W], -2048.0, None, A.add, None, ["inL"], ["L0%d" % h], W)
-        ts(tl[:, 0, W:2 * W], inp[:, 256 + W * h:256 + W * h + W], -2048.0, None, A.add, None, ["inA"], ["a0%d" % h], W)
-        cp(tl[:, 0, 2 * W:3 * W], inp[:, 512 + W * h:512 + W * h + W], ["inC"], ["C0%d" % h], W)
-    ts(T["th16"][0:W, :], pm[0:W, 304:304 + 8 * NP], -0.5, None, A.add, None, ["pm_t%d" % h for h in range(NP)], ["th16"], 8 * NP)
+        H, W, x = str(h), WS[h], AT[h]
+        o = T["ph" + H][0:W, 0:8]
+        mm([(o, T["thf"][0:8, x:x + W], T["I32"][0:8, :], 256), (o, rows[0:1, 0, 0:W], rows[0:1, 14, ::16], 64)], ["thf", "I32", "r1", "rgo"],
+           ["ph%s_0" % H])
+        ts(T["th16"][0:W, 8 * h:8 * h + 8], o, -0.5, None, A.add, None, ["ph%s_0" % H], ["th16"], 8)
+        tl = T["tl" + H]
+        ms(tl[:, 0, 2 * W:4 * W:2], 0.0, ["zero" + H], W)
+        ms(T["to" + H][:, 2 * W:4 * W:2], 0.0, ["zto" + H], W)
+        ms(T["sz" + H][:, 0::2], 0.0, ["zsz" + H], W)
+        ts(tl[:, 0, 0:W], inp[:, x:x + W], -2048.0, None, A.add, None, ["inL"], ["L0" + H], W)
+        ts(tl[:, 0, 2 * W + 1:4 * W:2], inp[:, 256 + x:256 + x + W], -2048.0, None, A.add, None, ["inA"], both("a0" + H), W)
+        ts(tl[:, 0, W:2 * W], inp[:, 512 + x:512 + x + W], CB, None, A.add, None, ["inC"], ["C0" + H], W)
+        ts(T["cst" + H][:, 0:W // 16], T["cz"][:, 0:W // 16], C["rk16"], None, A.add, None, ["cz", "rk16"], ["cst" + H], 8)
+        ms(T["cst" + H][:, W // 16:W // 8], 592, ["cst" + H], 8)
     ms(rs[:], FAR, ["thr"], 128 * NP)
-    cp(rs[0:W, ::16], T["th16"][0:W, :], ["th16"], ["thr"], 8 * NP)
+    cp(rs[0:WM, ::16], T["th16"][0:WM, :], ["th16"], ["thr"], 8 * NP)
     ms(T["cnt"][:], 0, ["cnt"], 16)
 
-    def slot(h, name):
-        if NP == 2:
-            b, j = {"key": ("ph%d" % h, 0), "x1": ("ph%d" % h, 1), "x2": ("ph%d" % h, 2), "x3": ("ph%d" % h, 3),
-                    "uo": ("pd%d" % (2 * h), 0), "a2": ("pd%d" % (2 * h), 1), "c2": ("pd%d" % (2 * h), 2), "zt": ("pd%d" % (2 * h), 3),
-                    "l1": ("pd%d" % (2 * h + 1), 0), "a1": ("pd%d" % (2 * h + 1), 1), "c1": ("pd%d" % (2 * h + 1), 2),
-                    "sm": ("pd%d" % (2 * h + 1), 3)}[name]
-        else:
-            b, j = "ph%d" % h, {"key": 0, "x1": 2, "x2": 3, "x3": 4, "uo": 0, "zt": 1, "a2": 2, "c2": 3, "l1": 4, "a1": 5, "c1": 6, "sm": 7}[name]
-            if name == "key":
-                return T[b][0:W, 0:128], [b + "_0", b + "_1"]
-        if name == "sm":
-            return (T[b][:, W * j:W * j + NL], T[b][:, W * j + 8:W * j + 8 + NL]), ["%s_%d" % (b, j)]
-        return T[b][:, W * j:W * j + W], ["%s_%d" % (b, j)]
-
     def state(t, h):
-        tl = T["tl%d" % h]
-        return tl[:, t, 0:W], tl[:, t, W:2 * W], tl[:, t, 2 * W:3 * W], "L%d%d" % (t, h), "a%d%d" % (t, h), "C%d%d" % (t, h)
+        tl, W = T["tl%d" % h], WS[h]
+        return tl[:, t, 0:W], tl[:, t, 2 * W + 1:4 * W:2], tl[:, t, W:2 * W], "L%d%d" % (t, h), both("a%d%d" % (t, h)), "C%d%d" % (t, h)
+
+    def half(t, h, lo, hi):
+        return T["tl%d" % h][:, t, 2 * WS[h] + 1 + 2 * lo:2 * WS[h] + 2 * hi:2]
 
     def index(t, h, final):
-        H = str(h)
+        H, W = str(h), WS[h]
         L, a, Cc, ln, an, cn = state(t, h)
-        v1, v = T["wf" + H][:, 0, :], T["wi" + H][:, 0, :]
-        tt(v1, pq[:, 2 * W * h:2 * W * h + W], a, A.mult, ["pq_L" + H, an], ["v1" + H], W)
-        tt(v, pq[:, 2 * W * h + W:2 * W * h + 2 * W], v1, A.add, ["pq_Q" + H, "v1" + H], ["v" + H], W)
-        ts(v, v, 5, 4095, A.arith_shift_right, A.bitwise_and, ["v" + H], ["v" + H], W)
+        for j, (lo, hi) in enumerate(halves(W)):
+            v, J = T["wi" + H][:, 0, lo:hi], H + str(j)
+            scan(T["vi" + H][:, 2 * lo:2 * hi], T["tl" + H][:, t, 2 * W + 2 * lo:2 * W + 2 * hi], pq[:, 2 * (AT[h] + lo):2 * (AT[h] + hi)], 0.0, A.mult, A.add,
+                 ["pq_L" + H, an[j], "zero" + H], ["vi" + J], 2 * (hi - lo))
+            ts(v, T["vi" + H][:, 2 * lo + 1:2 * hi:2], 5, 4095, A.arith_shift_right, A.bitwise_and, ["vi" + J], ["v" + J], hi - lo)
+            if not final:
+                cp(T["off" + H][:, lo:hi], v, ["v" + J], ["off" + J], hi - lo)
         if final:
-            x1, k1 = slot(h, "x1")
-            tt(v, x1, v, A.max, k1 + ["v" + H], ["v" + H], W)
-            ts(T["off" + H][:], v, 4096.0, None, A.min, None, ["v" + H], ["off" + H], W)
-        else:
-            cp(T["off" + H][:], v, ["v" + H], ["off" + H], W)
+            (x1, k1), v, ix = place_(h, "emp"), T["wi" + H][:, 0, :], T["tl" + H][:, t, 4 * W + 1:6 * W:2]
+            tt(ix, x1, v, A.add, k1 + both("v" + H), ["ix" + H], W)
+            ts(T["off" + H][:], ix, 2048.0, 4096.0, A.add, A.min, ["ix" + H], both("off" + H), W // 2)
 
     def xnames(t):
-        return ["Xz%d" % (t % 2)] + (["Xl%d" % j for j in range(4)] if t == 0 else []) + ["X%d%d" % (t % 2, h) for h in range(NP)]
+        return ["Xz%d" % (t % 2)] + (["Xl0", "Xl1"] if t == 0 else []) + ["X%d%d" % (t % 2, h) for h in range(NP)]
 
-    def gather(t, h):
-        H, n = str(h), W // NU
-        for c in range(NU):
-            src = T["X%d" % (t % 2)][:, 0:4112].indirect(T["off" + H][:, n * c:n * c + n])
-            either(T["rec" + H][:, 16 * n * c:16 * n * (c + 1)], src, xnames(t) + ["off" + H], ["rec%s%d" % (H, c)], ("g", 16 * n))
+    def recs(h, lo, hi):
+        return ["rec%d%d" % (h, c) for c in range(lo // 16, hi // 16)]
 
-    def pick(h, rst, rn):
+    def gather(t, h, lo, hi):
         H = str(h)
-        (key, k0), pmin, bm = slot(h, "key"), T["pn" + H], T["bm" + H]
-        scan(pmin[0:W, :], rst, key, FAR, A.max if rn == "rstm" else A.min, A.min, [rn] + k0, ["least" + H], 128)
-        scan(bm[0:W, ::-1], T["rstm"][0:W, :], pmin[0:W, ::-1], 0.0, A.max, A.min, ["rstm", "least" + H], ["bm" + H], 128)
-        tt(T["ou" + H][0:W, 0, :], key, bm[0:W, :], A.is_equal, k0 + ["bm" + H], ["ohU" + H], 128)
+        cuts = [c for c in PAR["gc"] if lo <= c <= hi]
+        for c, e in zip(cuts, cuts[1:]):
+            pickup(T["rec" + H][:, 16 * c:16 * e], T["X%d" % (t % 2)][:, 0:4112].indirect(T["off" + H][:, c:e]),
+                   xnames(t) + ["off%s%d" % (H, j) for j, (x, y) in enumerate(halves(WS[h])) if x < e and c < y], recs(h, c, e), 16 * (e - c))
+
+    turn = [0]
 
     def step(t, h, si):
-        H, s = str(h), SH[si]
+        H, s, W = str(h), SH[si], WS[h]
         L, a, Cc, ln, an, cn = state(t, h)
-        (key, k0), (x1, k1), (x2, k2), (x3, k3) = [slot(h, x) for x in ("key", "x1", "x2", "x3")]
+        bank_ = T["ph" + H]
+        key, k0, kall = bank_[0:W, 0:128], ["ph%s_0" % H, "ph%s_1" % H], ["ph%s_%d" % (H, j) for j in range(8)]
+        (x1, k1), (m0, n0) = place_(h, "cc"), place_(h, "sh")
         index(t, h, False)
-        eqk, w, m = T["wb" + H][:, 0, :], T["wh" + H][:, 0, :], T["wb" + H][:, 1, :]
-        if PAR["hl"]:
-            hl, w2 = T["hl" + H], T["w2" + H]
-            mm([(x3, M["Sh%d" % si], a, W)], ["Sh%d" % si, an], k3)
-            tt(hl[:, 0:W], x3, a, A.max, k3 + [an], ["hi" + H], W)
-            tt(hl[:, W:2 * W], x3, a, A.min, k3 + [an], ["lo" + H], W)
-        mm([(x1, M["SI%d" % si], a, W)], ["SI%d" % si, an] + k3, k1)
-        ts(eqk, x1, 0.0, C["kB"], A.is_equal, A.add, k1 + ["kB"], ["eqk" + H], W)
-        terms, R = [(key, eqk, M["BI"], 128), (key, one, RW["rgo"], 128)], ["eqk" + H, "BI", "r1", "rgo"]
+        eqk, wh = T["wb" + H][:, 0, :], T["wh" + H]
+        mm([(m0, M["Sh%d" % si], a, W)], ["Sh%d" % si] + an, n0)
+        tt(eqk, m0, a, A.is_equal, n0 + an, ["eqk" + H], W)
+        tt(wh[:, 0, :], m0, a, A.max, n0 + an, ["hi" + H], W)
+        tt(wh[:, 1, :], m0, a, A.min, n0 + an, ["lo" + H], W)
+        terms, R = [(key, rows[0:2, 0, 0:W], RW["rgo%d" % si], 128)], ["eqk" + H, "BI", "r1", "rgo%d" % si]
         for e in range(si):
             terms.append((key, T["ex" + H][:, e, :], M["pen%d%d" % (e, si)], 128))
-            R += ["ex%d%d" % (e, h), "pen%d%d" % (e, si)]
-        mm(terms, R, k0, last=False)
-        rec, abd, nq = T["rec" + H], T["abd" + H], W // 64
-        gather(t, h)
-        recn = ["rec%s%d" % (H, c) for c in range(NU)]
-        own = not (t == 0 or si or h)
-        for kh in range(2 if NP == 4 else 0):
-            pd, pn = T["pd%d" % kh], ["pd%d_%d" % (kh, j) for j in range(4)]
-            terms = [(pd[:, k::8], M[sign], rec[:, (8 * kh + k + d) & 15::16], 64) for k in range(8) for sign, d in (("I", 0), ("nI", s))]
-            for x in range(0, 16, PAR["pu"]):
-                mm(terms[x:x + PAR["pu"]], ["I", "nI"] + recn, pn, pairs=True)
-            o = abd[:, 512 * kh:512 * kh + 512]
-            op("act", [lambda o=o, pd=pd: S.activation(o, pd[:], F.Abs)], pn, ["abd%s%d" % (H, kh)], 512)
-            mm([(T["ph" + H][0:W, 8 * kh + k:128:16], abd[:, 512 * kh + k:512 * kh + 512:8], T["blkD"][:], 64) for k in range(8)],
-               ["blkD", "abd%s%d" % (H, kh)], k0, first=False, last=kh == 1)
-        for q in range(2 if NP == 2 else 0):
-            b = 2 * h + q
-            pd, pn = T["pd%d" % b], ["pd%d_%d" % (b, j) for j in range(4)]
-            terms = [(pd[:, k::8], M[sign], rec[:, 1024 * q + ((k + d) & 15):1024 * q + 1024:16], 64) for k in range(8) for sign, d in (("I", 0), ("nI", s))]
-            for x in range(0, 16, PAR["pu"]):
-                mm(terms[x:x + PAR["pu"]], ["I", "nI"] + recn[q * NU // 2:(q + 1) * NU // 2], pn, pairs=True)
-            o = abd[:, 512 * q:512 * q + 512]
-            op("act", [lambda o=o, pd=pd: S.activation(o, pd[:], F.Abs)], pn, ["abd%s0%d" % (H, q)], 512)
-        if NP == 2:
-            mm([(T["ph" + H][:, k:128:16], abd[:, k:1024:8], T["blkD"][:], 64) for k in range(8)], ["blkD", "abd%s00" % H, "abd%s01" % H], k0,
-               first=False, last=False)
-        nd = PAR["nd"][si]
-        for q in range(2 if NP == 2 else 0):
-            b = 2 * (h if own else 1 - h) + q
-            pd, pn = T["pd%d" % b], ["pd%d_%d" % (b, j) for j in range(4)]
-            ks = list(range(8 + 4 * q, 12 + 4 * q))
-            pk = [k for k in ks if k < 16 - nd]
-            an_ = []
-            if pk:
-                terms = [(pd[:, 128 * (k % 4):128 * (k % 4) + 128], M[sign], rec[:, (k + d) & 15::16], 128) for k in pk for sign, d in (("I", 0), ("nI", s))]
-                for x in range(0, len(terms), PAR["pu"] // 2):
-                    mm(terms[x:x + PAR["pu"] // 2], ["I", "nI"] + recn, pn, pairs=True)
-                o, i_ = abd[:, 128 * pk[0]:128 * pk[-1] + 128], pd[:, 0:128 * len(pk)]
-                op("act", [lambda o=o, i_=i_: S.activation(o, i_, F.Abs)], pn, ["abd%s1%d" % (H, q)], 128 * len(pk))
-                an_.append("abd%s1%d" % (H, q))
-            dk = [k for k in ks if k not in pk]
-            if dk:
-                for k in dk:
-                    tt(abd[:, 128 * k:128 * k + 128], rec[:, k::16], rec[:, (k + s) & 15::16], A.subtract, recn, ["df%s%d" % (H, k)], 128)
-                o = abd[:, 128 * dk[0]:128 * dk[-1] + 128]
-                dn = ["df%s%d" % (H, k) for k in dk]
-                op("act", [lambda o=o: S.activation(o, o, F.Abs)], dn, dn, 128 * len(dk))
-                an_ += dn
-            mm([(T["ph" + H][:, k:128:16], abd[:, 128 * k:128 * k + 128], T["blkD"][:], 64) for k in ks], ["blkD"] + an_, k0, first=False, last=q == 1)
-        pick(h, rs[0:W, 128 * h:128 * h + 128], "thr")
-        en, oh = "ex%d%d" % (si, h), T["ex" + H][:, si, :]
+            R += both("ex%d%d" % (e, h)) + ["pen%d%d" % (e, si)]
+        mm(terms + [(key, eqk, M["BI"], 128)], R, kall, last=False)
+        rec, abd = T["rec" + H], T["abd" + H]
+        lo = 0
+        if s == 1 and PAR["mx"]:
+            gather(t, h, 0, W)
+            mx, ks = (T["top" + H], T["mx" + H]), range(0, 15, 3 - PAR["mx"])
+            names = [["%s%s%d" % (x, H, c) for c in range(0, W, PAR["mc"])] for x in ("top", "mx")]
+            for j, c in enumerate(range(0, W, PAR["mc"])):
+                for d in range(PAR["mx"]):
+                    x, y = 16 * c + d, 16 * (c + PAR["mc"])
+                    scan(mx[d][:, x:y], T["rst2"][:, 0:y - x], rec[:, x:y], 0.0, A.mult, A.max, ["rst2"] + recs(h, c, c + PAR["mc"]), [names[d][j]], (y - x) // 2)
+            rest = [k for k in range(16) if k not in ks]
+            for j in range(0, len(rest), 4):
+                b, some = turn[0] % ND, rest[j:j + 4]
+                turn[0] += 1
+                pd, m = T["pd%d" % b], len(some)
+                mm([(pd[:, i:W * m:m], M[sign], rec[:, (k + d) & 15::16], W) for i, k in enumerate(some) for sign, d in (("I", 0), ("nI", s))],
+                   ["I", "nI"] + recs(h, 0, W), ["pd%d_0" % b], each=2)
+                o, i_ = abd[:, :, some[0]:some[-1] + 1:2], pd[:, 0:W * m]
+                an_ = ["abd%s%d_%d" % (H, x, k) for k in some for x in range(2)]
+                op("act", [lambda o=o, i_=i_: S.activation(o, i_, F.Abs)], ["pd%d_0" % b], an_, W * m)
+                mm([(bank_[0:W, k:128:16], abd[:, :, k], T["blkD"][:, 0:8], 64) for k in some], ["blkD"] + an_, kall, first=False, last=False)
+            for j in range(0, len(ks), 4):
+                mm([(bank_[0:W, k:128:16], rec[:, k + d::16], T["blkD"][:, 8:16], 64) for k in ks[j:j + 4] for d in (0, 1)], ["blkD"] + recs(h, 0, W), kall,
+                   first=False, last=False)
+            for d in range(PAR["mx"]):
+                mm([(bank_[0:W, k:128:16], mx[d][:, k + 1::16], T["blkD"][:, 16:24], 64) for k in ks if k % 2 == d], ["blkD"] + names[d], kall,
+                   first=False, last=d == PAR["mx"] - 1)
+        for q, (w, n) in enumerate(() if s == 1 and PAR["mx"] else PAR["kn"][W]):
+            hi = lo + w
+            gather(t, h, lo, hi)
+            for j in range(0, 16, n):
+                b, e = turn[0] % ND, min(16, j + n)
+                turn[0] += 1
+                pd, o, i_ = T["pd%d" % b], abd[:, lo:hi, j:e], T["pd%d" % b][:, 0:w * (e - j)]
+                for x in range(j, e, PAR["pu"]):
+                    mm([(pd[:, k - j:w * (e - j):e - j], M[sign], rec[:, 16 * lo + ((k + d) & 15):16 * hi:16], max(w, 64))
+                        for k in range(x, min(e, x + PAR["pu"])) for sign, d in (("I", 0), ("nI", s))], ["I", "nI"] + recs(h, lo, hi), ["pd%d_0" % b], each=2)
+                op("act", [lambda o=o, i_=i_: S.activation(o, i_, F.Abs)], ["pd%d_0" % b], ["abd%s%d_%d" % (H, q, k) for k in range(j, e)], w * (e - j))
+                if hi == W:
+                    mm([(bank_[0:W, k:128:16], abd[:, :, k], T["blkD"][:, 0:8], 64) for k in range(j, e)],
+                       ["blkD"] + ["abd%s%d_%d" % (H, x, k) for k in range(j, e) for x in range(q + 1)], kall, first=False, last=e == 16)
+            lo = hi
+        pn, bm, ou, on = T["pn" + H], T["bm" + H], T["oz" + H][0:W, :], "oz" + H
+        scan(pn[0:W, :], rs[0:W, 128 * h:128 * h + 128], key, FAR, A.min, A.min, ["thr"] + k0, ["least" + H], 128)
+        scan(bm[0:W, ::-1], T["rstm"][0:W, :], pn[0:W, ::-1], 0.0, A.max, A.min, ["rstm", "least" + H], ["bm" + H], 128)
+        tt(ou, key, bm[0:W, :], A.is_equal, k0 + ["bm" + H], [on], 128)
         if (t, si) != (NV - 1, 2):
-            tt(T["go"][0:W, 8 * h:8 * h + 8], T["pn" + H][0:W, 15::16], rs[0:W, 128 * h:128 * h + 128:16], A.is_lt, ["least" + H, "thr"], ["go" + H], 8)
-        mm([(x2, T["ou" + H][0:W, 0, :], T["mb"][0:W, 0, 0:W], W)], ["ohU" + H, "I"], k2)
-        cc = pm[:, W * h:W * h + W]
-        if PAR["hl"]:
-            mm([(x3, T["ou" + H][0:W, 0, :], T["mb"][0:W, 0, 0:W], W)], ["ohU" + H, "I"], k3)
-            tt(w2[:], T["ph" + H][:, 2 * W:4 * W], hl[:], A.mult, k2 + k3 + ["hi" + H, "lo" + H], ["w" + H], 2 * W)
-            mm([(x1, M["Ih"], a, W), (x1, M["nblk"], w2[:, 0:W], W)], ["Ih", "nblk", an, "w" + H], k1)
-            mm([(x3, M["blk"], w2[:, 0:W], W), (x3, M["nblk"], w2[:, W:2 * W], W)], ["blk", "nblk", "w" + H], k3)
-            ts(m, x1, 0.0, None, A.is_equal, None, k1, ["m" + H], W)
-            tt(x3, x3, m, A.mult, k3 + ["m" + H], k3, W)
-            tt(a, a, x3, A.subtract, [an] + k3, [an], W)
-            if PAR["dm"]:
-                mm([(pm[:, 384:384 + W], T["ou" + H][0:W, 0, :], T["mb"][0:W, 0, 0:W], W)], ["ohU" + H, "I"], ["pm_d"])
-                either(oh, pm[:, 384:384 + W], ["pm_d"], [en], W)
-            else:
-                either(oh, x2, k2, [en], W)
-            mm([(cc, M["Sh%d" % si], Cc, W), const(cc, "rBIG"), (cc, T["ou" + H][0:W, 0, :], T["mb"][0:W, 3, 0:W], W)],
-               ["Sh%d" % si, cn, "r1", "rBIG", "ohU" + H, "nBI"], ["pm_c" + H])
-            tt(Cc, cc, Cc, A.min, ["pm_c" + H, cn], [cn], W)
-            return
-        either(oh, x2, k2, [en], W)
-        mm([(x1, M["IJ%d" % si], oh, W)], [en, "IJ%d" % si], k1)
-        tt(w, x1, a, A.mult, k1 + [an], ["w" + H], W)
-        xd, kd = (pm[:, 384:384 + W], ["pm_d"]) if PAR["dm"] else (x2, k2)
-        mm([(xd, M["sig%d" % si], w, W)], ["sig%d" % si, "w" + H], kd)
-        ad = T["wf" + H][:, 1, :]
-        if PAR["relu"]:
-            mm([(x3, M["I2h"], a, W), (x3, M["bit%d" % si], w, W)], ["I2h", "bit%d" % si, an, "w" + H], k3)
-        mm([(x1, M["I2h"], a, W), (x1, M["nblk"], w, W)], ["I2h", "nblk", an, "w" + H], k1)
-        if PAR["relu"]:
-            affine(ad, xd, "relu", 2.0, 0.0, kd, ["ad" + H], W)
-            tt(m, x3, ad, A.is_equal, k3 + ["ad" + H], ["m" + H], W)
+            tt(T["go"][0:W, 8 * h:8 * h + 8], pn[0:W, 15::16], rs[0:W, 128 * h:128 * h + 128:16], A.is_lt, ["least" + H, "thr"], ["go" + H], 8)
+        for j, (lo, hi) in enumerate(halves(W)):
+            w, J, aj = hi - lo, H + str(j), half(t, h, lo, hi)
+            x2, k2 = place_(h, "oh%d" % j, 1, 0, w)
+            (m1, n1), (m2, n2) = place_(h, "e%d" % j, 1, 0, w), place_(h, "e%d" % j, 1, w, 2 * w)
+            tb, ex = T["wb" + H][:, 5, lo:hi], T["ex" + H][:, si, lo:hi]
+            mm([(x2, ou, T["mb"][0:W, 0, lo:hi], w)], [on, "I"], k2)
+            tt(wh[:, 2, lo:hi], x2, wh[:, 0, lo:hi], A.mult, k2 + ["hi" + H], ["wa" + J], w)
+            tt(wh[:, 3, lo:hi], x2, wh[:, 1, lo:hi], A.mult, k2 + ["lo" + H], ["wi" + J], w)
+            mm([(m1, M["blk"], wh[:, 2, lo:hi], w)], ["blk", "wa" + J], n1)
+            tt(tb, m1, aj, A.not_equal, n1 + [an[j]], ["tb" + J], w)
+            mm([(m2, M["blk"], wh[:, 3, lo:hi], w), (m2, M["I8k"], tb, w)], ["blk", "wi" + J, "I8k", "tb" + J], n2)
+            tt(aj, m2, aj, A.min, n2 + [an[j]], [an[j]], w)
+            affine(ex, x2, 1.0, EX[si], k2, ["ex%d%s" % (si, J)], w)
+        if si < 2:
+            mm([(x1, M["Sh%d" % si], Cc, W), (x1, M["nBI"], T["ex" + H][:, si, :], W)], ["Sh%d" % si, cn, "nBI"] + both("ex%d%d" % (si, h)), k1)
         else:
-            op("act", [lambda: S.activation(ad, xd, F.Abs)], kd, ["ad" + H], W)
-            tt(m, x1, ad, A.is_equal, k1 + ["ad" + H], ["m" + H], W)
-        tt(x1, x1, m, A.mult, k1 + ["m" + H], k1, W)
-        tt(a, a, x1, A.subtract, [an] + k1, [an], W)
-        cc = pm[:, W * h:W * h + W]
-        mm([(cc, M["Sh%d" % si], Cc, W), const(cc, "rBIG"), (cc, M["nBI"], oh, W)], ["Sh%d" % si, cn, "r1", "rBIG", en, "nBI"], ["pm_c" + H])
-        tt(Cc, cc, Cc, A.min, ["pm_c" + H, cn], [cn], W)
+            mm([(x1, M["Sh%d" % si], Cc, W), const(x1, "rBIG", W), (x1, ou, T["mb"][0:W, 3, 0:W], W)], ["Sh%d" % si, cn, "r1", "rBIG", on, "nBI"], k1)
+        tt(Cc, x1, Cc, A.min, k1 + [cn], [cn], W)
 
     def count():
-        go, o, n = T["go"], T["one16"][0:W, 0:W], 8 * NP
-        terms = [(pm[0:W, 256:256 + n], o, go[0:W, :], n)]
+        go, o, n, p0, W = T["go"], T["one16"][0:WM, 0:WM], 8 * NP, T["pm0"], WM
+        terms = [(p0[0:W, 480:480 + n], o, go[0:W, :], 64)]
         for r in range(8, n, 8):
-            terms += [(pm[0:W, 256:256 + n - r], o, go[0:W, r:n], n), (pm[0:W, 256 + n - r:256 + n], o, go[0:W, 0:r], n)]
-        mm(terms, ["one16"] + ["go%d" % h for h in range(NP)], ["pm_n"])
+            terms += [(p0[0:W, 480:480 + n - r], o, go[0:W, r:n], 64), (p0[0:W, 480 + n - r:480 + n], o, go[0:W, 0:r], 64)]
+        mm(terms, ["one16"] + ["go%d" % h for h in range(NP)], ["pm0_n"])
         cnt = T["cnt"][0:W, :]
-        tt(cnt, pm[0:W, 256:256 + n], cnt, A.add, ["pm_n", "cnt"], ["cnt"], n)
+        tt(cnt, p0[0:W, 480:480 + n], cnt, A.add, ["pm0_n", "cnt"], ["cnt"], n)
         ts(cnt, cnt, 511, None, A.bitwise_and, None, ["cnt"], ["cnt"], n)
         tt(rs[0:W, ::16], T["th16"][0:W, :], cnt, A.add, ["th16", "cnt"], ["thr"], n)
 
     def refill(t, h):
-        H, last = str(h), t == NV - 1
+        H, last, W = str(h), t == NV - 1, WS[h]
+        NL = W // 16
         L, a, Cc, ln, an, cn = state(t, h)
-        (key, k0), (x1, k1), (x2, k2), (x3, k3) = [slot(h, x) for x in ("key", "x1", "x2", "x3")]
-        ex, ohU, kexp = T["ex" + H], T["ou" + H][0:W, 0, :], T["ou" + H]
-        J, exn = ["J%d" % e for e in range(3)], ["ex%d%d" % (e, h) for e in range(3)]
+        key, k0 = T["ph" + H][0:W, 0:128], ["ph%s_0" % H, "ph%s_1" % H]
+        (x1, k1), (x2, k2), (m0, n0) = place_(h, "emp"), place_(h, "oz"), place_(h, "new")
+        zp, kz = place_(h, "lz")
+        eye = {"I": T["mb"][0:W, 0, 0:W], "I8k": T["mb"][0:W, 4, 0:W], "Ih": T["mh"][0:W, 0, 0:W]}
+        ex, J, en = [T["ex" + H][:, e, :] for e in range(3)], [M["J%d" % e] for e in range(3)], ["J0", "J1", "J2"]
+        for e in range(3):
+            en += both("ex%d%d" % (e, h))
         off = 0.0 if last else 2048.0
-        si_, sf, su, sk = T["si" + H], T["sf" + H], T["su" + H], T["sk" + H]
-        z, nb, wa, wc = T["wb" + H][:, 3, :], T["wb" + H][:, 2, :], T["wh" + H][:, 1, :], T["wh" + H][:, 2, :]
-        (zp, ul), ks = slot(h, "sm")
-        mm([(x1, M[J[e]], ex[:, e, :], W) for e in range(3)], exn + J, k1)
+        ll, su, tl = T["ll" + H], T["su" + H], T["tl" + H]
+        nb, z, y, ck = [T["wb" + H][:, j, :] for j in range(1, 5)]
+        oz, pn, bm, wh = T["oz" + H][0:W, :], T["pnh" + H], T["bmh" + H], T["wh" + H]
+        mm([(x1, J[e], ex[e], W) for e in range(3)], en, k1)
         index(t, h, True)
-        gather(t, h)
-        mm([(key, Cc, M["n16h"], 128), (key, T["mb"][:, 0, 0:W], T["mk"][:], 128)] + [(key, ex[:, e, :], M[J[e]], 128) for e in range(3)],
-           [cn, "n16h", "I", "mk"] + J + exn, k0)
-        pick(h, T["rstm"][0:W, :], "rstm")
-        cp(si_[0:W, 4, :], T["pn" + H][0:W, 15::16], ["least" + H], ["sx" + H], 8)
-        ts(sk[0:W, :], si_[0:W, 4, :], 15, None, A.bitwise_and, None, ["sx" + H], ["sk" + H], 8)
-        tt(kexp[:, 1, :], sk[:, 0:8].indirect(T["l16"][:, 0:8]), M["mP"], A.mult, ["sk" + H, "l16", "mP"], ["kexp" + H], 128, True)
-        mm([(zp, kexp[0:W, 1, :], T["blkD"][0:W, 0:NL], 8), (zp, M["I"], T["cz"][:, 0:NL], 8)], ["kexp" + H, "blkD", "I", "cz"], ks)
-        ts(su[:, 0:NL], zp, C["rk16"], None, A.add, None, ks + ["rk16"], ["zo" + H], 8)
-        en = "ohU" + H
-        mm([(x2, ohU, T["mb"][0:W, 0, 0:W], W)], [en, "I"], k2)
-        mm([(x3, ohU, T["mb"][0:W, 2, 0:W], W)] + [(x3, M[J[e]], ex[:, e, :], W) for e in range(3)], [en, "BI"] + J + exn, k3)
-        affine(nb, x3, "id", -(8192.0 + off) / BIG, 8192.0, k3, ["nb" + H], W)
-        tt(wa, x2, a, A.mult, k2 + [an], ["wa" + H], W)
-        tt(wc, x2, Cc, A.mult, k2 + [cn], ["wc" + H], W)
-        rf, top, nq = T["rec" + H], T["top" + H], W // 64
-        rfn = ["rec%s%d" % (H, c) for c in range(NU)]
-        for c in range(nq):
-            scan(top[:, 1024 * c:1024 * c + 1024], T["rst1"][:], rf[:, 1024 * c:1024 * c + 1024], 0.0, A.mult, A.max,
-                 ["rst1"] + rfn[c * NU // nq:(c + 1) * NU // nq], ["top%s%d" % (H, c)], 512)
-        either(z, rf[:, 0:16 * W].indirect(su[:, 0:NL]), rfn + ["zo" + H], ["z" + H], ("g", W))
-        ui, sl, u, n = [si_[:, j, 0:NL] for j in range(4)]
-        if PAR["ul"]:
-            mm([(key, M["Wq"], z, W)], ["Wq", "z" + H], k0)
-            tt(T["bm" + H][:], key, M["mP"], A.mult, k0 + ["mP"], ["bm" + H], W)
-            scan(T["pn" + H][:], T["rst1"][:, 0:W], T["bm" + H][:], 0.0, A.mult, A.add, ["rst1", "bm" + H], ["least" + H], W)
-            ts(ui, T["pn" + H][:, 15::16], 16.0, None, A.mult, None, ["least" + H], ["ui" + H], 8)
-        else:
-            mm([(ul, T["Wb"][:, 15 - p:143 - p], T["wb" + H][:, 3, p::16], 8) for p in range(16)], ["Wb", "z" + H], ks)
-            cp(ui, ul, ks, ["ui" + H], 8)
-        (uo, ku), (a2, ka2), (c2, kc2), (zt, kz), (l1, kl1), (a1, ka1), (c1, kc1) = [slot(h, x) for x in ("uo", "a2", "c2", "zt", "l1", "a1", "c1")]
-        mm([(zt, M["I"], z, W), (zt, M["I"], top[:, 15::16], W)], ["I", "z" + H] + ["top%s%d" % (H, c) for c in range(nq)], kz)
-        zti, uoi, ae, ck = [T["wi" + H][:, j, :] for j in range(1, 5)]
-        ts(zti, zt, 0.5, -0.25, A.mult, A.add, kz, ["zti" + H], W)
-        ts(sl, ui, 15, None, A.bitwise_and, None, ["ui" + H], ["sl" + H], 8)
-        tt(sl, sl, T["csl"][:, 0:NL], A.add, ["sl" + H, "csl"], ["sl" + H], 8)
-        cp(su[:, 8:8 + NL], sl, ["sl" + H], ["sl16" + H], 8)
+        gather(t, h, 0, W)
+        mm([(key, Cc, M["n16h"], 128), (key, rows[0:2, 0, 0:W], RW["rk"], 128)] + [(key, ex[e], J[e], 128) for e in range(3)],
+           [cn, "n16h", "r1", "rk"] + en, k0)
+        scan(pn[0:W, :], T["rsth"][0:W, :], key, 0.0, A.max, A.min, ["rsth"] + k0, ["leasth" + H], 128)
+        scan(bm[0:W, ::-1], T["rsth"][0:W, :], pn[0:W, ::-1], 0.0, A.max, A.min, ["rsth", "leasth" + H], ["bmh" + H], 64)
+        tt(oz, key, bm[0:W, :], A.is_equal, k0 + ["bmh" + H], ["oz" + H], 128)
+        mm([(x2, oz, eye["I"], W)], ["oz" + H, "I"], k2)
+        tt(wh[:, 3, :], x2, tl[:, t, 4 * W + 1:6 * W:2], A.mult, k2 + ["ix" + H], both("wi" + H), W)
+        tt(wh[:, 2, :], x2, a, A.mult, k2 + an, both("wa" + H), W)
+        zs, us = T["wf" + H][:, 0, :], T["wi" + H][:, 0, :]
+        mm([(zp, M["I"], M["else"][:, 0:W], W), (zp, M["blk"], wh[:, 3, :], W)], ["I", "else", "blk"] + both("wi" + H), kz)
+        scan(zs, T["rstm"][:, 0:W], zp, 0.0, A.max, A.min, ["rstm"] + kz, ["zs" + H], W)
+        ts(su[:, 0:NL], zs[:, 15::16], 2048.0, None, A.add, None, ["zs" + H], ["zo" + H], 8)
+        pickup(z, T["X%d" % (t % 2)][:, 0:4112].indirect(su[:, 0:NL]), xnames(t) + ["zo" + H], ["z" + H], W)
+        mm([(m0, J[e], ex[e], W) for e in range(3)] + [(m0, oz, eye["I8k"], W)], ["oz" + H, "I8k"] + en, n0)
+        affine(nb, m0, -(8192.0 + off) / 8192, 8192.0 - (8192.0 + off) / 4, n0, ["nb" + H], W)
+        mm([(zp, M["I"], M["else"][:, 0:W], W), (zp, M["Wq"], z, W)], ["I", "else", "Wq", "z" + H], kz)
+        ui, nn = us[:, 15::16], ll[:, 24 + NL:24 + 2 * NL]
+        scan(us, T["rstm"][:, 0:W], zp, 0.0, A.max, A.min, ["rstm"] + kz, both("v" + H), W)
+        ts(ll[:, 8 + NL:8 + 2 * NL], ui, 4095, None, A.bitwise_and, None, both("v" + H), ["u12" + H], 8)
+        ts(ll[:, 8:8 + NL], ui, 15, None, A.bitwise_and, None, both("v" + H), ["u4" + H], 8)
+        tt(ll[:, 24:24 + 2 * NL], ll[:, 8:8 + 2 * NL], T["cst" + H][:, 0:2 * NL], A.add, ["u4" + H, "u12" + H, "cst" + H], ["sl" + H], 16)
+        tt(nn, nn, nn, A.mult, ["sl" + H], ["sl" + H], 8)
+        ts(nn, nn, 5, 1023, A.arith_shift_right, A.bitwise_and, ["sl" + H], ["sl" + H], 8)
+        cp(su[:, 8:8 + 2 * NL], ll[:, 24:24 + 2 * NL], ["sl" + H], ["su" + H], 16)
+        (pU, kU), (zt, kt), (c2, kc2), (c1, kc1), (l1, kl1), (a2, ka2), (a1, ka1) = [place_(h, x) for x in ("U", "zt", "c2", "c1", "l1", "a2", "a1")]
+        uv, ku = place_(h, "u", 2)
+        pu, pv = uv[:, 0::2], uv[:, 1::2]
+        mm([(pU, M["WqE"], z, W)], ["WqE", "z" + H], kU)
+        affine(y, pU, 1.0 / 4096, CB - 0.5 + 1.0 / 8192, kU, ["y" + H], W)
+        mm([(pu, M["WqE"], z, W), (pu, M["nI12"], y, W)], ["WqE", "z" + H, "nI12", "y" + H], ku)
+        mm(([] if last else [(pv, M["WqE2"], z, W), (pv, M["nI23"], y, W)]) + ([const(pv, "rev%d" % t, W)] if t else []),
+           ["WqE2", "z" + H, "nI23", "y" + H, "r1", "rev%d" % t], ku)
+        rec, top = T["rec" + H], T["top" + H]
+        for c in range(0, W, 64):
+            e = min(W, c + 64)
+            scan(top[:, 16 * c:16 * e], T["rst1"][:, 0:16 * (e - c)], rec[:, 16 * c:16 * e], 0.0, A.mult, A.max,
+                 ["rst1"] + recs(h, c, e), ["top%s%d" % (H, c)], 8 * (e - c))
+        mm([(zt, M["I"], z, W), (zt, M["I"], top[:, 15::16], W)], ["I", "z" + H] + ["top%s%d" % (H, c) for c in range(0, W, 64)], kt)
+        zti, ae, ci = [T["wi" + H][:, j, :] for j in range(1, 4)]
+        ts(zti, zt, 0.5, -0.25, A.mult, A.add, kt, ["zti" + H], W)
         dst, dn = T["X%d" % ((t + 1) % 2)], "X%d%d" % ((t + 1) % 2, h)
-        win = dst[:, 16 * W * h:16 * W * (h + 1)]
-        op("dve", [lambda: V.tensor_copy(win.indirect(su[:, 8:8 + NL]), zti)], ["zti" + H, "sl16" + H, dn], [dn], ("s", W))
+        win = dst[:, 16 * AT[h]:16 * (AT[h] + W)]
+        op("dve", [lambda: V.tensor_copy(win.indirect(su[:, 8:8 + NL]), zti)], ["zti" + H, "su" + H, dn], [dn], ("s", W))
         if last:
-            dma("sp", T["yx"][:, 16 * W * h:16 * W * (h + 1)], win, [dn], [], "sx" + H, 3500)
-        ts(u, ui, 4095, None, A.bitwise_and, None, ["ui" + H], ["u" + H], 8)
-        ts(sf[:, 0, 0:NL], u, -2048.0, None, A.add, None, ["u" + H], ["t1" + H], 8)
-        ts(sf[:, 1, 0:NL], u, 3232.0, None, A.add, None, ["u" + H], ["t2" + H], 8)
-        tt(n, sf[:, 0, 0:NL], sf[:, 1, 0:NL], A.mult, ["t1" + H, "t2" + H], ["n" + H], 8)
-        ts(n, n, 5, 1023, A.arith_shift_right, A.bitwise_and, ["n" + H], ["n" + H], 8)
-        cp(su[:, 16:16 + NL], n, ["n" + H], ["nl" + H], 8)
-        mm([(uo, M["WqO"], z, W)], ["WqO", "z" + H], ku)
-        cp(uoi, uo, ku, ["uo" + H], W)
-        ts(uoi, uoi, 4095, None, A.bitwise_and, None, ["uo" + H], ["uo" + H], W)
+            dma("sp", T["yx"][:, 16 * AT[h]:16 * (AT[h] + W)], win, [dn], [], "sx" + H, 2000 + 12 * W)
         keep = "r10240" if last else "r8192"
-        mm([(a2, M["odd"], wa, W), (a2, M["I"], nb, W), const(a2, "rodd")], ["odd", "wa" + H, "I", "nb" + H, "r1", "rodd"], ka2)
-        mm([(c2, M["blk"], wc, W), (c2, M["I2"], nb, W)] + ([] if last else [const(c2, "r4096")]), ["blk", "wc" + H, "I2", "nb" + H, "r1", "r4096"], kc2)
-        mm([(l1, M["Ih"], L, W), (l1, M["nI"], nb, W), const(l1, keep)], ["Ih", ln, "nI", "nb" + H, "r1", keep], kl1)
-        mm([(a1, M["Ih"], a, W), (a1, M["nI"], nb, W), const(a1, keep)], ["Ih", an, "nI", "nb" + H, "r1", keep], ka1)
-        mm([(c1, M["Ih"], Cc, W), (c1, M["nI"], nb, W), const(c1, "r8192")], ["Ih", cn, "nI", "nb" + H, "r1", "r8192"], kc1)
-        body = T["rbs"][:, 0:1024].indirect(su[:, 16:16 + NL])
-        sL, sA = T["wf" + H][:, 2, :], T["wf" + H][:, 3, :]
+        sL, sA = T["sz" + H][:, 1::2], T["wf" + H][:, 2, :]
         to = T[("tf" if last else "to") + H]
+        oL, oC, oA = to[:, 0:W], to[:, W:2 * W], to[:, 2 * W:3 * W] if last else to[:, 2 * W + 1:4 * W:2]
         o = ["%s%d%d" % ("f" if last else "o", h, j) for j in range(3)]
-        ts(ck, c2, 0.5, -0.25, A.mult, A.add, kc2, ["ck" + H], W)
-        tt(to[:, 2 * W:3 * W], c1, ck, A.min, kc1 + ["ck" + H], [o[2]], W)
-        tt(ae, body, uoi, A.mult, ["rbs", "nl" + H, "uo" + H], ["ae" + H], W, True)
-        if t:
-            ts(ae, ae, C["ev%d" % t], None, A.add, None, ["ae" + H, "ev%d" % t], ["ae" + H], W)
-        ts(ae, ae, 5, 4095, A.arith_shift_right, A.bitwise_and, ["ae" + H], ["ae" + H], W)
-        tt(sA, a2, ae, A.add, ka2 + ["ae" + H], ["sA" + H], W)
-        tt(to[:, W:2 * W], a1, sA, A.min, ka1 + ["sA" + H], [o[1]], W)
-        tt(sL, body, nb, A.add, ["rbs", "nl" + H, "nb" + H], ["sL" + H], W, True)
-        tt(to[:, 0:W], l1, sL, A.min, kl1 + ["sL" + H], [o[0]], W)
+        mm([(c2, bm[0:W, :], eye["Ih"], W), (c2, M["nI2"], nb, W)], ["bmh" + H, "Ih", "nI2", "nb" + H], kc2)
+        mm([(c1, M["Ih"], Cc, W), (c1, M["nI"], nb, W), const(c1, "r8192", W)] + ([const(c1, "rnCB", W)] if last else []),
+           ["Ih", cn, "nI", "nb" + H, "r1", "r8192", "rnCB"], kc1)
         if last:
-            for j, y in enumerate(("yl", "ya", "yc")):
-                dma("sp", T[y][:, W * h:W * h + W], to[:, W * j:W * j + W], [o[j]], [], "sy%d%d" % (h, j), 2500)
+            ck = ci
+            ts(ck, c2, -1.0 / 32, 64 - 0.484375, A.mult, A.add, kc2, ["ck" + H], W)
+        else:
+            affine(ck, c2, -1.0 / 32, CB + 64 + off / 16 - 0.484375, kc2, ["ck" + H], W)
+        tt(oC, c1, ck, A.min, kc1 + ["ck" + H], [o[1]], W)
+        tt(sL, T["rbs"][:, 0:1024].indirect(su[:, 8 + NL:8 + 2 * NL]), nb, A.add, ["rbs0", "rbs1", "su" + H, "nb" + H], ["sL" + H], W, True)
+        mm([(l1, M["Ih"], L, W), (l1, M["nI"], nb, W), const(l1, keep, W)], ["Ih", ln, "nI", "nb" + H, "r1", keep], kl1)
+        tt(oL, l1, sL, A.min, kl1 + ["sL" + H], [o[0]], W)
+        mm([(a2, M["odd"], wh[:, 2, :], W), (a2, M["I"], nb, W), const(a2, "rodd", W)], ["odd", "I", "nb" + H, "r1", "rodd"] + both("wa" + H), ka2)
+        mm([(a1, M["Ih"], a, W), (a1, M["nI"], nb, W), const(a1, keep, W)], ["Ih", "nI", "nb" + H, "r1", keep] + an, ka1)
+        scan(T["vi" + H][:], T["sz" + H][:], uv, 0.0, A.mult, A.add, ku + ["sL" + H, "zsz" + H], both("vi" + H), 2 * W)
+        ts(ae, T["vi" + H][:, 1::2], 5, 4095, A.arith_shift_right, A.bitwise_and, both("vi" + H), ["ae" + H], W)
+        tt(sA, a2, ae, A.add, ka2 + ["ae" + H], ["sA" + H], W)
+        tt(oA, a1, sA, A.min, ka1 + ["sA" + H], [o[2]], W)
+        if last:
+            for j, yn in enumerate(("yl", "yc", "ya")):
+                dma("sp", T[yn][:, AT[h]:AT[h] + W], to[:, W * j:W * j + W], [o[j]], [], "sy%d%d" % (h, j), 2500)
             return
-        land, ar, sn = T["tl" + H][:, t + 1, :], "ar%d%d" % (t, h), "sn%d%d" % (t, h)
-        snd = op("pool", [lambda: g.remote_dma(land, to[:], T.sem[ar], T.sem[sn], pid, rid, mask)], o, [], 1000, sem=sn, inc=-len(eng), lat=2000)
-        op(None, [], [], ["%s%d%d" % (x, t + 1, h) for x in "LaC"], 0, sem=ar, inc=-len(eng), lat=200, after=snd)
+        for j, (lo, hi, R, names) in enumerate(((0, 2 * W, o[:2], "LC"), (2 * W, 4 * W, [o[2], "zto" + H], "a")) if PAR["two"] else
+                                               ((0, 4 * W, o + ["zto" + H], "LaC"),)):
+            land, src, ar, sn = tl[:, t + 1, lo:hi], to[:, lo:hi], "ar%d%d%d" % (t, h, j), "sn%d%d%d" % (t, h, j)
+            snd = op("pool", [lambda land=land, src=src, ar=ar, sn=sn: g.remote_dma(land, src, T.sem[ar], T.sem[sn], pid, rid, mask)], R, [], 1000,
+                     sem=sn, inc=-len(eng), lat=2000)
+            op(None, [], [], ["%s%d%d" % (x, t + 1, h) for x in names if x != "a"] + (both("a%d%d" % (t + 1, h)) if "a" in names else []), 0,
+               sem=ar, inc=-len(eng), lat=200, after=snd)
 
     for t in range(NV):
-        stage[0] = 4 * NP * t
-        dma("sp", T["X%d" % ((t + 1) % 2)][:, 0:4096], T["X%d" % (t % 2)][:, 0:4096], xnames(t)[1:], ["X%d%d" % ((t + 1) % 2, h) for h in range(NP)],
-            "cx%d" % t, 6000)
         for si in range(4):
+            if si == 1:
+                dma("sp", T["X%d" % ((t + 1) % 2)][:, 0:4096], T["X%d" % (t % 2)][:, 0:4096], xnames(t)[1:],
+                    ["X%d%d" % ((t + 1) % 2, h) for h in range(NP)], "cx%d" % t, 6000)
+                ops[-1]["after"] = max(i for i, o in enumerate(ops) if o["W"][:1] == ["off%d0" % (NP - 1)])
             for h in range(NP):
                 stage[0] = 4 * NP * t + NP * si + h
                 if si == 0:
-                    L, ln = state(t, h)[0], state(t, h)[3]
-                    lp, qp = pq[:, 2 * W * h:2 * W * h + W], pq[:, 2 * W * h + W:2 * W * h + 2 * W]
-                    mm([(lp, M["Ih"], L, W), const(lp, "r3232")], ["Ih", ln, "r1", "r3232"], ["pq_L%d" % h])
-                    mm([(qp, M["I2080"], L, W)], ["I2080", ln], ["pq_Q%d" % h])
+                    L, ln, W = state(t, h)[0], state(t, h)[3], WS[h]
+                    lp, qp = pq[:, 2 * AT[h]:2 * (AT[h] + W):2], pq[:, 2 * AT[h] + 1:2 * (AT[h] + W):2]
+                    mm([(lp, M["Ih"], L, W), const(lp, "r3232", W)], ["Ih", ln, "r1", "r3232"], ["pq_L%d" % h])
+                    mm([(qp, M["I2080"], L, W)], ["I2080", ln], ["pq_L%d" % h])
                 if si < 3:
                     step(t, h, si)
                 else:
@@ -617,11 +639,12 @@ def refine(ops, par):
             late[i] = NV * (4 * per + extra) + s % NP * per / NP
         for d in deps[i]:
             late[d] = min(late[d], late[i] - dur[d] - fwd(d, i))
+    seen = {}
     for i in range(n):
-        key = "%d%s" % (ops[i]["stage"] % (4 * NP), (ops[i]["W"] + [""])[0])
-        late[i] += 100.0 * par["bias"].get(key, 0)
         if qs[i] == "any":
-            qs[i] = {"a": "act", "d": "dve"}.get(par["force"].get(key), "any")
+            key = ("s" if ops[i]["stage"] % (4 * NP) < 3 * NP else "r") + ops[i]["W"][0][:2]
+            k = seen[key, ops[i]["stage"]] = seen.get((key, ops[i]["stage"]), -1) + 1
+            qs[i] = {"A": "act", "D": "dve"}.get((par["force"].get(key, "") + "-" * 9)[k], "any")
     st, out = place(ops, par, dur, deps, fwd, late, qs)
     best = None
     for _ in range(par["rounds"]):
@@ -641,6 +664,259 @@ def refine(ops, par):
     return best
 
 
+def rhythm(ops, par, plan, tries, heat, steps, upto, seed=1):
+    n = len(ops)
+    deps = edges(ops)
+    qn = {"dve": 0, "act": 1, "pe": 2, "pool": 3, "sp": 4, None: 5}
+    dur, lat, hop = [cost(o, par) for o in ops], [o["lat"] for o in ops], par["hop"]
+    pre = [[(d, lat[d] + (0.0 if ops[d]["q"] == "pe" == ops[i]["q"] else hop)) for d in deps[i]] for i in range(n)]
+    succ = [[] for _ in range(n)]
+    for i in range(n):
+        for d in deps[i]:
+            succ[d].append(i)
+    names = sorted(set(b for o in ops for b in o["banks"]))
+    bk = [[3 * names.index(b) for b in o["banks"]] for o in ops]
+    other = [[(b + e, b + me) for b in bk[i] for e in (0, 1, 2) if e != me] for me in (0, 1, 2) for i in range(n)]
+    free = [o["q"] == "any" for o in ops]
+    kinds, kind, seen, base, N = {}, [], {}, [], n
+    for o in ops:
+        x = (o["W"] + o["R"] + ["-"])[0]
+        x = x[0] + x[2:] if x[0] in "aLCX" and x[1:].isdigit() else ("o" + x[1:] if x[0] == "f" else x)
+        s = o["stage"] % (4 * NP)
+        tied = steps and s < 3 * NP
+        x = x[:2] + x[3:] if tied and x[:2] == "ex" else ("pd" if tied and x[:2] == "pd" else x)
+        k = seen[o["stage"], x, o["q"], 1] = seen.get((o["stage"], x, o["q"], 1), -1) + 1
+        kind.append(kinds.setdefault((s % NP if tied else s + NP, x, o["q"], k), len(kinds)))
+        base.append(o["stage"] // (4 * NP) * par["period"] + (s // NP * par["beat"] if tied else 0.0))
+    phase, eng = [0.0] * len(kinds), [0] * len(kinds)
+    for i in sorted(range(n), key=lambda i: -abs(ops[i]["stage"] - 5.6 * NP)):
+        phase[kind[i]], eng[kind[i]] = plan[1][i] - base[i], qn[plan[3][i]]
+    some = sum(1 for o in ops if o["stage"] < upto)
+    dl = [list(d) for d in deps]
+
+    def run(phase, eng, n=some):
+        rank = [0.0] * n
+        for i in range(n):
+            r = base[i] + phase[kind[i]]
+            for d in dl[i]:
+                if rank[d] >= r:
+                    r = rank[d] + 0.001
+            rank[i] = r
+        order = sorted(range(n), key=lambda i: rank[i])
+        end, why, last, use = [0.0] * (n + 1), [n] * n, [n] * 6, [n] * (3 * len(names))
+        for i in order:
+            me = eng[kind[i]]
+            w = last[me]
+            s = end[w]
+            for d, x in pre[i]:
+                if end[d] + x > s:
+                    s, w = end[d] + x, d
+            if bk[i]:
+                for b, mine in other[me * N + i]:
+                    if end[use[b]] + hop > s:
+                        w = use[b]
+                        s = end[w] + hop
+                    use[mine] = i
+            end[i], why[i], last[me] = s + dur[i], w, i
+            last[5] = n
+        i = max(range(n), key=lambda j: end[j] + lat[j])
+        total, path = end[i] + lat[i], []
+        while why[i] < n:
+            if why[i] not in deps[i] or free[i]:
+                path.append((why[i], i))
+            i = why[i]
+        return total, path, order, rank
+    cur, path, order, rank = run(phase, eng)
+    best = (cur, phase, eng)
+    for it in range(tries):
+        seed = (seed * 1103515245 + 12345) % 2147483648
+        u, v = path[(seed >> 8) % len(path)]
+        p2, e2 = phase, eng
+        if free[v] and (u in deps[v] or (seed >> 4) % 4 == 0):
+            e2 = list(eng)
+            e2[kind[v]] = 1 - e2[kind[v]]
+        elif free[u] and (seed >> 4) % 4 == 1:
+            e2 = list(eng)
+            e2[kind[u]] = 1 - e2[kind[u]]
+        else:
+            if u in deps[v]:
+                continue
+            p2, todo, step = list(phase), [v if (seed >> 6) % 2 else u], ((seed >> 9) % 3) * 100.0 + 1.0
+            if (seed >> 6) % 2:
+                goal = rank[u] - step
+                while todo:
+                    x = todo.pop()
+                    if rank[x] > goal and p2[kind[x]] + base[x] > goal:
+                        p2[kind[x]] = goal - base[x]
+                        todo += deps[x]
+            else:
+                p2[kind[u]] = rank[v] + step - base[u]
+        r = run(p2, e2)
+        if r[0] <= cur + heat * (1.0 - it / tries) * ((seed >> 12) % 100) / 100.0:
+            cur, path, order, rank = r
+            phase, eng = p2, e2
+            if cur < best[0]:
+                best = (cur, phase, eng)
+    back = {x: k for k, x in qn.items()}
+    r = run(best[1], best[2], n)
+    return [r[2], r[3], r[0], [back[best[2][kind[i]]] for i in range(n)]]
+
+
+def search(ops, par, seed=1):
+    n = len(ops)
+    deps = edges(ops)
+    qn = {"dve": 0, "act": 1, "pe": 2, "pool": 3, "sp": 4, None: 5}
+    dur, lat, hop = [cost(o, par) for o in ops], [o["lat"] for o in ops], par["hop"]
+    pre = [[(d, dur[d] + lat[d] + (0.0 if ops[d]["q"] == "pe" == ops[i]["q"] else hop)) for d in deps[i]] for i in range(n)]
+    post = [[] for _ in range(n)]
+    for i in range(n):
+        for d, x in pre[i]:
+            post[d].append((i, x - dur[d] + dur[i]))
+    names = sorted(set(b for o in ops for b in o["banks"]))
+    bk = [[6 + names.index(b) for b in o["banks"]] for o in ops]
+    free = [o["q"] == "any" for o in ops]
+    kinds, kind, seen, eng = {}, [], {}, []
+    for o in ops:
+        x = (o["W"] + o["R"] + ["-"])[0]
+        x = x[0] + x[2:] if x[0] in "aLCX" and x[1:].isdigit() else ("o" + x[1:] if x[0] == "f" else x)
+        k = seen[o["stage"], x, o["q"]] = seen.get((o["stage"], x, o["q"]), -1) + 1
+        kind.append(kinds.setdefault((o["stage"] % (4 * NP) if o["stage"] >= 0 else -1, x, o["q"], k), len(kinds)))
+        mine = x[:3] == "rec" and x[4:] == "2" and (NP if par["mx"] else 0) <= o["stage"] % (4 * NP) < 3 * NP
+        eng.append(qn[o["q"]] if o["q"] != "any" else (0 if mine else 1))
+    same = [[] for _ in kinds]
+    for i in range(n):
+        same[kind[i]].append(i)
+
+    def lay(order, pre, eng, first):
+        st, why = [0.0] * n, [-1] * n
+        ends = [[-1e9] for _ in range(6 + len(names))]
+        who = [[0] for _ in range(6 + len(names))]
+        for i in order:
+            t, w, me, du = first[i], -1, eng[i], dur[i]
+            for d, x in pre[i]:
+                if st[d] + x > t:
+                    t, w = st[d] + x, d
+            if me < 5:
+                E, Wn = ends[me], who[me]
+                k = m = len(E)
+                while E[k - 1] > t:
+                    k -= 1
+                while True:
+                    while k < m and (E[k] <= t or st[Wn[k]] < t + du):
+                        if E[k] > t:
+                            t, w = E[k], Wn[k]
+                        k += 1
+                    t0 = t
+                    for b in bk[i]:
+                        B, Wb = ends[b], who[b]
+                        j = len(B)
+                        while B[j - 1] > t - hop:
+                            j -= 1
+                        while j < len(B) and st[Wb[j]] - hop < t + du:
+                            if eng[Wb[j]] != me:
+                                t, w = B[j] + hop, Wb[j]
+                            j += 1
+                    if t == t0:
+                        break
+                E.insert(k, t + du)
+                Wn.insert(k, i)
+                for b in bk[i]:
+                    B = ends[b]
+                    j = len(B)
+                    while B[j - 1] > t + du:
+                        j -= 1
+                    B.insert(j, t + du)
+                    who[b].insert(j, i)
+            st[i], why[i] = t, w
+        return st, why
+    zero = [0.0] * n
+
+    def run(rank, eng, rounds):
+        rank = list(rank)
+        for i in range(n):
+            r = rank[i]
+            for d, x in pre[i]:
+                if rank[d] >= r:
+                    r = rank[d] + 0.001
+            rank[i] = r
+        st, why = lay(sorted(range(n), key=lambda i: rank[i]), pre, eng, zero)
+        for _ in range(rounds):
+            back = lay(sorted(range(n), key=lambda i: (-st[i] - dur[i], -i)), post, eng, lat)[0]
+            st, why = lay(sorted(range(n), key=lambda i: (-back[i] - dur[i], i)), pre, eng, zero)
+        order, total, path = sorted(range(n), key=lambda i: (st[i], i)), 0.0, []
+        for du, la, pr, hp, scale in cases:
+            end, why, last, use = [0.0] * (n + 1), [n] * n, [n] * 6, [n] * (3 * len(names) + 18)
+            for i in order:
+                me = eng[i]
+                w = last[me]
+                s = end[w]
+                for d, x in pr[i]:
+                    if end[d] + x > s:
+                        s, w = end[d] + x, d
+                if bk[i]:
+                    for b, mine in other[me * n + i]:
+                        if end[use[b]] + hp > s:
+                            w = use[b]
+                            s = end[w] + hp
+                        use[mine] = i
+                end[i], why[i], last[me] = s + du[i], w, i
+                last[5] = n
+            i = max(tails, key=lambda j: end[j] + la[j])
+            total += (end[i] + la[i]) * scale
+            while why[i] < n:
+                if why[i] not in deps[i] or free[i]:
+                    path.append((why[i], i))
+                i = why[i]
+        return total, path, st
+    other = [[(3 * b + e, 3 * b + me) for b in bk[i] for e in (0, 1, 2) if e != me] for me in (0, 1, 2) for i in range(n)]
+    tails = [i for i in range(n) if not post[i]]
+    cases = []
+    for x in par["cases"]:
+        p = dict(par)
+        p.update(x)
+        la = [o["lat"] * p["dma"] for o in ops]
+        cases.append(([cost(o, p) for o in ops], la,
+                      [[(d, la[d] + (0.0 if ops[d]["q"] == "pe" == ops[i]["q"] else p["hop"])) for d in deps[i]] for i in range(n)], p["hop"],
+                      p["weight"]))
+    per, extra = par["per"], par["extra"]
+    late = [1e12] * n
+    for i in range(n - 1, -1, -1):
+        s = ops[i]["stage"]
+        if ops[i]["W"] and ops[i]["W"][0][:3] == "off":
+            late[i] = min(late[i], s * per / NP + s // (4 * NP) * extra)
+        if late[i] == 1e12:
+            late[i] = NV * (4 * per + extra) + s % NP * per / NP
+        for d, x in pre[i]:
+            late[d] = min(late[d], late[i] - x)
+    cur, path, st = run(late, eng, 3)
+    best = (cur, st, eng)
+    for tries, heat in par["search"]:
+        cur, path, st = run(best[1], best[2], 0)
+        eng = best[2]
+        for it in range(tries):
+            r2, e2 = list(st), eng
+            for _ in range(1 + seed % 3):
+                seed = (seed * 1103515245 + 12345) % 2147483648
+                u, v = path[(seed >> 8) % len(path)]
+                if free[v] and (u in deps[v] or (seed >> 4) % 4 == 0) or free[u] and (seed >> 4) % 4 == 1:
+                    x = v if free[v] and (u in deps[v] or (seed >> 4) % 4 == 0) else u
+                    e2 = list(e2)
+                    for j in same[kind[x]]:
+                        e2[j] = 1 - eng[x]
+                elif u not in deps[v]:
+                    sh = st[v] - st[u] + 1.0 + ((seed >> 9) % 3) * par["amp"]
+                    for j in same[kind[u]]:
+                        r2[j] += sh
+            r = run(r2, e2, (seed >> 7) % 2)
+            if r[0] <= cur + heat * (1.0 - it / tries) * ((seed >> 12) % 100) / 100.0:
+                cur, path, st = r
+                eng = e2
+                if cur < best[0]:
+                    best = (cur, st, eng)
+    back = {x: k for k, x in qn.items()}
+    return [sorted(range(n), key=lambda i: (best[1][i], i)), best[1], best[0], [back[x] for x in best[2]]]
+
+
 def polish(ops, par, plan, tries, seed=1):
     n = len(ops)
     deps = edges(ops)
@@ -657,41 +933,57 @@ def polish(ops, par, plan, tries, seed=1):
     bk = [[3 * names.index(b) for b in o["banks"]] for o in ops]
     order, q = list(plan[0]), [qn[x] for x in plan[3]]
 
-    def run(order, q):
-        end, why, last, use = [0.0] * (n + 1), [n] * n, [n] * 6, [n] * (3 * len(names))
-        for i in order:
-            me = q[i]
-            w = last[me] if me < 5 else n
-            s = end[w]
-            for d, x in pre[i]:
-                if end[d] + x > s:
-                    s, w = end[d] + x, d
-            for b in bk[i]:
-                for e in (0, 1, 2):
-                    if e != me and end[use[b + e]] + hop > s:
-                        w = use[b + e]
-                        s = end[w] + hop
-                use[b + me] = i
-            end[i], why[i], last[me] = s + dur[i], w, i
-        i = max(range(n), key=lambda j: end[j] + lat[j])
-        total, path = end[i] + lat[i], []
+    other = [[(b + e, b + me) for b in bk[i] for e in (0, 1, 2) if e != me] for me in (0, 1, 2) for i in range(n)]
+    ends = [i for i in range(n) if not succ[i]]
+    free = [ops[i]["q"] == "any" for i in range(n)]
+    gap = 32
+
+    def run(order, q, first, old):
+        c = first // gap
+        end, why, marks = list(old[0]), list(old[1]), old[2][:c + 1]
+        last, use = list(marks[c][0]), list(marks[c][1])
+        for c in range(c * gap, n, gap):
+            for i in order[c:c + gap]:
+                me = q[i]
+                w = last[me]
+                s = end[w]
+                for d, x in pre[i]:
+                    if end[d] + x > s:
+                        s, w = end[d] + x, d
+                if bk[i]:
+                    for b, mine in other[me * n + i]:
+                        if end[use[b]] + hop > s:
+                            w = use[b]
+                            s = end[w] + hop
+                        use[mine] = i
+                end[i], why[i], last[me] = s + dur[i], w, i
+                last[5] = n
+            marks.append((list(last), list(use)))
+        i = max(ends, key=lambda j: end[j] + lat[j])
+        return end[i] + lat[i], i, (end, why, marks)
+
+    def trail(i, why):
+        path = []
         while why[i] < n:
-            if why[i] not in deps[i] or ops[i]["q"] == "any":
+            if why[i] not in deps[i] or free[i]:
                 path.append((why[i], i))
             i = why[i]
-        return total, path
-    cur, path = run(order, q)
+        return path
+    cur, i, state = run(order, q, 0, ([0.0] * (n + 1), [n] * n, [([n] * 6, [n] * (3 * len(names)))]))
+    path = trail(i, state[1])
     best = (cur, order, q)
     for it in range(tries):
         seed = (seed * 1103515245 + 12345) % 2147483648
         u, v = path[(seed >> 8) % len(path)]
         o2, q2 = order, q
-        if ops[v]["q"] == "any" and (u in deps[v] or (seed >> 4) % 4 == 0):
+        if free[v] and (u in deps[v] or (seed >> 4) % 4 == 0):
             q2 = list(q)
             q2[v] = 1 - q2[v]
-        elif ops[u]["q"] == "any" and (seed >> 4) % 4 == 1:
+            a = order.index(v)
+        elif free[u] and (seed >> 4) % 4 == 1:
             q2 = list(q)
             q2[u] = 1 - q2[u]
+            a = order.index(u)
         else:
             a, b = order.index(u), order.index(v)
             mid = order[a:b + 1]
@@ -711,9 +1003,9 @@ def polish(ops, par, plan, tries, seed=1):
                 if v in move:
                     continue
                 o2 = order[:a] + [x for x in mid if x not in move] + [x for x in mid if x in move] + order[b + 1:]
-        t, p = run(o2, q2)
+        t, i, st = run(o2, q2, a, state)
         if t <= cur + par["heat"] * (1.0 - it / tries) * ((seed >> 12) % 100) / 100.0:
-            cur, path, order, q = t, p, o2, q2
+            cur, path, order, q, state = t, trail(i, st[1]), o2, q2, st
             if t < best[0]:
                 best = (t, o2, q2)
     back = {x: k for k, x in qn.items()}
@@ -732,8 +1024,10 @@ def rank_program(g, core, T, topo):
         return
     ops = build(g, core, T, topo)
     if "plan" not in CACHE:
-        CACHE["plan"] = polish(ops, PAR, refine(ops, PAR), PAR["tries"])
+        CACHE["plan"] = polish(ops, PAR, search(ops, PAR), PAR["tries"])
     order, deps = CACHE["plan"][:2]
+    loads = [i for i, o in enumerate(ops) if o["stage"] < 0 and o["sem"]]
+    order = loads + [i for i in order if i not in loads]
     for i, o in enumerate(ops):
         if o["q"] == "any":
             o["q"] = CACHE["plan"][3][i]

from concourse.mybir import AluOpType as A, ActivationFunctionType as F

NV, SH = 4, (1, 2, 4)
WS = (128, 128)
NP = len(WS)
WM = max(WS)
AT = [sum(WS[:_h]) for _h in range(NP)]
ND = 3
PLACE = {2: {"sh": ("m", 2), "cc": ("m", 2), "oh0": ("h", 1), "e0": ("h", 2), "oh1": ("m", 0), "e1": ("m", 1), "emp": ("h", 1), "oz": ("h", 2), "new": ("m", 0),
             "lz": ("m", 1), "U": ("h", 0), "u": ("h", 1), "zt": ("h", 3), "c2": ("m", 1), "c1": ("m", 2), "l1": ("m", 1),
             "a2": ("m", 0), "a1": ("h", 0)},
         3: {"sh": ("m", -1), "cc": ("m", -1), "oh0": ("h", 1), "e0": ("h", 3), "emp": ("h", 1), "oz": ("h", 2), "new": ("h", 4),
             "lz": ("h", 1), "U": ("h", 4), "u": ("h", 2), "zt": ("h", 1), "c2": ("h", 0), "c1": ("m", 3), "l1": ("m", -1),
             "a2": ("h", 4), "a1": ("m", 4)}}[NP]
NM = {2: 2, 3: 1}[NP]
BIG = 131072.0
FAR = 16777216.0
CB = 129.0
EX = (-1.0, -1.0, 1.75)
ROT = 712
f32, b16, h16, i32, u16 = "float32", "bfloat16", "float16", "int32", "uint16"

SCRATCH = {"X0": ("sbuf", [128, 4112], b16), "X1": ("sbuf", [128, 4112], b16), "rbs": ("sbuf", [128, 1024], i32),
           "inp": ("sbuf", [128, 768], i32), "thi": ("sbuf", [128, 256], i32), "thf": ("sbuf", [128, 256], f32),
           "th16": ("sbuf", [128, 8 * NP], f32), "rs": ("sbuf", [128, 128 * NP], f32), "cnt": ("sbuf", [128, 8 * NP], i32),
           "go": ("sbuf", [128, 8 * NP], b16),
           "ri": ("sbuf", [128, 8], i32), "col": ("sbuf", [128, 24], f32), "im": ("sbuf", [128, 128], f32),
           "mg": ("sbuf", [128, 128], f32), "mgE": ("sbuf", [128, 128], f32),
           "mgO": ("sbuf", [128, 128], f32), "tx": ("sbuf", [128, 8, 32], f32), "mk": ("sbuf", [128, 128], b16),
           "cz": ("sbuf", [128, 8], f32),
           "rstm": ("sbuf", [128, 128], f32), "rsth": ("sbuf", [128, 128], h16), "rst1": ("sbuf", [128, 1024], b16),
           "rows": ("sbuf", [128, 19, 128], b16),
           "one16": ("sbuf", [128, 128], b16), "I32": ("sbuf", [128, 8], f32), "blkD": ("sbuf", [128, 24], b16), "rst2": ("sbuf", [128, 1024], b16),
           "mb": ("sbuf", [128, 18, 128], b16), "mh": ("sbuf", [128, 9, 128], h16),
           "pq": ("psum", [128, 512], f32)}
for _h, _w in enumerate(WS):
    for _n, _sh, _d in (("tl", [128, NV, 6 * _w], h16), ("to", [128, 4 * _w], h16), ("tf", [128, 3 * _w], f32),
                        ("rec", [128, 16 * _w], b16), ("abd", [128, _w, 16], b16), ("top", [128, 16 * _w], b16), ("mx", [128, 16 * _w], b16),
                        ("ex", [128, 3, _w], b16), ("oz", [128, 128], b16),
                        ("pn", [128, 128], f32), ("bm", [128, 128], f32), ("pnh", [128, 128], h16), ("bmh", [128, 128], h16),
                        ("off", [128, _w], u16), ("wf", [128, 4, _w], f32), ("wi", [128, 4, _w], i32), ("vi", [128, 2 * _w], i32), ("sz", [128, 2 * _w], f32),
                        ("wh", [128, 4, _w], h16), ("wb", [128, 6, _w], b16),
                        ("ll", [128, 40], i32), ("su", [128, 24], u16), ("cst", [128, 16], i32)):
        SCRATCH[_n + str(_h)] = ("sbuf", _sh, _d)
    SCRATCH["ph%d" % _h] = ("psum", [128, 512], f32)
for _b in range(NM):
    SCRATCH["pm%d" % _b] = ("psum", [128, 512], f32)
for _b in range(ND):
    SCRATCH["pd%d" % _b] = ("psum", [128, 512], f32)

SEMAPHORES = ["pe", "dve", "act", "pool", "lx0", "lx1", "ll", "la", "lc", "lth", "lrb0", "lrb1"] + \
    ["cx%d" % _t for _t in range(NV)] + ["sx%d" % _h for _h in range(NP)] + ["sy%d%d" % (_h, _j) for _h in range(NP) for _j in range(3)] + \
    ["%s%d%d%d" % (_p, _t, _h, _j) for _p in ("ar", "sn") for _t in range(NV - 1) for _h in range(NP) for _j in range(2)]

PAR = {"g": 1.5, "cyc": 0.87, "pe": 0.52, "fix": 25.0, "hop": 220.0, "heat": 100.0, "tries": 0, "pen": 600.0, "per": 7500.0, "extra": 3000.0,
       "rounds": 2, "gc": (0, 32, 64, 96, 128), "sp": 1, "pu": 8, "period": 42000.0, "beat": 9500.0, "amp": 300.0, "search": ((6000, 1200.0), (3000, 300.0)),
       "dma": 1.0, "cases": ({"g": 1.3, "cyc": 0.84, "pe": 0.45, "hop": 200.0, "weight": 0.35}, {"g": 1.4, "pe": 0.7, "hop": 200.0, "weight": 0.3},
                             {"g": 1.9, "cyc": 1.05, "pe": 0.55, "hop": 280.0, "dma": 1.2, "weight": 0.22}),
       "force": {}, "two": 1, "mx": 0, "mc": 64, "kn": {128: ((64, 8), (64, 8)), 96: ((96, 4),), 64: ((64, 8),)}}
CACHE = {}


def build(g, core, T, topo):
    ops, stage = [], [-1]
    V, S, P = g.vector, g.scalar, g.tensor
    rank = T.rank_of(core)
    nxt = T.cores[(rank + 1) % len(T.cores)]
    rid, pid = topo.addr(nxt)[:2]
    eng = topo.engines(core, nxt)
    mask = sum(1 << e for e in eng)

    def bank(names):
        return sorted(set(n.split("_")[0] for n in names if n[0] == "p" and n[1] in "dhmq" and "_" in n))

    def op(q, calls, R, Wr, cyc, sem=None, inc=1, lat=0.0, after=None):
        ops.append({"q": q, "calls": calls, "R": list(R), "W": list(Wr), "cyc": cyc, "banks": bank(list(R) + list(Wr)), "sem": sem,
                    "inc": inc, "lat": lat, "after": after, "stage": stage[0]})
        return len(ops) - 1

    def tt(out, a, b, o, R, Wr, n, gat=False):
        op("dve", [lambda: V.tensor_tensor(out, a, b, o)], R, Wr, ("g", n) if gat else (n if bank(R) else 2 * n))

    def ts(out, a, s1, s2, o0, o1, R, Wr, n):
        if o1 is None:
            op("dve", [lambda: V.tensor_scalar(out, a, s1, None, o0)], R, Wr, n)
        else:
            op("dve", [lambda: V.tensor_scalar(out, a, s1, s2, o0, o1)], R, Wr, n)

    def cp(out, a, R, Wr, n):
        op("dve", [lambda: V.tensor_copy(out, a)], R, Wr, n)

    def scan(out, d0, d1, init, o0, o1, R, Wr, n):
        op("dve", [lambda: V.tensor_tensor_scan(out, d0, d1, init, o0, o1)], R, Wr, n)

    def either(dve, act, R, Wr, n):
        ops[op("any", None, R, Wr, n)]["alt"] = {"dve": [dve], "act": [act]}

    def pickup(out, a, R, Wr, n):
        either(lambda: V.tensor_copy(out, a), lambda: S.activation(out, a, F.Copy), R, Wr, ("g", n))

    def affine(out, a, scale, bias, R, Wr, n):
        either(lambda: V.tensor_scalar(out, a, scale, bias, A.mult, A.add), lambda: S.activation(out, a, F.Identity, bias=bias, scale=scale), R, Wr, n)

    def ms(out, c, Wr, n):
        op("dve", [lambda: V.memset(out, c)], [], Wr, n)

    def mm(terms, R, Wr, first=True, last=True, each=False):
        calls = []
        for j, (o, l, r, n) in enumerate(terms):
            st, sp = (j % each == 0, j % each == each - 1) if each else (first and j == 0, last and j == len(terms) - 1)
            calls.append(lambda o=o, l=l, r=r, st=st, sp=sp: P.matmul(o, l, r, st, sp))
        op("pe", calls, R, Wr, sum(x[3] for x in terms))

    def iota(out, pat, base, cm, Wr, n, flt=True):
        if flt:
            op("pool", [lambda: g.iota(out, pat, base, cm, allow_small_or_imprecise_dtypes=True)], [], Wr, 160 + 2 * n)
        else:
            op("pool", [lambda: g.iota(out, pat, base, cm)], [], Wr, 160 + 2 * n)

    def dma(q, out, a, R, Wr, sem, lat):
        e = {"sp": g.sync, "act": g.scalar}[q]
        op(q, [lambda: e.dma_start(out, a)], R, Wr, 60, sem=sem, inc=16, lat=lat)

    inp = T["inp"]
    dma("sp", inp[:, 0:256], T["lt"][:], [], ["inL"], "ll", 2000)
    dma("act", inp[:, 256:512], T["ag"][:], [], ["inA"], "la", 2000)
    for j in range(2):
        dma(("sp", "act")[j], T["X0"][:, 2048 * j:2048 * j + 2048], T["xs"][:, 2048 * j:2048 * j + 2048], [], ["Xl%d" % j], "lx%d" % j, 5000)
    dma("sp", inp[:, 512:768], T["cs"][:], [], ["inC"], "lc", 5500)
    dma("sp", T["thi"][0:8, :], T["th"][:], [], ["thi"], "lth", 5500)
    dma("sp", T["rbs"][:, ROT:1024], T["rb"][:, 0:1024 - ROT], [], ["rbs0"], "lrb0", 7000)
    dma("sp", T["rbs"][:, 0:ROT], T["rb"][:, 1024 - ROT:1024], [], ["rbs1"], "lrb1", 7000)
    for b in range(2):
        ms(T["X%d" % b][:, 4096:4112], 0.0, ["Xz%d" % b], 16)

    ri, col = T["ri"], T["col"]
    iota(T["im"][:], [[1, 128]], 0, -1, ["im"], 128)
    iota(ri[:, 0:1], [[0, 1]], 0, 1, ["ri0"], 1, False)
    iota(T["mg"][:], [[1, 8], [0, 16]], 0, 0, ["mg"], 128)
    iota(T["tx"][:], [[16, 8], [0, 2], [1, 16]], 0, -1, ["tx"], 256)
    iota(T["mk"][:], [[0, 8], [1, 16]], 1, 0, ["mk"], 128)
    iota(T["cz"][:], [[256, 8]], 0, 0, ["cz"], 8)
    iota(T["mgE"][:], [[1, 8], [0, 8], [100, 2]], 0, 0, ["mgE"], 128)
    iota(T["mgO"][:], [[1, 8], [0, 8], [-100, 2]], 100, 0, ["mgO"], 128)
    ts(ri[:, 1:2], ri[:, 0:1], 15, None, A.bitwise_and, None, ["ri0"], ["ri1"], 1)
    ts(ri[:, 2:3], ri[:, 0:1], 4, None, A.arith_shift_right, None, ["ri0"], ["ri2"], 1)
    ts(ri[:, 3:4], ri[:, 0:1], 1, None, A.bitwise_and, None, ["ri0"], ["ri3"], 1)
    C, M, RW = {}, {}, {}

    def column(name, src, m, a):
        C[name] = col[:, len(C):len(C) + 1]
        ts(C[name], ri[:, src:src + 1], m, a, A.mult, A.add, ["ri%d" % src], [name], 1)
    column("rg", 2, 1.0, 0.0)
    column("rk16", 1, 16.0, 0.0)
    column("rk1", 1, 1.0, 1.0)
    column("wq", 1, 2.0, 1.0)
    column("wq2", 1, 4096.0, 2048.0)
    column("gp", 0, 1048576.0, -1048576.0)
    column("cp", 0, 1.0, 0.0)
    column("np", 0, -6144.0, 6144.0)
    for si in range(3):
        column("up%d" % si, 0, -2 * BIG * si, 2 * BIG * si)
    column("ev", 3, -1.0, 1.0)
    used = {"mb": 0, "mh": 0}

    def matrix(name, buf, src, srcn, s1, s2, extra=()):
        M[name] = T[buf][:, used[buf], :]
        used[buf] += 1
        ts(M[name], src, s1, s2, A.is_equal, A.mult, [srcn] + list(extra), [name], 128)
    im, mg, tx = T["im"][:], T["mg"][:], T["tx"]
    for name, buf, c in (("Ih", "mh", 1.0), ("I2080", "mh", 2080.0), ("I", "mb", 1.0), ("n16h", "mh", -16.0)):
        matrix(name, buf, im, "im", 0.0, c)
    for name, c in (("nI", -1.0), ("BI", BIG), ("nBI", -BIG), ("I8k", 8192.0), ("nI2", -2.0)):
        M[name] = T["mb"][:, used["mb"], :]
        used["mb"] += 1
        affine(M[name], M["I"], c, 0.0, ["I"], [name], 128)
    matrix("nI12", "mb", im, "im", -1.0, 4096.0)
    matrix("nI23", "mb", im, "im", 0.0, 4096.0)
    tt(M["nI12"], M["nI12"], M["nI23"], A.subtract, ["nI12", "nI23"], ["nI12"], 128)
    ms(T["mb"][:, used["mb"] - 2, 1::2], 0.0, ["nI12"], 64)
    affine(M["nI23"], M["nI12"], 2048.0, 0.0, ["nI12"], ["nI23"], 128)
    for si in range(3):
        s = SH[si]
        matrix("Sh%d" % si, "mh", tx[:, :, s:s + 16], "tx", 0.0, 1.0)
        matrix("J%d" % si, "mb", tx[:, :, 16 - s:32 - s], "tx", 0.0, 8192.0)
    for e, si in ((0, 1), (0, 2), (1, 2)):
        nm, d = "pen%d%d" % (e, si), SH[si] - SH[e]
        matrix(nm, "mb", tx[:, :, d:d + 16], "tx", 0.0, 8192.0)
        tt(M[nm], M[nm], M["J%d" % e], A.add, [nm, "J%d" % e], [nm], 128)
        ts(M[nm], M[nm], BIG / 8192, None, A.mult, None, [nm], [nm], 64)
    matrix("blk", "mh", mg, "mg", C["rg"], 1.0, ["rg"])
    matrix("odd", "mh", T["mgO"][:], "mgO", C["rg"], 1.0, ["rg"])
    matrix("WqE", "mb", T["mgE"][:], "mgE", C["rg"], C["wq"], ["rg", "wq"])
    matrix("WqE2", "mb", T["mgE"][:], "mgE", C["rg"], C["wq2"], ["rg", "wq2"])
    for j, c in enumerate((16.0, -16.0, 32.0)):
        ts(T["blkD"][:, 8 * j:8 * j + 8], T["mg"][:, ::16], C["rg"], c, A.is_equal, A.mult, ["mg", "rg"], ["blkD"], 8)
    ms(T["rst2"][:], 1.0, ["rst2"], 512)
    ms(T["rst2"][:, ::2], 0.0, ["rst2"], 256)
    ts(T["I32"][:], T["im"][:, 0:8], 0.0, 16.0, A.is_equal, A.mult, ["im"], ["I32"], 8)
    matrix("Wq", "mb", mg, "mg", C["rg"], C["wq"], ["rg", "wq"])
    M["else"] = T["mb"][:, used["mb"], :]
    ts(M["else"], T["mk"][:], C["rk1"], BIG, A.not_equal, A.mult, ["mk", "rk1"], ["else"], 64)
    ms(T["rstm"][:], -FAR, ["rstm"], 128)
    ms(T["rstm"][:, ::16], FAR, ["rstm"], 8)
    ms(T["rsth"][:], -30000.0, ["rsth"], 64)
    ms(T["rsth"][:, ::16], 30000.0, ["rsth"], 8)
    ms(T["rst1"][:], 1.0, ["rst1"], 512)
    ms(T["rst1"][:, ::16], 0.0, ["rst1"], 64)
    ms(T["one16"][:], 16.0, ["one16"], 64)
    rows = T["rows"]
    ms(rows[0:2, 0, :], 1.0, ["r1"], 64)
    for name, val in (("r3232", 3232.0), ("rBIG", BIG), ("r8192", 8192.0), ("r10240", 10240.0), ("rnCB", -CB),
                      ("rodd", 0.0)) + tuple(("rev%d" % t, 0.0) for t in range(1, NV)):
        j = len(RW) + 1
        RW[name] = rows[0:1, j, :]
        affine(RW[name], rows[0:1, 0, :], val, 0.0, ["r1"], [name], 128)
        if name == "rodd":
            ms(rows[0:1, j, 1::2], 2048.0, [name], 64)
        if name[:3] == "rev":
            ms(rows[0:1, j, 0::2], 32.0 * int(name[3]), [name], 64)
    RW["rgo"] = rows[0:2, 14, :]
    ts(RW["rgo"], T["mg"][0:2, :], col[0:2, 5:6], None, A.mult, None, ["mg", "gp"], ["rgo"], 128)
    ts(rows[0:2, 13, :], T["mk"][0:2, :], -1.0, col[0:2, 6:7], A.add, A.mult, ["mk", "cp"], ["rtmp"], 128)
    tt(RW["rgo"], RW["rgo"], rows[0:2, 13, :], A.add, ["rgo", "rtmp"], ["rgo"], 128)
    for si in range(3):
        RW["rgo%d" % si] = rows[0:2, 16 + si, :]
        ts(RW["rgo%d" % si], RW["rgo"], col[0:2, 8 + si:9 + si], None, A.add, None, ["rgo", "up%d" % si], ["rgo%d" % si], 64)
    RW["rk"] = rows[0:2, 15, :]
    ts(RW["rk"], T["mk"][0:2, :], col[0:2, 6:7], col[0:2, 7:8], A.mult, A.add, ["mk", "cp", "np"], ["rk"], 128)

    def place_(h, name, n=1, lo=0, hi=None):
        W = WS[h]
        b, j = PLACE[name]
        j = h if j < 0 else j
        bn, c = ("ph%d" % h, 128 + W * (j - 1) if j else 0) if b == "h" else ("pm%d" % (h % NM), WM * j)
        lo, hi = c + lo, c + (n * W if hi is None else hi)
        return T[bn][:, lo:hi], ["%s_%d" % (bn, x) for x in range(lo // 64, (hi + 63) // 64)]

    def halves(W):
        return ((0, W // 2), (W // 2, W)) if PAR["sp"] else ((0, W),)

    def both(name):
        return [name + str(j) for j in range(2 if PAR["sp"] else 1)]

    def const(out, name, W):
        return (out, RW[name], rows[0:1, 0, 0:W], max(W, 64))

    pq, rs = T["pq"], T["rs"]
    cp(T["thf"][0:8, :], T["thi"][0:8, :], ["thi"], ["thf"], 256)
    ms(T["th16"][:], 0.0, ["th16"], 8 * NP)
    ms(T["go"][:], 0.0, ["go%d" % h for h in range(NP)], 8 * NP)
    for h in range(NP):
        H, W, x = str(h), WS[h], AT[h]
        o = T["ph" + H][0:W, 0:8]
        mm([(o, T["thf"][0:8, x:x + W], T["I32"][0:8, :], 256), (o, rows[0:1, 0, 0:W], rows[0:1, 14, ::16], 64)], ["thf", "I32", "r1", "rgo"],
           ["ph%s_0" % H])
        ts(T["th16"][0:W, 8 * h:8 * h + 8], o, -0.5, None, A.add, None, ["ph%s_0" % H], ["th16"], 8)
        tl = T["tl" + H]
        ms(tl[:, 0, 2 * W:4 * W:2], 0.0, ["zero" + H], W)
        ms(T["to" + H][:, 2 * W:4 * W:2], 0.0, ["zto" + H], W)
        ms(T["sz" + H][:, 0::2], 0.0, ["zsz" + H], W)
        ts(tl[:, 0, 0:W], inp[:, x:x + W], -2048.0, None, A.add, None, ["inL"], ["L0" + H], W)
        ts(tl[:, 0, 2 * W + 1:4 * W:2], inp[:, 256 + x:256 + x + W], -2048.0, None, A.add, None, ["inA"], both("a0" + H), W)
        ts(tl[:, 0, W:2 * W], inp[:, 512 + x:512 + x + W], CB, None, A.add, None, ["inC"], ["C0" + H], W)
        ts(T["cst" + H][:, 0:W // 16], T["cz"][:, 0:W // 16], C["rk16"], None, A.add, None, ["cz", "rk16"], ["cst" + H], 8)
        ms(T["cst" + H][:, W // 16:W // 8], 592, ["cst" + H], 8)
    ms(rs[:], FAR, ["thr"], 128 * NP)
    cp(rs[0:WM, ::16], T["th16"][0:WM, :], ["th16"], ["thr"], 8 * NP)
    ms(T["cnt"][:], 0, ["cnt"], 16)

    def state(t, h):
        tl, W = T["tl%d" % h], WS[h]
        return tl[:, t, 0:W], tl[:, t, 2 * W + 1:4 * W:2], tl[:, t, W:2 * W], "L%d%d" % (t, h), both("a%d%d" % (t, h)), "C%d%d" % (t, h)

    def half(t, h, lo, hi):
        return T["tl%d" % h][:, t, 2 * WS[h] + 1 + 2 * lo:2 * WS[h] + 2 * hi:2]

    def index(t, h, final):
        H, W = str(h), WS[h]
        L, a, Cc, ln, an, cn = state(t, h)
        for j, (lo, hi) in enumerate(halves(W)):
            v, J = T["wi" + H][:, 0, lo:hi], H + str(j)
            scan(T["vi" + H][:, 2 * lo:2 * hi], T["tl" + H][:, t, 2 * W + 2 * lo:2 * W + 2 * hi], pq[:, 2 * (AT[h] + lo):2 * (AT[h] + hi)], 0.0, A.mult, A.add,
                 ["pq_L" + H, an[j], "zero" + H], ["vi" + J], 2 * (hi - lo))
            ts(v, T["vi" + H][:, 2 * lo + 1:2 * hi:2], 5, 4095, A.arith_shift_right, A.bitwise_and, ["vi" + J], ["v" + J], hi - lo)
            if not final:
                cp(T["off" + H][:, lo:hi], v, ["v" + J], ["off" + J], hi - lo)
        if final:
            (x1, k1), v, ix = place_(h, "emp"), T["wi" + H][:, 0, :], T["tl" + H][:, t, 4 * W + 1:6 * W:2]
            tt(ix, x1, v, A.add, k1 + both("v" + H), ["ix" + H], W)
            ts(T["off" + H][:], ix, 2048.0, 4096.0, A.add, A.min, ["ix" + H], both("off" + H), W // 2)

    def xnames(t):
        return ["Xz%d" % (t % 2)] + (["Xl0", "Xl1"] if t == 0 else []) + ["X%d%d" % (t % 2, h) for h in range(NP)]

    def recs(h, lo, hi):
        return ["rec%d%d" % (h, c) for c in range(lo // 16, hi // 16)]

    def gather(t, h, lo, hi):
        H = str(h)
        cuts = [c for c in PAR["gc"] if lo <= c <= hi]
        for c, e in zip(cuts, cuts[1:]):
            pickup(T["rec" + H][:, 16 * c:16 * e], T["X%d" % (t % 2)][:, 0:4112].indirect(T["off" + H][:, c:e]),
                   xnames(t) + ["off%s%d" % (H, j) for j, (x, y) in enumerate(halves(WS[h])) if x < e and c < y], recs(h, c, e), 16 * (e - c))

    turn = [0]

    def step(t, h, si):
        H, s, W = str(h), SH[si], WS[h]
        L, a, Cc, ln, an, cn = state(t, h)
        bank_ = T["ph" + H]
        key, k0, kall = bank_[0:W, 0:128], ["ph%s_0" % H, "ph%s_1" % H], ["ph%s_%d" % (H, j) for j in range(8)]
        (x1, k1), (m0, n0) = place_(h, "cc"), place_(h, "sh")
        index(t, h, False)
        eqk, wh = T["wb" + H][:, 0, :], T["wh" + H]
        mm([(m0, M["Sh%d" % si], a, W)], ["Sh%d" % si] + an, n0)
        tt(eqk, m0, a, A.is_equal, n0 + an, ["eqk" + H], W)
        tt(wh[:, 0, :], m0, a, A.max, n0 + an, ["hi" + H], W)
        tt(wh[:, 1, :], m0, a, A.min, n0 + an, ["lo" + H], W)
        terms, R = [(key, rows[0:2, 0, 0:W], RW["rgo%d" % si], 128)], ["eqk" + H, "BI", "r1", "rgo%d" % si]
        for e in range(si):
            terms.append((key, T["ex" + H][:, e, :], M["pen%d%d" % (e, si)], 128))
            R += both("ex%d%d" % (e, h)) + ["pen%d%d" % (e, si)]
        mm(terms + [(key, eqk, M["BI"], 128)], R, kall, last=False)
        rec, abd = T["rec" + H], T["abd" + H]
        lo = 0
        if s == 1 and PAR["mx"]:
            gather(t, h, 0, W)
            mx, ks = (T["top" + H], T["mx" + H]), range(0, 15, 3 - PAR["mx"])
            names = [["%s%s%d" % (x, H, c) for c in range(0, W, PAR["mc"])] for x in ("top", "mx")]
            for j, c in enumerate(range(0, W, PAR["mc"])):
                for d in range(PAR["mx"]):
                    x, y = 16 * c + d, 16 * (c + PAR["mc"])
                    scan(mx[d][:, x:y], T["rst2"][:, 0:y - x], rec[:, x:y], 0.0, A.mult, A.max, ["rst2"] + recs(h, c, c + PAR["mc"]), [names[d][j]], (y - x) // 2)
            rest = [k for k in range(16) if k not in ks]
            for j in range(0, len(rest), 4):
                b, some = turn[0] % ND, rest[j:j + 4]
                turn[0] += 1
                pd, m = T["pd%d" % b], len(some)
                mm([(pd[:, i:W * m:m], M[sign], rec[:, (k + d) & 15::16], W) for i, k in enumerate(some) for sign, d in (("I", 0), ("nI", s))],
                   ["I", "nI"] + recs(h, 0, W), ["pd%d_0" % b], each=2)
                o, i_ = abd[:, :, some[0]:some[-1] + 1:2], pd[:, 0:W * m]
                an_ = ["abd%s%d_%d" % (H, x, k) for k in some for x in range(2)]
                op("act", [lambda o=o, i_=i_: S.activation(o, i_, F.Abs)], ["pd%d_0" % b], an_, W * m)
                mm([(bank_[0:W, k:128:16], abd[:, :, k], T["blkD"][:, 0:8], 64) for k in some], ["blkD"] + an_, kall, first=False, last=False)
            for j in range(0, len(ks), 4):
                mm([(bank_[0:W, k:128:16], rec[:, k + d::16], T["blkD"][:, 8:16], 64) for k in ks[j:j + 4] for d in (0, 1)], ["blkD"] + recs(h, 0, W), kall,
                   first=False, last=False)
            for d in range(PAR["mx"]):
                mm([(bank_[0:W, k:128:16], mx[d][:, k + 1::16], T["blkD"][:, 16:24], 64) for k in ks if k % 2 == d], ["blkD"] + names[d], kall,
                   first=False, last=d == PAR["mx"] - 1)
        for q, (w, n) in enumerate(() if s == 1 and PAR["mx"] else PAR["kn"][W]):
            hi = lo + w
            gather(t, h, lo, hi)
            for j in range(0, 16, n):
                b, e = turn[0] % ND, min(16, j + n)
                turn[0] += 1
                pd, o, i_ = T["pd%d" % b], abd[:, lo:hi, j:e], T["pd%d" % b][:, 0:w * (e - j)]
                for x in range(j, e, PAR["pu"]):
                    mm([(pd[:, k - j:w * (e - j):e - j], M[sign], rec[:, 16 * lo + ((k + d) & 15):16 * hi:16], max(w, 64))
                        for k in range(x, min(e, x + PAR["pu"])) for sign, d in (("I", 0), ("nI", s))], ["I", "nI"] + recs(h, lo, hi), ["pd%d_0" % b], each=2)
                op("act", [lambda o=o, i_=i_: S.activation(o, i_, F.Abs)], ["pd%d_0" % b], ["abd%s%d_%d" % (H, q, k) for k in range(j, e)], w * (e - j))
                if hi == W:
                    mm([(bank_[0:W, k:128:16], abd[:, :, k], T["blkD"][:, 0:8], 64) for k in range(j, e)],
                       ["blkD"] + ["abd%s%d_%d" % (H, x, k) for k in range(j, e) for x in range(q + 1)], kall, first=False, last=e == 16)
            lo = hi
        pn, bm, ou, on = T["pn" + H], T["bm" + H], T["oz" + H][0:W, :], "oz" + H
        scan(pn[0:W, :], rs[0:W, 128 * h:128 * h + 128], key, FAR, A.min, A.min, ["thr"] + k0, ["least" + H], 128)
        scan(bm[0:W, ::-1], T["rstm"][0:W, :], pn[0:W, ::-1], 0.0, A.max, A.min, ["rstm", "least" + H], ["bm" + H], 128)
        tt(ou, key, bm[0:W, :], A.is_equal, k0 + ["bm" + H], [on], 128)
        if (t, si) != (NV - 1, 2):
            tt(T["go"][0:W, 8 * h:8 * h + 8], pn[0:W, 15::16], rs[0:W, 128 * h:128 * h + 128:16], A.is_lt, ["least" + H, "thr"], ["go" + H], 8)
        for j, (lo, hi) in enumerate(halves(W)):
            w, J, aj = hi - lo, H + str(j), half(t, h, lo, hi)
            x2, k2 = place_(h, "oh%d" % j, 1, 0, w)
            (m1, n1), (m2, n2) = place_(h, "e%d" % j, 1, 0, w), place_(h, "e%d" % j, 1, w, 2 * w)
            tb, ex = T["wb" + H][:, 5, lo:hi], T["ex" + H][:, si, lo:hi]
            mm([(x2, ou, T["mb"][0:W, 0, lo:hi], w)], [on, "I"], k2)
            tt(wh[:, 2, lo:hi], x2, wh[:, 0, lo:hi], A.mult, k2 + ["hi" + H], ["wa" + J], w)
            tt(wh[:, 3, lo:hi], x2, wh[:, 1, lo:hi], A.mult, k2 + ["lo" + H], ["wi" + J], w)
            mm([(m1, M["blk"], wh[:, 2, lo:hi], w)], ["blk", "wa" + J], n1)
            tt(tb, m1, aj, A.not_equal, n1 + [an[j]], ["tb" + J], w)
            mm([(m2, M["blk"], wh[:, 3, lo:hi], w), (m2, M["I8k"], tb, w)], ["blk", "wi" + J, "I8k", "tb" + J], n2)
            tt(aj, m2, aj, A.min, n2 + [an[j]], [an[j]], w)
            affine(ex, x2, 1.0, EX[si], k2, ["ex%d%s" % (si, J)], w)
        if si < 2:
            mm([(x1, M["Sh%d" % si], Cc, W), (x1, M["nBI"], T["ex" + H][:, si, :], W)], ["Sh%d" % si, cn, "nBI"] + both("ex%d%d" % (si, h)), k1)
        else:
            mm([(x1, M["Sh%d" % si], Cc, W), const(x1, "rBIG", W), (x1, ou, T["mb"][0:W, 3, 0:W], W)], ["Sh%d" % si, cn, "r1", "rBIG", on, "nBI"], k1)
        tt(Cc, x1, Cc, A.min, k1 + [cn], [cn], W)

    def count():
        go, o, n, p0, W = T["go"], T["one16"][0:WM, 0:WM], 8 * NP, T["pm0"], WM
        terms = [(p0[0:W, 480:480 + n], o, go[0:W, :], 64)]
        for r in range(8, n, 8):
            terms += [(p0[0:W, 480:480 + n - r], o, go[0:W, r:n], 64), (p0[0:W, 480 + n - r:480 + n], o, go[0:W, 0:r], 64)]
        mm(terms, ["one16"] + ["go%d" % h for h in range(NP)], ["pm0_n"])
        cnt = T["cnt"][0:W, :]
        tt(cnt, p0[0:W, 480:480 + n], cnt, A.add, ["pm0_n", "cnt"], ["cnt"], n)
        ts(cnt, cnt, 511, None, A.bitwise_and, None, ["cnt"], ["cnt"], n)
        tt(rs[0:W, ::16], T["th16"][0:W, :], cnt, A.add, ["th16", "cnt"], ["thr"], n)

    def refill(t, h):
        H, last, W = str(h), t == NV - 1, WS[h]
        NL = W // 16
        L, a, Cc, ln, an, cn = state(t, h)
        key, k0 = T["ph" + H][0:W, 0:128], ["ph%s_0" % H, "ph%s_1" % H]
        (x1, k1), (x2, k2), (m0, n0) = place_(h, "emp"), place_(h, "oz"), place_(h, "new")
        zp, kz = place_(h, "lz")
        eye = {"I": T["mb"][0:W, 0, 0:W], "I8k": T["mb"][0:W, 4, 0:W], "Ih": T["mh"][0:W, 0, 0:W]}
        ex, J, en = [T["ex" + H][:, e, :] for e in range(3)], [M["J%d" % e] for e in range(3)], ["J0", "J1", "J2"]
        for e in range(3):
            en += both("ex%d%d" % (e, h))
        off = 0.0 if last else 2048.0
        ll, su, tl = T["ll" + H], T["su" + H], T["tl" + H]
        nb, z, y, ck = [T["wb" + H][:, j, :] for j in range(1, 5)]
        oz, pn, bm, wh = T["oz" + H][0:W, :], T["pnh" + H], T["bmh" + H], T["wh" + H]
        mm([(x1, J[e], ex[e], W) for e in range(3)], en, k1)
        index(t, h, True)
        gather(t, h, 0, W)
        mm([(key, Cc, M["n16h"], 128), (key, rows[0:2, 0, 0:W], RW["rk"], 128)] + [(key, ex[e], J[e], 128) for e in range(3)],
           [cn, "n16h", "r1", "rk"] + en, k0)
        scan(pn[0:W, :], T["rsth"][0:W, :], key, 0.0, A.max, A.min, ["rsth"] + k0, ["leasth" + H], 128)
        scan(bm[0:W, ::-1], T["rsth"][0:W, :], pn[0:W, ::-1], 0.0, A.max, A.min, ["rsth", "leasth" + H], ["bmh" + H], 64)
        tt(oz, key, bm[0:W, :], A.is_equal, k0 + ["bmh" + H], ["oz" + H], 128)
        mm([(x2, oz, eye["I"], W)], ["oz" + H, "I"], k2)
        tt(wh[:, 3, :], x2, tl[:, t, 4 * W + 1:6 * W:2], A.mult, k2 + ["ix" + H], both("wi" + H), W)
        tt(wh[:, 2, :], x2, a, A.mult, k2 + an, both("wa" + H), W)
        zs, us = T["wf" + H][:, 0, :], T["wi" + H][:, 0, :]
        mm([(zp, M["I"], M["else"][:, 0:W], W), (zp, M["blk"], wh[:, 3, :], W)], ["I", "else", "blk"] + both("wi" + H), kz)
        scan(zs, T["rstm"][:, 0:W], zp, 0.0, A.max, A.min, ["rstm"] + kz, ["zs" + H], W)
        ts(su[:, 0:NL], zs[:, 15::16], 2048.0, None, A.add, None, ["zs" + H], ["zo" + H], 8)
        pickup(z, T["X%d" % (t % 2)][:, 0:4112].indirect(su[:, 0:NL]), xnames(t) + ["zo" + H], ["z" + H], W)
        mm([(m0, J[e], ex[e], W) for e in range(3)] + [(m0, oz, eye["I8k"], W)], ["oz" + H, "I8k"] + en, n0)
        affine(nb, m0, -(8192.0 + off) / 8192, 8192.0 - (8192.0 + off) / 4, n0, ["nb" + H], W)
        mm([(zp, M["I"], M["else"][:, 0:W], W), (zp, M["Wq"], z, W)], ["I", "else", "Wq", "z" + H], kz)
        ui, nn = us[:, 15::16], ll[:, 24 + NL:24 + 2 * NL]
        scan(us, T["rstm"][:, 0:W], zp, 0.0, A.max, A.min, ["rstm"] + kz, both("v" + H), W)
        ts(ll[:, 8 + NL:8 + 2 * NL], ui, 4095, None, A.bitwise_and, None, both("v" + H), ["u12" + H], 8)
        ts(ll[:, 8:8 + NL], ui, 15, None, A.bitwise_and, None, both("v" + H), ["u4" + H], 8)
        tt(ll[:, 24:24 + 2 * NL], ll[:, 8:8 + 2 * NL], T["cst" + H][:, 0:2 * NL], A.add, ["u4" + H, "u12" + H, "cst" + H], ["sl" + H], 16)
        tt(nn, nn, nn, A.mult, ["sl" + H], ["sl" + H], 8)
        ts(nn, nn, 5, 1023, A.arith_shift_right, A.bitwise_and, ["sl" + H], ["sl" + H], 8)
        cp(su[:, 8:8 + 2 * NL], ll[:, 24:24 + 2 * NL], ["sl" + H], ["su" + H], 16)
        (pU, kU), (zt, kt), (c2, kc2), (c1, kc1), (l1, kl1), (a2, ka2), (a1, ka1) = [place_(h, x) for x in ("U", "zt", "c2", "c1", "l1", "a2", "a1")]
        uv, ku = place_(h, "u", 2)
        pu, pv = uv[:, 0::2], uv[:, 1::2]
        mm([(pU, M["WqE"], z, W)], ["WqE", "z" + H], kU)
        affine(y, pU, 1.0 / 4096, CB - 0.5 + 1.0 / 8192, kU, ["y" + H], W)
        mm([(pu, M["WqE"], z, W), (pu, M["nI12"], y, W)], ["WqE", "z" + H, "nI12", "y" + H], ku)
        mm(([] if last else [(pv, M["WqE2"], z, W), (pv, M["nI23"], y, W)]) + ([const(pv, "rev%d" % t, W)] if t else []),
           ["WqE2", "z" + H, "nI23", "y" + H, "r1", "rev%d" % t], ku)
        rec, top = T["rec" + H], T["top" + H]
        for c in range(0, W, 64):
            e = min(W, c + 64)
            scan(top[:, 16 * c:16 * e], T["rst1"][:, 0:16 * (e - c)], rec[:, 16 * c:16 * e], 0.0, A.mult, A.max,
                 ["rst1"] + recs(h, c, e), ["top%s%d" % (H, c)], 8 * (e - c))
        mm([(zt, M["I"], z, W), (zt, M["I"], top[:, 15::16], W)], ["I", "z" + H] + ["top%s%d" % (H, c) for c in range(0, W, 64)], kt)
        zti, ae, ci = [T["wi" + H][:, j, :] for j in range(1, 4)]
        ts(zti, zt, 0.5, -0.25, A.mult, A.add, kt, ["zti" + H], W)
        dst, dn = T["X%d" % ((t + 1) % 2)], "X%d%d" % ((t + 1) % 2, h)
        win = dst[:, 16 * AT[h]:16 * (AT[h] + W)]
        op("dve", [lambda: V.tensor_copy(win.indirect(su[:, 8:8 + NL]), zti)], ["zti" + H, "su" + H, dn], [dn], ("s", W))
        if last:
            dma("sp", T["yx"][:, 16 * AT[h]:16 * (AT[h] + W)], win, [dn], [], "sx" + H, 2000 + 12 * W)
        keep = "r10240" if last else "r8192"
        sL, sA = T["sz" + H][:, 1::2], T["wf" + H][:, 2, :]
        to = T[("tf" if last else "to") + H]
        oL, oC, oA = to[:, 0:W], to[:, W:2 * W], to[:, 2 * W:3 * W] if last else to[:, 2 * W + 1:4 * W:2]
        o = ["%s%d%d" % ("f" if last else "o", h, j) for j in range(3)]
        mm([(c2, bm[0:W, :], eye["Ih"], W), (c2, M["nI2"], nb, W)], ["bmh" + H, "Ih", "nI2", "nb" + H], kc2)
        mm([(c1, M["Ih"], Cc, W), (c1, M["nI"], nb, W), const(c1, "r8192", W)] + ([const(c1, "rnCB", W)] if last else []),
           ["Ih", cn, "nI", "nb" + H, "r1", "r8192", "rnCB"], kc1)
        if last:
            ck = ci
            ts(ck, c2, -1.0 / 32, 64 - 0.484375, A.mult, A.add, kc2, ["ck" + H], W)
        else:
            affine(ck, c2, -1.0 / 32, CB + 64 + off / 16 - 0.484375, kc2, ["ck" + H], W)
        tt(oC, c1, ck, A.min, kc1 + ["ck" + H], [o[1]], W)
        tt(sL, T["rbs"][:, 0:1024].indirect(su[:, 8 + NL:8 + 2 * NL]), nb, A.add, ["rbs0", "rbs1", "su" + H, "nb" + H], ["sL" + H], W, True)
        mm([(l1, M["Ih"], L, W), (l1, M["nI"], nb, W), const(l1, keep, W)], ["Ih", ln, "nI", "nb" + H, "r1", keep], kl1)
        tt(oL, l1, sL, A.min, kl1 + ["sL" + H], [o[0]], W)
        mm([(a2, M["odd"], wh[:, 2, :], W), (a2, M["I"], nb, W), const(a2, "rodd", W)], ["odd", "I", "nb" + H, "r1", "rodd"] + both("wa" + H), ka2)
        mm([(a1, M["Ih"], a, W), (a1, M["nI"], nb, W), const(a1, keep, W)], ["Ih", "nI", "nb" + H, "r1", keep] + an, ka1)
        scan(T["vi" + H][:], T["sz" + H][:], uv, 0.0, A.mult, A.add, ku + ["sL" + H, "zsz" + H], both("vi" + H), 2 * W)
        ts(ae, T["vi" + H][:, 1::2], 5, 4095, A.arith_shift_right, A.bitwise_and, both("vi" + H), ["ae" + H], W)
        tt(sA, a2, ae, A.add, ka2 + ["ae" + H], ["sA" + H], W)
        tt(oA, a1, sA, A.min, ka1 + ["sA" + H], [o[2]], W)
        if last:
            for j, yn in enumerate(("yl", "yc", "ya")):
                dma("sp", T[yn][:, AT[h]:AT[h] + W], to[:, W * j:W * j + W], [o[j]], [], "sy%d%d" % (h, j), 2500)
            return
        for j, (lo, hi, R, names) in enumerate(((0, 2 * W, o[:2], "LC"), (2 * W, 4 * W, [o[2], "zto" + H], "a")) if PAR["two"] else
                                               ((0, 4 * W, o + ["zto" + H], "LaC"),)):
            land, src, ar, sn = tl[:, t + 1, lo:hi], to[:, lo:hi], "ar%d%d%d" % (t, h, j), "sn%d%d%d" % (t, h, j)
            snd = op("pool", [lambda land=land, src=src, ar=ar, sn=sn: g.remote_dma(land, src, T.sem[ar], T.sem[sn], pid, rid, mask)], R, [], 1000,
                     sem=sn, inc=-len(eng), lat=2000)
            op(None, [], [], ["%s%d%d" % (x, t + 1, h) for x in names if x != "a"] + (both("a%d%d" % (t + 1, h)) if "a" in names else []), 0,
               sem=ar, inc=-len(eng), lat=200, after=snd)

    for t in range(NV):
        for si in range(4):
            if si == 1:
                dma("sp", T["X%d" % ((t + 1) % 2)][:, 0:4096], T["X%d" % (t % 2)][:, 0:4096], xnames(t)[1:],
                    ["X%d%d" % ((t + 1) % 2, h) for h in range(NP)], "cx%d" % t, 6000)
                ops[-1]["after"] = max(i for i, o in enumerate(ops) if o["W"][:1] == ["off%d0" % (NP - 1)])
            for h in range(NP):
                stage[0] = 4 * NP * t + NP * si + h
                if si == 0:
                    L, ln, W = state(t, h)[0], state(t, h)[3], WS[h]
                    lp, qp = pq[:, 2 * AT[h]:2 * (AT[h] + W):2], pq[:, 2 * AT[h] + 1:2 * (AT[h] + W):2]
                    mm([(lp, M["Ih"], L, W), const(lp, "r3232", W)], ["Ih", ln, "r1", "r3232"], ["pq_L%d" % h])
                    mm([(qp, M["I2080"], L, W)], ["I2080", ln], ["pq_L%d" % h])
                if si < 3:
                    step(t, h, si)
                else:
                    refill(t, h)
            if si < 3 and (t, si) != (NV - 1, 2):
                count()
    return ops


def cost(o, par):
    c = o["cyc"]
    if o["q"] is None:
        return 0.0
    if o["q"] == "pe":
        return c * par["pe"] + par["fix"]
    if isinstance(c, tuple):
        c = 60 + c[1] * (par["g"] if c[0] == "g" else 2.4 * par["g"])
    return max(c, 64) * par["cyc"] + par["fix"]


def edges(ops):
    writer, readers, deps = {}, {}, []
    for i, o in enumerate(ops):
        d = set()
        for r in o["R"]:
            if r in writer:
                d.add(writer[r])
        for w in o["W"]:
            if w in writer:
                d.add(writer[w])
            d.update(readers.get(w, ()))
        if o["after"] is not None:
            d.add(o["after"])
        d.discard(i)
        deps.append(d)
        for r in o["R"]:
            readers.setdefault(r, []).append(i)
        for w in o["W"]:
            writer[w] = i
            readers[w] = []
    return deps


def length(ops, par, plan):
    free, end = {}, [0.0] * len(ops)
    for i in plan[0]:
        q = plan[3][i]
        st = max([free.get(q, 0.0) if q else 0.0] + [end[d] + (0.0 if q == "pe" == ops[d]["q"] else par["hop"]) for d in plan[1][i]])
        free[q] = st + cost(ops[i], par)
        end[i] = free[q] + ops[i]["lat"]
    return max(end)


def place(ops, par, dur, pre, delay, rank, qs):
    n = len(ops)
    left = [len(p) for p in pre]
    post = [[] for _ in range(n)]
    for i in range(n):
        for d in pre[i]:
            post[d].append(i)
    ready = sorted((rank[i], i) for i in range(n) if left[i] == 0)
    line, used, st, out = {}, {}, [0.0] * n, list(qs)
    hop = par["hop"]
    while ready:
        i = ready.pop(0)[1]
        o = ops[i]
        r = max([0.0] + [st[d] + dur[d] + delay(d, i) for d in pre[i]])
        best = None
        for me in (("dve", "act") if qs[i] == "any" else (qs[i],)):
            t = r
            moved = me is not None
            while moved:
                moved = False
                for a, b in reversed(line.get(me, ())):
                    if b <= t:
                        break
                    if a < t + dur[i]:
                        t, moved = b, True
                        break
                for bk in o["banks"]:
                    for a, b, q in used.get(bk, ())[-40:]:
                        if q != me and a - hop < t + dur[i] and b + hop > t:
                            t, moved = b + hop, True
            sc = t + (par["pen"] if me == "dve" else 0.0)
            if best is None or sc < best[0]:
                best = (sc, t, me)
        t, me = best[1:]
        st[i], out[i] = t, me
        if me:
            ln = line.setdefault(me, [])
            k = len(ln)
            while k and ln[k - 1][0] > t:
                k -= 1
            ln.insert(k, (t, t + dur[i]))
        for bk in o["banks"]:
            u = used.setdefault(bk, [])
            u.append((t, t + dur[i], me))
            u.sort()
        for j in post[i]:
            left[j] -= 1
            if left[j] == 0:
                ready.append((rank[j], j))
        ready.sort()
    return st, out


def refine(ops, par):
    n = len(ops)
    dur = [cost(o, par) for o in ops]
    deps = edges(ops)
    succ = [[] for _ in range(n)]
    for i in range(n):
        for d in deps[i]:
            succ[d].append(i)
    qs = [o["q"] for o in ops]

    def fwd(d, i):
        return ops[d]["lat"] + (0.0 if qs[d] == "pe" == qs[i] else par["hop"])
    per, extra = par["per"], par["extra"]
    late = [1e12] * n
    for i in range(n - 1, -1, -1):
        s = ops[i]["stage"]
        if ops[i]["W"] and ops[i]["W"][0][:3] == "off":
            late[i] = min(late[i], s * per / NP + s // (4 * NP) * extra)
        if late[i] == 1e12:
            late[i] = NV * (4 * per + extra) + s % NP * per / NP
        for d in deps[i]:
            late[d] = min(late[d], late[i] - dur[d] - fwd(d, i))
    seen = {}
    for i in range(n):
        if qs[i] == "any":
            key = ("s" if ops[i]["stage"] % (4 * NP) < 3 * NP else "r") + ops[i]["W"][0][:2]
            k = seen[key, ops[i]["stage"]] = seen.get((key, ops[i]["stage"]), -1) + 1
            qs[i] = {"A": "act", "D": "dve"}.get((par["force"].get(key, "") + "-" * 9)[k], "any")
    st, out = place(ops, par, dur, deps, fwd, late, qs)
    best = None
    for _ in range(par["rounds"]):
        order = sorted(range(n), key=lambda i: (st[i], i))
        full, users = [set(d) for d in deps], {}
        for i in order:
            for b in ops[i]["banks"]:
                u = users.setdefault(b, {})
                full[i].update(j for q, j in u.items() if q != out[i])
                u[out[i]] = i
        cand = [order, full, 0.0, out]
        cand[2] = length(ops, par, cand)
        if best is None or cand[2] < best[2]:
            best = cand
        back = place(ops, par, dur, succ, lambda d, i: fwd(i, d), [-(st[i] + dur[i] + ops[i]["lat"]) for i in range(n)], qs)[0]
        st, out = place(ops, par, dur, deps, fwd, [-(back[i] + dur[i]) for i in range(n)], qs)
    return best


def rhythm(ops, par, plan, tries, heat, steps, upto, seed=1):
    n = len(ops)
    deps = edges(ops)
    qn = {"dve": 0, "act": 1, "pe": 2, "pool": 3, "sp": 4, None: 5}
    dur, lat, hop = [cost(o, par) for o in ops], [o["lat"] for o in ops], par["hop"]
    pre = [[(d, lat[d] + (0.0 if ops[d]["q"] == "pe" == ops[i]["q"] else hop)) for d in deps[i]] for i in range(n)]
    succ = [[] for _ in range(n)]
    for i in range(n):
        for d in deps[i]:
            succ[d].append(i)
    names = sorted(set(b for o in ops for b in o["banks"]))
    bk = [[3 * names.index(b) for b in o["banks"]] for o in ops]
    other = [[(b + e, b + me) for b in bk[i] for e in (0, 1, 2) if e != me] for me in (0, 1, 2) for i in range(n)]
    free = [o["q"] == "any" for o in ops]
    kinds, kind, seen, base, N = {}, [], {}, [], n
    for o in ops:
        x = (o["W"] + o["R"] + ["-"])[0]
        x = x[0] + x[2:] if x[0] in "aLCX" and x[1:].isdigit() else ("o" + x[1:] if x[0] == "f" else x)
        s = o["stage"] % (4 * NP)
        tied = steps and s < 3 * NP
        x = x[:2] + x[3:] if tied and x[:2] == "ex" else ("pd" if tied and x[:2] == "pd" else x)
        k = seen[o["stage"], x, o["q"], 1] = seen.get((o["stage"], x, o["q"], 1), -1) + 1
        kind.append(kinds.setdefault((s % NP if tied else s + NP, x, o["q"], k), len(kinds)))
        base.append(o["stage"] // (4 * NP) * par["period"] + (s // NP * par["beat"] if tied else 0.0))
    phase, eng = [0.0] * len(kinds), [0] * len(kinds)
    for i in sorted(range(n), key=lambda i: -abs(ops[i]["stage"] - 5.6 * NP)):
        phase[kind[i]], eng[kind[i]] = plan[1][i] - base[i], qn[plan[3][i]]
    some = sum(1 for o in ops if o["stage"] < upto)
    dl = [list(d) for d in deps]

    def run(phase, eng, n=some):
        rank = [0.0] * n
        for i in range(n):
            r = base[i] + phase[kind[i]]
            for d in dl[i]:
                if rank[d] >= r:
                    r = rank[d] + 0.001
            rank[i] = r
        order = sorted(range(n), key=lambda i: rank[i])
        end, why, last, use = [0.0] * (n + 1), [n] * n, [n] * 6, [n] * (3 * len(names))
        for i in order:
            me = eng[kind[i]]
            w = last[me]
            s = end[w]
            for d, x in pre[i]:
                if end[d] + x > s:
                    s, w = end[d] + x, d
            if bk[i]:
                for b, mine in other[me * N + i]:
                    if end[use[b]] + hop > s:
                        w = use[b]
                        s = end[w] + hop
                    use[mine] = i
            end[i], why[i], last[me] = s + dur[i], w, i
            last[5] = n
        i = max(range(n), key=lambda j: end[j] + lat[j])
        total, path = end[i] + lat[i], []
        while why[i] < n:
            if why[i] not in deps[i] or free[i]:
                path.append((why[i], i))
            i = why[i]
        return total, path, order, rank
    cur, path, order, rank = run(phase, eng)
    best = (cur, phase, eng)
    for it in range(tries):
        seed = (seed * 1103515245 + 12345) % 2147483648
        u, v = path[(seed >> 8) % len(path)]
        p2, e2 = phase, eng
        if free[v] and (u in deps[v] or (seed >> 4) % 4 == 0):
            e2 = list(eng)
            e2[kind[v]] = 1 - e2[kind[v]]
        elif free[u] and (seed >> 4) % 4 == 1:
            e2 = list(eng)
            e2[kind[u]] = 1 - e2[kind[u]]
        else:
            if u in deps[v]:
                continue
            p2, todo, step = list(phase), [v if (seed >> 6) % 2 else u], ((seed >> 9) % 3) * 100.0 + 1.0
            if (seed >> 6) % 2:
                goal = rank[u] - step
                while todo:
                    x = todo.pop()
                    if rank[x] > goal and p2[kind[x]] + base[x] > goal:
                        p2[kind[x]] = goal - base[x]
                        todo += deps[x]
            else:
                p2[kind[u]] = rank[v] + step - base[u]
        r = run(p2, e2)
        if r[0] <= cur + heat * (1.0 - it / tries) * ((seed >> 12) % 100) / 100.0:
            cur, path, order, rank = r
            phase, eng = p2, e2
            if cur < best[0]:
                best = (cur, phase, eng)
    back = {x: k for k, x in qn.items()}
    r = run(best[1], best[2], n)
    return [r[2], r[3], r[0], [back[best[2][kind[i]]] for i in range(n)]]


def search(ops, par, seed=1):
    n = len(ops)
    deps = edges(ops)
    qn = {"dve": 0, "act": 1, "pe": 2, "pool": 3, "sp": 4, None: 5}
    dur, lat, hop = [cost(o, par) for o in ops], [o["lat"] for o in ops], par["hop"]
    pre = [[(d, dur[d] + lat[d] + (0.0 if ops[d]["q"] == "pe" == ops[i]["q"] else hop)) for d in deps[i]] for i in range(n)]
    post = [[] for _ in range(n)]
    for i in range(n):
        for d, x in pre[i]:
            post[d].append((i, x - dur[d] + dur[i]))
    names = sorted(set(b for o in ops for b in o["banks"]))
    bk = [[6 + names.index(b) for b in o["banks"]] for o in ops]
    free = [o["q"] == "any" for o in ops]
    kinds, kind, seen, eng = {}, [], {}, []
    for o in ops:
        x = (o["W"] + o["R"] + ["-"])[0]
        x = x[0] + x[2:] if x[0] in "aLCX" and x[1:].isdigit() else ("o" + x[1:] if x[0] == "f" else x)
        k = seen[o["stage"], x, o["q"]] = seen.get((o["stage"], x, o["q"]), -1) + 1
        kind.append(kinds.setdefault((o["stage"] % (4 * NP) if o["stage"] >= 0 else -1, x, o["q"], k), len(kinds)))
        mine = x[:3] == "rec" and x[4:] == "2" and (NP if par["mx"] else 0) <= o["stage"] % (4 * NP) < 3 * NP
        eng.append(qn[o["q"]] if o["q"] != "any" else (0 if mine else 1))
    same = [[] for _ in kinds]
    for i in range(n):
        same[kind[i]].append(i)

    def lay(order, pre, eng, first):
        st, why = [0.0] * n, [-1] * n
        ends = [[-1e9] for _ in range(6 + len(names))]
        who = [[0] for _ in range(6 + len(names))]
        for i in order:
            t, w, me, du = first[i], -1, eng[i], dur[i]
            for d, x in pre[i]:
                if st[d] + x > t:
                    t, w = st[d] + x, d
            if me < 5:
                E, Wn = ends[me], who[me]
                k = m = len(E)
                while E[k - 1] > t:
                    k -= 1
                while True:
                    while k < m and (E[k] <= t or st[Wn[k]] < t + du):
                        if E[k] > t:
                            t, w = E[k], Wn[k]
                        k += 1
                    t0 = t
                    for b in bk[i]:
                        B, Wb = ends[b], who[b]
                        j = len(B)
                        while B[j - 1] > t - hop:
                            j -= 1
                        while j < len(B) and st[Wb[j]] - hop < t + du:
                            if eng[Wb[j]] != me:
                                t, w = B[j] + hop, Wb[j]
                            j += 1
                    if t == t0:
                        break
                E.insert(k, t + du)
                Wn.insert(k, i)
                for b in bk[i]:
                    B = ends[b]
                    j = len(B)
                    while B[j - 1] > t + du:
                        j -= 1
                    B.insert(j, t + du)
                    who[b].insert(j, i)
            st[i], why[i] = t, w
        return st, why
    zero = [0.0] * n

    def run(rank, eng, rounds):
        rank = list(rank)
        for i in range(n):
            r = rank[i]
            for d, x in pre[i]:
                if rank[d] >= r:
                    r = rank[d] + 0.001
            rank[i] = r
        st, why = lay(sorted(range(n), key=lambda i: rank[i]), pre, eng, zero)
        for _ in range(rounds):
            back = lay(sorted(range(n), key=lambda i: (-st[i] - dur[i], -i)), post, eng, lat)[0]
            st, why = lay(sorted(range(n), key=lambda i: (-back[i] - dur[i], i)), pre, eng, zero)
        order, total, path = sorted(range(n), key=lambda i: (st[i], i)), 0.0, []
        for du, la, pr, hp, scale in cases:
            end, why, last, use = [0.0] * (n + 1), [n] * n, [n] * 6, [n] * (3 * len(names) + 18)
            for i in order:
                me = eng[i]
                w = last[me]
                s = end[w]
                for d, x in pr[i]:
                    if end[d] + x > s:
                        s, w = end[d] + x, d
                if bk[i]:
                    for b, mine in other[me * n + i]:
                        if end[use[b]] + hp > s:
                            w = use[b]
                            s = end[w] + hp
                        use[mine] = i
                end[i], why[i], last[me] = s + du[i], w, i
                last[5] = n
            i = max(tails, key=lambda j: end[j] + la[j])
            total += (end[i] + la[i]) * scale
            while why[i] < n:
                if why[i] not in deps[i] or free[i]:
                    path.append((why[i], i))
                i = why[i]
        return total, path, st
    other = [[(3 * b + e, 3 * b + me) for b in bk[i] for e in (0, 1, 2) if e != me] for me in (0, 1, 2) for i in range(n)]
    tails = [i for i in range(n) if not post[i]]
    cases = []
    for x in par["cases"]:
        p = dict(par)
        p.update(x)
        la = [o["lat"] * p["dma"] for o in ops]
        cases.append(([cost(o, p) for o in ops], la,
                      [[(d, la[d] + (0.0 if ops[d]["q"] == "pe" == ops[i]["q"] else p["hop"])) for d in deps[i]] for i in range(n)], p["hop"],
                      p["weight"]))
    per, extra = par["per"], par["extra"]
    late = [1e12] * n
    for i in range(n - 1, -1, -1):
        s = ops[i]["stage"]
        if ops[i]["W"] and ops[i]["W"][0][:3] == "off":
            late[i] = min(late[i], s * per / NP + s // (4 * NP) * extra)
        if late[i] == 1e12:
            late[i] = NV * (4 * per + extra) + s % NP * per / NP
        for d, x in pre[i]:
            late[d] = min(late[d], late[i] - x)
    cur, path, st = run(late, eng, 3)
    best = (cur, st, eng)
    for tries, heat in par["search"]:
        cur, path, st = run(best[1], best[2], 0)
        eng = best[2]
        for it in range(tries):
            r2, e2 = list(st), eng
            for _ in range(1 + seed % 3):
                seed = (seed * 1103515245 + 12345) % 2147483648
                u, v = path[(seed >> 8) % len(path)]
                if free[v] and (u in deps[v] or (seed >> 4) % 4 == 0) or free[u] and (seed >> 4) % 4 == 1:
                    x = v if free[v] and (u in deps[v] or (seed >> 4) % 4 == 0) else u
                    e2 = list(e2)
                    for j in same[kind[x]]:
                        e2[j] = 1 - eng[x]
                elif u not in deps[v]:
                    sh = st[v] - st[u] + 1.0 + ((seed >> 9) % 3) * par["amp"]
                    for j in same[kind[u]]:
                        r2[j] += sh
            r = run(r2, e2, (seed >> 7) % 2)
            if r[0] <= cur + heat * (1.0 - it / tries) * ((seed >> 12) % 100) / 100.0:
                cur, path, st = r
                eng = e2
                if cur < best[0]:
                    best = (cur, st, eng)
    back = {x: k for k, x in qn.items()}
    return [sorted(range(n), key=lambda i: (best[1][i], i)), best[1], best[0], [back[x] for x in best[2]]]


def polish(ops, par, plan, tries, seed=1):
    n = len(ops)
    deps = edges(ops)
    qn = {"dve": 0, "act": 1, "pe": 2, "pool": 3, "sp": 4, None: 5}
    dur = [cost(o, par) for o in ops]
    lat = [o["lat"] for o in ops]
    hop = par["hop"]
    pre = [[(d, lat[d] + (0.0 if ops[d]["q"] == "pe" == ops[i]["q"] else hop)) for d in deps[i]] for i in range(n)]
    succ = [[] for _ in range(n)]
    for i in range(n):
        for d in deps[i]:
            succ[d].append(i)
    names = sorted(set(b for o in ops for b in o["banks"]))
    bk = [[3 * names.index(b) for b in o["banks"]] for o in ops]
    order, q = list(plan[0]), [qn[x] for x in plan[3]]

    other = [[(b + e, b + me) for b in bk[i] for e in (0, 1, 2) if e != me] for me in (0, 1, 2) for i in range(n)]
    ends = [i for i in range(n) if not succ[i]]
    free = [ops[i]["q"] == "any" for i in range(n)]
    gap = 32

    def run(order, q, first, old):
        c = first // gap
        end, why, marks = list(old[0]), list(old[1]), old[2][:c + 1]
        last, use = list(marks[c][0]), list(marks[c][1])
        for c in range(c * gap, n, gap):
            for i in order[c:c + gap]:
                me = q[i]
                w = last[me]
                s = end[w]
                for d, x in pre[i]:
                    if end[d] + x > s:
                        s, w = end[d] + x, d
                if bk[i]:
                    for b, mine in other[me * n + i]:
                        if end[use[b]] + hop > s:
                            w = use[b]
                            s = end[w] + hop
                        use[mine] = i
                end[i], why[i], last[me] = s + dur[i], w, i
                last[5] = n
            marks.append((list(last), list(use)))
        i = max(ends, key=lambda j: end[j] + lat[j])
        return end[i] + lat[i], i, (end, why, marks)

    def trail(i, why):
        path = []
        while why[i] < n:
            if why[i] not in deps[i] or free[i]:
                path.append((why[i], i))
            i = why[i]
        return path
    cur, i, state = run(order, q, 0, ([0.0] * (n + 1), [n] * n, [([n] * 6, [n] * (3 * len(names)))]))
    path = trail(i, state[1])
    best = (cur, order, q)
    for it in range(tries):
        seed = (seed * 1103515245 + 12345) % 2147483648
        u, v = path[(seed >> 8) % len(path)]
        o2, q2 = order, q
        if free[v] and (u in deps[v] or (seed >> 4) % 4 == 0):
            q2 = list(q)
            q2[v] = 1 - q2[v]
            a = order.index(v)
        elif free[u] and (seed >> 4) % 4 == 1:
            q2 = list(q)
            q2[u] = 1 - q2[u]
            a = order.index(u)
        else:
            a, b = order.index(u), order.index(v)
            mid = order[a:b + 1]
            if (seed >> 6) % 2:
                move = {v}
                for x in reversed(mid):
                    if x in move:
                        move.update(deps[x])
                if u in move:
                    continue
                o2 = order[:a] + [x for x in mid if x in move] + [x for x in mid if x not in move] + order[b + 1:]
            else:
                move = {u}
                for x in mid:
                    if x in move:
                        move.update(succ[x])
                if v in move:
                    continue
                o2 = order[:a] + [x for x in mid if x not in move] + [x for x in mid if x in move] + order[b + 1:]
        t, i, st = run(o2, q2, a, state)
        if t <= cur + par["heat"] * (1.0 - it / tries) * ((seed >> 12) % 100) / 100.0:
            cur, path, order, q, state = t, trail(i, st[1]), o2, q2, st
            if t < best[0]:
                best = (t, o2, q2)
    back = {x: k for k, x in qn.items()}
    out = [back[x] for x in best[2]]
    full, users = [set(d) for d in deps], {}
    for i in best[1]:
        for b in ops[i]["banks"]:
            u = users.setdefault(b, {})
            full[i].update(j for e, j in u.items() if e != out[i])
            u[out[i]] = i
    return [best[1], full, best[0], out]


def rank_program(g, core, T, topo):
    if T.rank_of(core) is None:
        return
    ops = build(g, core, T, topo)
    if "plan" not in CACHE:
        CACHE["plan"] = polish(ops, PAR, search(ops, PAR), PAR["tries"])
    order, deps = CACHE["plan"][:2]
    loads = [i for i, o in enumerate(ops) if o["stage"] < 0 and o["sem"]]
    order = loads + [i for i in order if i not in loads]
    for i, o in enumerate(ops):
        if o["q"] == "any":
            o["q"] = CACHE["plan"][3][i]
            o["calls"] = o["alt"][o["q"]]
    queue = {"pe": g.tensor, "dve": g.vector, "act": g.scalar, "pool": g, "sp": g.sync}
    total, known, mark, clock = {}, {q: {} for q in queue}, {}, {}
    for i in order:
        o = ops[i]
        q = o["q"]
        sem = o["sem"] or q
        if q is None:
            mark[i] = (sem, -o["inc"])
            clock[i] = {sem: -o["inc"]}
            total[sem] = -o["inc"]
            continue
        kn = known[q]
        need = {}
        for d in deps[i]:
            if not (q == "pe" and ops[d]["q"] == "pe"):
                s, c = mark[d]
                if kn.get(s, 0) < c:
                    need.setdefault(s, []).append(d)
        tops = sorted((max(ds, key=lambda d: mark[d][1]) for ds in need.values()), reverse=True, key=lambda d: len(clock[d]))
        for d in tops:
            s, c = mark[d]
            if kn.get(s, 0) < c:
                queue[q].wait_ge(T.sem[s], c)
                for s2, c2 in clock[d].items():
                    if kn.get(s2, 0) < c2:
                        kn[s2] = c2
        for call in o["calls"]:
            ins = call()
            if o["inc"] > 0:
                ins.then_inc(T.sem[sem], o["inc"])
            total[sem] = total.get(sem, 0) + abs(o["inc"])
        mark[i] = (sem, total[sem])
        clock[i] = dict(kn)
        clock[i][sem] = total[sem]
    for s in sorted(total):
        g.wait_ge(T.sem[s], total[s])
